import numpy as np
import ml_dtypes


def mxq(x, axis, fmt="e4m3"):
    dtype, down = {"e4m3": (ml_dtypes.float8_e4m3fn, 7), "e5m2": (ml_dtypes.float8_e5m2, 14)}[fmt]
    v = np.moveaxis(np.asarray(x, np.float32).astype(ml_dtypes.bfloat16).astype(np.float64), axis, -1)
    blocks = v.reshape(v.shape[:-1] + (-1, 32))
    amax = np.abs(blocks).max(-1, keepdims=True)
    byte = np.maximum(np.where(amax > 0, np.frexp(amax)[1] - 1 + 127, 0) - down, 1)
    scale = np.exp2(byte - 127.0)
    codes = (blocks / scale).astype(np.float32).astype(dtype).astype(np.float64)
    return np.moveaxis((codes * scale).reshape(v.shape), -1, axis)


WIDE = False


def mx_kscale(k):
    if not WIDE:
        return np.ones(k)
    levels = np.array([10, -10, 5, -5, 0])
    if k % 512:
        return np.exp2(np.random.permutation(np.resize(levels, k // 32))).repeat(32)
    a = np.empty((k // 512, 16))
    for p in range(k // 512):
        a[p, :8] = np.random.permutation(np.resize(levels, 8))
        for g in range(8):
            far = levels[np.abs(levels - a[p, g]) >= 10]
            a[p, g + 8] = far[np.random.randint(len(far))]
    return np.exp2(a.ravel()).repeat(32)


def f64(x):
    return np.asarray(x).astype(np.float64)


def striped(idx):
    return np.tile(idx.reshape(-1, 16).T, (8, 1)).astype(np.uint16)


def unstriped(offs):
    return offs[:16].T.reshape(-1).astype(np.int64)


E2M1 = np.array([0.0, 0.5, 1.0, 1.5, 2.0, 3.0, 4.0, 6.0, -0.0, -0.5, -1.0, -1.5, -2.0, -3.0, -4.0, -6.0])


def pack_weight(w, fmt):
    k, n = w.shape
    w = f64(np.asarray(w, np.float32).astype(ml_dtypes.bfloat16)).reshape(k // 32, 32, n)
    amax = np.abs(w).max(1)
    if fmt == "e4m3":
        byte = np.frexp(amax)[1] - 1 + 127 - 7
    else:
        mant, ex = np.frexp(amax / 6.0)
        byte = np.where(mant > 0.5, ex, ex - 1) + 127
    byte = np.clip(np.where(amax > 0, byte, 1), 1, 254)
    scaled = (w * np.exp2(127.0 - byte)[:, None, :]).reshape(k, n).astype(np.float32)
    by_word = np.ascontiguousarray(scaled.reshape(k // 512, 128, 4, n).transpose(0, 1, 3, 2))
    if fmt == "e4m3":
        words = by_word.astype(ml_dtypes.float8_e4m3fn).view(np.uint8)
    else:
        c = by_word.astype(ml_dtypes.float4_e2m1fn).view(np.uint8) & 0xF
        words = (c[..., 0::2] | (c[..., 1::2] << 4)).reshape(k // 512, 128, 2 * n)
    return np.ascontiguousarray(words), np.ascontiguousarray(byte.astype(np.uint8).reshape(k // 512, 16, n))


def unpack_weight(words, scales, fmt):
    g, _, n = scales.shape
    words = np.ascontiguousarray(words).reshape(g, 128, n, -1)
    if fmt == "e4m3":
        vals = words.view(ml_dtypes.float8_e4m3fn).astype(np.float64)
    else:
        nib = np.empty((g, 128, n, 4), np.uint8)
        nib[..., 0::2] = words & 0xF
        nib[..., 1::2] = words >> 4
        vals = E2M1[nib]
    vals = vals * np.repeat(np.exp2(scales.astype(np.float64) - 127.0), 8, axis=1)[..., None]
    return vals.transpose(0, 1, 3, 2).reshape(g * 512, n)


def silu(v):
    return v / (1.0 + np.exp(-np.maximum(v, -700.0)))


K, T, E1, C1, E2, C2, H = 1024, 512, 2, 256, 4, 128, 512
N = 256


def by_expert(wq, xq, E, C):
    return np.concatenate([wq[e].T @ xq[:, e * C:(e + 1) * C] for e in range(E)], axis=1)


def setup_inputs():
    n = np.random.standard_normal
    s = mx_kscale(K)
    u = mx_kscale(H)
    slots1, slots2 = np.random.permutation(T), np.random.permutation(T)
    x = pack_weight(n((K, T)) * s[:, None], "e4m3")
    wa = [pack_weight(m, "e2m1") for m in n((E1, K, H)) / np.sqrt(K) / s[None, :, None]]
    wb = [pack_weight(m, "e2m1") for m in n((E2, K, H)) / np.sqrt(K) / s[None, :, None] * u]
    w2 = pack_weight(n((H, N)) / np.sqrt(H) / u[:, None], "e2m1")
    return {
        "x_words": x[0],
        "x_scales": x[1],
        "wa_words": np.stack([m[0] for m in wa]),
        "wa_scales": np.stack([m[1] for m in wa]),
        "wb_words": np.stack([m[0] for m in wb]),
        "wb_scales": np.stack([m[1] for m in wb]),
        "w2_words": w2[0],
        "w2_scales": w2[1],
        "offs": striped(slots1),
        "offs2": striped(slots2),
    }


def reference(x_words, x_scales, wa_words, wa_scales, wb_words, wb_scales, w2_words, w2_scales, offs, offs2):
    wa = np.stack([unpack_weight(wa_words[e], wa_scales[e], "e2m1") for e in range(E1)])
    wb = np.stack([unpack_weight(wb_words[e], wb_scales[e], "e2m1") for e in range(E2)])
    w2 = unpack_weight(w2_words, w2_scales, "e2m1")
    idx, idx2 = unstriped(offs), unstriped(offs2)
    x = unpack_weight(x_words, x_scales, "e4m3")
    a, c = np.zeros((H, T)), np.zeros((H, T))
    a[:, idx] = by_expert(wa, x[:, idx], E1, C1)
    c[:, idx2] = by_expert(wb, x[:, idx2], E2, C2)
    return w2.T @ mxq(silu(a) * c, 0, "e4m3")

@@ -1,0 +1,207 @@
+from contextlib import ExitStack
+
+import concourse.mybir as mybir
+from concourse.masks import make_identity
+
+K, T, H, N = 1024, 512, 512, 256
+E1, C1, E2, C2 = 2, 256, 4, 128
+FLOPS = 2 * K * H * T * 2 + 2 * H * N * T
+
+F32 = mybir.dt.float32
+BF16 = mybir.dt.bfloat16
+I32 = mybir.dt.int32
+U32 = mybir.dt.uint32
+U16 = mybir.dt.uint16
+U8 = mybir.dt.uint8
+FP8X4 = mybir.dt.float8_e4m3fn_x4
+FP4X4 = mybir.dt.float4_e2m1fn_x4
+SILU = mybir.ActivationFunctionType.Silu
+MULT = mybir.AluOpType.mult
+
+P = 128
+PACK = 4
+PASSES = 2
+BLOCK = 128
+BLOCKS = T // BLOCK
+WIDE = 704
+PIECE = 256
+RUN = 4
+EXPERT = PASSES * 2 * H
+
+
+def tile_moe_pool_silu_kernel(
+    tc, x_words, x_scales, wa_words, wa_scales, wb_words, wb_scales, w2_words, w2_scales, offs, offs2, out
+):
+    nc = tc.nc
+    with ExitStack() as ctx:
+        lists = ctx.enter_context(tc.tile_pool(name="lists", bufs=1))
+        keep = ctx.enter_context(tc.tile_pool(name="keep", bufs=1))
+        ring = ctx.enter_context(tc.tile_pool(name="ring", bufs=4))
+        psum = ctx.enter_context(tc.psum_pool(name="psum", bufs=4))
+
+        list_a = lists.tile([P, T // 16], U16, name="list_a")
+        list_b = lists.tile([P, T // 16], U16, name="list_b")
+
+        x_sc = keep.tile([P, WIDE], U8, name="x_sc", tag="after_scales", align_bytes=64)
+        x_w = keep.tile([P, PASSES * T], I32, name="x_w", tag="after_words", align_bytes=64)
+        wa_sc = keep.tile([P, E1 * PASSES * H], U8, name="wa_sc", align_bytes=64)
+        first_w = keep.tile([P, EXPERT], U8, name="first_w", align_bytes=64)
+        got_sc = [keep.tile([P, T], U8, name="got_sc%d" % g, align_bytes=64) for g in range(2)]
+        moved_sc = [keep.tile([P, T], U8, name="moved_sc%d" % g, tag="moved%d" % g, align_bytes=64) for g in range(2)]
+        ident = keep.tile([P, P], F32, name="ident")
+        warm = keep.tile([P, 1], F32, name="warm")
+
+        nc.gpsimd.memset(x_sc[:].bitcast(I32), 0)
+        nc.gpsimd.memset(wa_sc[:].bitcast(I32), 0)
+        make_identity(nc, ident[:])
+
+        def load_words(queue, tile, words):
+            queue.dma_start(
+                out=tile.bitcast(I32).rearrange("p (s c) -> p s c", s=PASSES),
+                in_=words.bitcast(I32).rearrange("s p c -> p s c"),
+            )
+
+        def load_scales(tile, scales, planes):
+            rows = scales.bitcast(I32)
+            for q in range(4):
+                nc.sync.dma_start(
+                    out=tile[32 * q : 32 * q + 4, :].bitcast(I32).rearrange("r (a c) -> r a c", a=planes),
+                    in_=rows[:, 4 * q : 4 * q + 4, :].rearrange("a r c -> r a c"),
+                )
+
+        nc.sync.dma_start(list_a[:], offs)
+        nc.sync.dma_start(
+            out=x_w[:].rearrange("p (s t) -> p s t", s=PASSES),
+            in_=x_words.rearrange("s p t d -> p s (t d)").bitcast(I32),
+        )
+        for q in range(4):
+            nc.sync.dma_start(
+                out=x_sc[32 * q : 32 * q + 8, 0:T].bitcast(I32),
+                in_=x_scales.bitcast(I32)[:, 4 * q : 4 * q + 4, :],
+            )
+        load_words(nc.scalar, first_w[:], wa_words[0])
+        nc.scalar.activation(warm[:], ident[:, 0:1], SILU)
+        nc.sync.dma_start(list_b[:], offs2)
+        load_scales(wa_sc[:], wa_scales.rearrange("e s b c -> (e s) b c"), E1 * PASSES)
+
+        def gather_scales(g, offsets):
+            nc.vector.tensor_copy(got_sc[g][:], x_sc[:].indirect(offsets[:]))
+            for first, count in ((0, 64), (64, 32), (96, 4)):
+                nc.sync.dma_start(
+                    out=moved_sc[g][first : first + count, :].bitcast(I32),
+                    in_=got_sc[g][first + 4 : first + 4 + count, :].bitcast(I32),
+                )
+
+        def gather_words(got, offsets, j):
+            for s in range(PASSES):
+                window = x_w[:, s * T : (s + 1) * T].bitcast(U32)
+                nc.vector.tensor_copy(got[:, s, :], window.indirect(offsets[:, j * PIECE // 16 : (j + 1) * PIECE // 16]))
+
+        def first_layer(g, b, words, scales, e, staged):
+            slots = slice(b * BLOCK, (b + 1) * BLOCK)
+            acc = psum.tile([P, H], F32, name="acc", tag="acc", bufs=1)
+            planes = (got_sc[g], moved_sc[g])
+            piece, first = divmod(b * BLOCK, PIECE)
+            for s in range(PASSES):
+                a = e * PASSES + s
+                nc.tensor.matmul_mx(
+                    out=acc[:],
+                    lhsT=got_w[g][piece][:, s, first : first + BLOCK].bitcast(FP8X4),
+                    lhsT_scale=planes[s][:, slots],
+                    rhs=words[:, s * 2 * H : (s + 1) * 2 * H].bitcast(FP4X4),
+                    rhs_scale=scales[:, a * H : (a + 1) * H],
+                    start=(s == 0),
+                    stop=(s == PASSES - 1),
+                )
+            parted = ring.tile([P, PACK, P], F32, name="parted")
+            stepped = acc[:].rearrange("u (m d) -> u d m", d=PACK)
+            if g == 0:
+                nc.scalar.activation(parted[:], stepped, SILU)
+            else:
+                nc.scalar.copy(parted[:], stepped)
+            turned = psum.tile([P, PACK, BLOCK], F32, name="turned", tag="turned", bufs=2)
+            for d in range(PACK):
+                nc.tensor.transpose(turned[:, d, :], parted[:, d, :], ident[:])
+            nc.scalar.copy(staged, turned[:])
+
+        gather_scales(0, list_a)
+        gather_scales(1, list_b)
+        got_first = keep.tile([P, PASSES, PIECE], U32, name="got_first", align_bytes=64)
+        got_rest = keep.tile([P, 3, PASSES, PIECE], U32, name="got_rest", tag="after_scales", align_bytes=64)
+        got_w = [[got_first[:], got_rest[:, 0]], [got_rest[:, 1], got_rest[:, 2]]]
+        for g, offsets in enumerate((list_a, list_b)):
+            for j in range(T // PIECE):
+                gather_words(got_w[g][j], offsets, j)
+        sizes = [EXPERT] * (E1 - 1 + E2) + [2 * N, E2 * PASSES * H, N]
+        late = keep.tile([P, sum(sizes)], U8, name="late", tag="after_words", align_bytes=64)
+        parts = [late[:, sum(sizes[:i]) : sum(sizes[: i + 1])] for i in range(len(sizes))]
+        wa_w = [first_w[:]] + parts[: E1 - 1]
+        wb_w = parts[E1 - 1 : E1 - 1 + E2]
+        w2_w, wb_sc, w2_sc = parts[E1 - 1 + E2 :]
+        load_words(nc.sync, wa_w[1], wa_words[1])
+        load_scales(wb_sc, wb_scales.rearrange("e s b c -> (e s) b c"), E2 * PASSES)
+        for e in range(E2):
+            load_words(nc.sync, wb_w[e], wb_words[e])
+        load_scales(w2_sc, w2_scales, 1)
+        nc.sync.dma_start(out=w2_w.bitcast(I32), in_=w2_words[0].bitcast(I32))
+
+        left = keep.tile([P, PACK * T], F32, name="left", tag="after_scales", align_bytes=64)
+        right = keep.tile([P, PACK * T], F32, name="right", tag="moved1", align_bytes=64)
+
+        win_a = [keep.tile([P, T], F32, name="win_a%d" % d) for d in range(PACK)]
+        for b in range(BLOCKS):
+            staged_a = ring.tile([P, PACK, BLOCK], F32, name="staged_a")
+            e = b * BLOCK // C1
+            first_layer(0, b, wa_w[e], wa_sc, e, staged_a[:])
+            for d in range(PACK):
+                nc.vector.tensor_copy(
+                    win_a[d][:].indirect(list_a[:, b * BLOCK // 16 : (b + 1) * BLOCK // 16]), staged_a[:, d, :]
+                )
+
+        staged_c = keep.tile([P, PACK, T], F32, name="staged_c")
+        win_c = {d: keep.tile([P, T], F32, name="win_c%d" % d) for d in range(1, PACK)}
+        for b in range(BLOCKS):
+            e = b * BLOCK // C2
+            slots = slice(b * BLOCK, (b + 1) * BLOCK)
+            first_layer(1, b, wb_w[e], wb_sc, e, staged_c[:, :, slots])
+            for d in range(1, PACK):
+                nc.vector.tensor_copy(
+                    win_c[d][:].indirect(list_b[:, b * BLOCK // 16 : (b + 1) * BLOCK // 16]), staged_c[:, d, slots]
+                )
+
+        for d in range(PACK):
+            side = right if d == 0 else left
+            nc.scalar.copy(side[:, d * T : (d + 1) * T], win_a[d][:])
+        for d in range(1, PACK):
+            nc.scalar.copy(right[:, d * T : (d + 1) * T], win_c[d][:])
+        nc.vector.tensor_copy(left[:].indirect(list_b[:]), staged_c[:, 0, :])
+
+        left_v = left[:].rearrange("p (d c i) -> p c d i", d=PACK, i=RUN)
+        right_v = right[:].rearrange("p (d c i) -> p c d i", d=PACK, i=RUN)
+        out_v = out.rearrange("(b p) t -> p b t", p=P)
+        runs = BLOCK // RUN
+        for j in range(BLOCKS):
+            h = ring.tile([P, BLOCK * PACK], BF16, name="h", align_bytes=64)
+            nc.vector.tensor_tensor(
+                h[:].rearrange("p (c i d) -> p c d i", d=PACK, i=RUN),
+                left_v[:, j * runs : (j + 1) * runs],
+                right_v[:, j * runs : (j + 1) * runs],
+                MULT,
+            )
+            h_w = ring.tile([P, BLOCK], U32, name="h_w", align_bytes=64)
+            h_sc = ring.tile([P, BLOCK], U8, name="h_sc", align_bytes=64)
+            nc.vector.quantize_mx(out=h_w[:].bitcast(FP8X4), scales=h_sc[:], in_=h[:])
+            acc = psum.tile([P, N // P, BLOCK], F32, name="acc2")
+            for n in range(N // P):
+                nc.tensor.matmul_mx(
+                    out=acc[:, n, :],
+                    lhsT=w2_w[:, n * 2 * P : (n + 1) * 2 * P].bitcast(FP4X4),
+                    lhsT_scale=w2_sc[:, n * P : (n + 1) * P],
+                    rhs=h_w[:].bitcast(FP8X4),
+                    rhs_scale=h_sc[:],
+                    start=True,
+                    stop=True,
+                )
+            result = ring.tile([P, N // P, BLOCK], F32, name="result")
+            nc.scalar.copy(result[:], acc[:])
+            nc.sync.dma_start(out=out_v[:, :, j * BLOCK : (j + 1) * BLOCK], in_=result[:])

@@ -24,8 +24,8 @@ PASSES = 2
 BLOCK = 128
 BLOCKS = T // BLOCK
 WIDE = 704
-PIECE = 256
 RUN = 4
+HALF = 2
 EXPERT = PASSES * 2 * H
 
 
@@ -43,15 +43,15 @@ def tile_moe_pool_silu_kernel(
         list_b = lists.tile([P, T // 16], U16, name="list_b")
 
         x_sc = keep.tile([P, WIDE], U8, name="x_sc", tag="after_scales", align_bytes=64)
-        x_w = keep.tile([P, PASSES * T], I32, name="x_w", tag="after_words", align_bytes=64)
-        wa_sc = keep.tile([P, E1 * PASSES * H], U8, name="wa_sc", align_bytes=64)
+        x_w = keep.tile([P, T + WIDE], I32, name="x_w", tag="after_words", align_bytes=64)
         first_w = keep.tile([P, EXPERT], U8, name="first_w", align_bytes=64)
+        wa_sc = keep.tile([P, E1 * PASSES * H], U8, name="wa_sc", align_bytes=64)
         got_sc = [keep.tile([P, T], U8, name="got_sc%d" % g, align_bytes=64) for g in range(2)]
         moved_sc = [keep.tile([P, T], U8, name="moved_sc%d" % g, tag="moved%d" % g, align_bytes=64) for g in range(2)]
         ident = keep.tile([P, P], F32, name="ident")
-        warm = keep.tile([P, 1], F32, name="warm")
 
         nc.gpsimd.memset(x_sc[:].bitcast(I32), 0)
+        nc.gpsimd.memset(x_w[:, PASSES * T - 8 :], 0)
         nc.gpsimd.memset(wa_sc[:].bitcast(I32), 0)
         make_identity(nc, ident[:])
 
@@ -70,18 +70,17 @@ def tile_moe_pool_silu_kernel(
                 )
 
         nc.sync.dma_start(list_a[:], offs)
-        nc.sync.dma_start(
-            out=x_w[:].rearrange("p (s t) -> p s t", s=PASSES),
-            in_=x_words.rearrange("s p t d -> p s (t d)").bitcast(I32),
-        )
+        nc.sync.dma_start(list_b[:], offs2)
         for q in range(4):
             nc.sync.dma_start(
                 out=x_sc[32 * q : 32 * q + 8, 0:T].bitcast(I32),
                 in_=x_scales.bitcast(I32)[:, 4 * q : 4 * q + 4, :],
             )
+        nc.sync.dma_start(
+            out=x_w[:, : PASSES * T].rearrange("p (s t) -> p s t", s=PASSES),
+            in_=x_words.rearrange("s p t d -> p s (t d)").bitcast(I32),
+        )
         load_words(nc.scalar, first_w[:], wa_words[0])
-        nc.scalar.activation(warm[:], ident[:, 0:1], SILU)
-        nc.sync.dma_start(list_b[:], offs2)
         load_scales(wa_sc[:], wa_scales.rearrange("e s b c -> (e s) b c"), E1 * PASSES)
 
         def gather_scales(g, offsets):
@@ -92,46 +91,46 @@ def tile_moe_pool_silu_kernel(
                     in_=got_sc[g][first + 4 : first + 4 + count, :].bitcast(I32),
                 )
 
-        def gather_words(got, offsets, j):
+        def gather_words(got, offsets, first, count):
             for s in range(PASSES):
-                window = x_w[:, s * T : (s + 1) * T].bitcast(U32)
-                nc.vector.tensor_copy(got[:, s, :], window.indirect(offsets[:, j * PIECE // 16 : (j + 1) * PIECE // 16]))
+                window = x_w[:, s * T : s * T + WIDE].bitcast(U32)
+                nc.vector.tensor_copy(
+                    got[:, s, first : first + count], window.indirect(offsets[:, first // 16 : (first + count) // 16])
+                )
 
         def first_layer(g, b, words, scales, e, staged):
             slots = slice(b * BLOCK, (b + 1) * BLOCK)
             acc = psum.tile([P, H], F32, name="acc", tag="acc", bufs=1)
             planes = (got_sc[g], moved_sc[g])
-            piece, first = divmod(b * BLOCK, PIECE)
             for s in range(PASSES):
                 a = e * PASSES + s
                 nc.tensor.matmul_mx(
                     out=acc[:],
-                    lhsT=got_w[g][piece][:, s, first : first + BLOCK].bitcast(FP8X4),
+                    lhsT=got_w[g][:, s, slots].bitcast(FP8X4),
                     lhsT_scale=planes[s][:, slots],
                     rhs=words[:, s * 2 * H : (s + 1) * 2 * H].bitcast(FP4X4),
                     rhs_scale=scales[:, a * H : (a + 1) * H],
                     start=(s == 0),
                     stop=(s == PASSES - 1),
                 )
-            parted = ring.tile([P, PACK, P], F32, name="parted")
             stepped = acc[:].rearrange("u (m d) -> u d m", d=PACK)
-            if g == 0:
-                nc.scalar.activation(parted[:], stepped, SILU)
-            else:
-                nc.scalar.copy(parted[:], stepped)
-            turned = psum.tile([P, PACK, BLOCK], F32, name="turned", tag="turned", bufs=2)
-            for d in range(PACK):
-                nc.tensor.transpose(turned[:, d, :], parted[:, d, :], ident[:])
-            nc.scalar.copy(staged, turned[:])
+            for d0 in range(0, PACK, HALF):
+                parted = ring.tile([P, HALF, P], F32, name="parted")
+                if g == 0:
+                    nc.scalar.activation(parted[:], stepped[:, d0 : d0 + HALF, :], SILU)
+                else:
+                    nc.scalar.copy(parted[:], stepped[:, d0 : d0 + HALF, :])
+                turned = psum.tile([P, HALF, BLOCK], F32, name="turned", tag="turned", bufs=2)
+                for d in range(HALF):
+                    nc.tensor.transpose(turned[:, d, :], parted[:, d, :], ident[:])
+                nc.scalar.copy(staged[:, d0 : d0 + HALF, :], turned[:])
 
         gather_scales(0, list_a)
         gather_scales(1, list_b)
-        got_first = keep.tile([P, PASSES, PIECE], U32, name="got_first", align_bytes=64)
-        got_rest = keep.tile([P, 3, PASSES, PIECE], U32, name="got_rest", tag="after_scales", align_bytes=64)
-        got_w = [[got_first[:], got_rest[:, 0]], [got_rest[:, 1], got_rest[:, 2]]]
-        for g, offsets in enumerate((list_a, list_b)):
-            for j in range(T // PIECE):
-                gather_words(got_w[g][j], offsets, j)
+        got_w = [keep.tile([P, PASSES, T], U32, name="got_w%d" % g, tag=tag, align_bytes=64) for g, tag in enumerate(("words_a", "after_scales"))]
+        for e in range(E1):
+            gather_words(got_w[0], list_a, e * C1, C1)
+        gather_words(got_w[1], list_b, 0, T)
         sizes = [EXPERT] * (E1 - 1 + E2) + [2 * N, E2 * PASSES * H, N]
         late = keep.tile([P, sum(sizes)], U8, name="late", tag="after_words", align_bytes=64)
         parts = [late[:, sum(sizes[:i]) : sum(sizes[: i + 1])] for i in range(len(sizes))]
@@ -191,10 +190,11 @@ def tile_moe_pool_silu_kernel(
             h_w = ring.tile([P, BLOCK], U32, name="h_w", align_bytes=64)
             h_sc = ring.tile([P, BLOCK], U8, name="h_sc", align_bytes=64)
             nc.vector.quantize_mx(out=h_w[:].bitcast(FP8X4), scales=h_sc[:], in_=h[:])
-            acc = psum.tile([P, N // P, BLOCK], F32, name="acc2")
+            result = ring.tile([P, N // P, BLOCK], F32, name="result")
             for n in range(N // P):
+                acc = psum.tile([P, BLOCK], F32, name="acc2")
                 nc.tensor.matmul_mx(
-                    out=acc[:, n, :],
+                    out=acc[:],
                     lhsT=w2_w[:, n * 2 * P : (n + 1) * 2 * P].bitcast(FP4X4),
                     lhsT_scale=w2_sc[:, n * P : (n + 1) * P],
                     rhs=h_w[:].bitcast(FP8X4),
@@ -202,6 +202,8 @@ def tile_moe_pool_silu_kernel(
                     start=True,
                     stop=True,
                 )
-            result = ring.tile([P, N // P, BLOCK], F32, name="result")
-            nc.scalar.copy(result[:], acc[:])
+                if j == BLOCKS - 1 and n == 1:
+                    nc.vector.tensor_copy(result[:, n, :], acc[:])
+                else:
+                    nc.scalar.copy(result[:, n, :], acc[:])
             nc.sync.dma_start(out=out_v[:, :, j * BLOCK : (j + 1) * BLOCK], in_=result[:])

@@ -100,7 +100,8 @@ def tile_moe_pool_silu_kernel(
 
         def first_layer(g, b, words, scales, e, staged):
             slots = slice(b * BLOCK, (b + 1) * BLOCK)
-            acc = psum.tile([P, H], F32, name="acc", tag="acc", bufs=1)
+            step = g * BLOCKS + b
+            acc = psum.tile([P, H], F32, name="acc", tag="odd" if step > 2 and step % 2 else "even", bufs=1)
             planes = (got_sc[g], moved_sc[g])
             for s in range(PASSES):
                 a = e * PASSES + s
@@ -114,29 +115,34 @@ def tile_moe_pool_silu_kernel(
                     stop=(s == PASSES - 1),
                 )
             stepped = acc[:].rearrange("u (m d) -> u d m", d=PACK)
-            for d0 in range(0, PACK, HALF):
-                parted = ring.tile([P, HALF, P], F32, name="parted")
+            count = HALF if step == 0 else PACK
+            for d0 in range(0, PACK, count):
+                parted = ring.tile([P, count, P], F32, name="parted")
                 if g == 0:
-                    nc.scalar.activation(parted[:], stepped[:, d0 : d0 + HALF, :], SILU)
+                    nc.scalar.activation(parted[:], stepped[:, d0 : d0 + count, :], SILU)
                 else:
-                    nc.scalar.copy(parted[:], stepped[:, d0 : d0 + HALF, :])
-                turned = psum.tile([P, HALF, BLOCK], F32, name="turned", tag="turned", bufs=2)
-                for d in range(HALF):
+                    nc.scalar.copy(parted[:], stepped[:, d0 : d0 + count, :])
+                if step == 1:
+                    turned = psum.tile([P, count, BLOCK], F32, name="turned", tag="odd", bufs=1)
+                else:
+                    turned = psum.tile([P, count, BLOCK], F32, name="turned", tag="turned", bufs=2)
+                for d in range(count):
                     nc.tensor.transpose(turned[:, d, :], parted[:, d, :], ident[:])
-                nc.scalar.copy(staged[:, d0 : d0 + HALF, :], turned[:])
+                nc.scalar.copy(staged[:, d0 : d0 + count, :], turned[:])
 
         gather_scales(0, list_a)
         gather_scales(1, list_b)
-        got_w = [keep.tile([P, PASSES, T], U32, name="got_w%d" % g, tag=tag, align_bytes=64) for g, tag in enumerate(("words_a", "after_scales"))]
+        got_w = [keep.tile([P, PASSES, T], U32, name="got_w%d" % g, tag=tag, align_bytes=64) for g, tag in enumerate(("words_a", "words_b"))]
         for e in range(E1):
             gather_words(got_w[0], list_a, e * C1, C1)
         gather_words(got_w[1], list_b, 0, T)
-        sizes = [EXPERT] * (E1 - 1 + E2) + [2 * N, E2 * PASSES * H, N]
+        second_w = keep.tile([P, EXPERT], U8, name="second_w", tag="after_scales", align_bytes=64)
+        sizes = [EXPERT] * E2 + [2 * N, E2 * PASSES * H, N]
         late = keep.tile([P, sum(sizes)], U8, name="late", tag="after_words", align_bytes=64)
         parts = [late[:, sum(sizes[:i]) : sum(sizes[: i + 1])] for i in range(len(sizes))]
-        wa_w = [first_w[:]] + parts[: E1 - 1]
-        wb_w = parts[E1 - 1 : E1 - 1 + E2]
-        w2_w, wb_sc, w2_sc = parts[E1 - 1 + E2 :]
+        wa_w = [first_w[:], second_w[:]]
+        wb_w = parts[:E2]
+        w2_w, wb_sc, w2_sc = parts[E2:]
         load_words(nc.sync, wa_w[1], wa_words[1])
         load_scales(wb_sc, wb_scales.rearrange("e s b c -> (e s) b c"), E2 * PASSES)
         for e in range(E2):
@@ -144,7 +150,7 @@ def tile_moe_pool_silu_kernel(
         load_scales(w2_sc, w2_scales, 1)
         nc.sync.dma_start(out=w2_w.bitcast(I32), in_=w2_words[0].bitcast(I32))
 
-        left = keep.tile([P, PACK * T], F32, name="left", tag="after_scales", align_bytes=64)
+        left = keep.tile([P, PACK * T], F32, name="left", tag="words_b", align_bytes=64)
         right = keep.tile([P, PACK * T], F32, name="right", tag="moved1", align_bytes=64)
 
         win_a = [keep.tile([P, T], F32, name="win_a%d" % d) for d in range(PACK)]

@@ -150,9 +150,6 @@ def tile_moe_pool_silu_kernel(
         load_scales(w2_sc, w2_scales, 1)
         nc.sync.dma_start(out=w2_w.bitcast(I32), in_=w2_words[0].bitcast(I32))
 
-        left = keep.tile([P, PACK * T], F32, name="left", tag="words_b", align_bytes=64)
-        right = keep.tile([P, PACK * T], F32, name="right", tag="moved1", align_bytes=64)
-
         win_a = [keep.tile([P, T], F32, name="win_a%d" % d) for d in range(PACK)]
         for b in range(BLOCKS):
             staged_a = ring.tile([P, PACK, BLOCK], F32, name="staged_a")
@@ -164,43 +161,42 @@ def tile_moe_pool_silu_kernel(
                 )
 
         staged_c = keep.tile([P, PACK, T], F32, name="staged_c")
-        win_c = {d: keep.tile([P, T], F32, name="win_c%d" % d) for d in range(1, PACK)}
+        last = PACK - 1
+        win_c = [keep.tile([P, WIDE if d == last else T], F32, name="win_c%d" % d) for d in range(PACK)]
         for b in range(BLOCKS):
             e = b * BLOCK // C2
             slots = slice(b * BLOCK, (b + 1) * BLOCK)
             first_layer(1, b, wb_w[e], wb_sc, e, staged_c[:, :, slots])
-            for d in range(1, PACK):
+            for d in range(last):
                 nc.vector.tensor_copy(
                     win_c[d][:].indirect(list_b[:, b * BLOCK // 16 : (b + 1) * BLOCK // 16]), staged_c[:, d, slots]
                 )
+        nc.vector.tensor_copy(win_c[last][:].indirect(list_b[:]), staged_c[:, last, :])
 
-        for d in range(PACK):
-            side = right if d == 0 else left
-            nc.scalar.copy(side[:, d * T : (d + 1) * T], win_a[d][:])
-        for d in range(1, PACK):
-            nc.scalar.copy(right[:, d * T : (d + 1) * T], win_c[d][:])
-        nc.vector.tensor_copy(left[:].indirect(list_b[:]), staged_c[:, 0, :])
-
-        left_v = left[:].rearrange("p (d c i) -> p c d i", d=PACK, i=RUN)
-        right_v = right[:].rearrange("p (d c i) -> p c d i", d=PACK, i=RUN)
+        planes_h = keep.tile([P, PACK, T], BF16, name="planes_h")
+        for d in range(last):
+            nc.gpsimd.tensor_tensor(planes_h[:, d, :], win_a[d][:], win_c[d][:], MULT)
         out_v = out.rearrange("(b p) t -> p b t", p=P)
-        runs = BLOCK // RUN
         for j in range(BLOCKS):
+            tokens = slice(j * BLOCK, (j + 1) * BLOCK)
+            nc.vector.tensor_tensor(planes_h[:, last, tokens], win_a[last][:, tokens], win_c[last][:, tokens], MULT)
+        for j in range(BLOCKS):
+            tokens = slice(j * BLOCK, (j + 1) * BLOCK)
             h = ring.tile([P, BLOCK * PACK], BF16, name="h", align_bytes=64)
-            nc.vector.tensor_tensor(
-                h[:].rearrange("p (c i d) -> p c d i", d=PACK, i=RUN),
-                left_v[:, j * runs : (j + 1) * runs],
-                right_v[:, j * runs : (j + 1) * runs],
-                MULT,
-            )
+            woven = h[:].rearrange("p (c i d) -> p c d i", d=PACK, i=RUN)
+            apart = planes_h[:, :, tokens].rearrange("p d (c i) -> p c d i", i=RUN)
+            if j in (0, BLOCKS - 1):
+                nc.scalar.copy(woven, apart)
+            else:
+                nc.vector.tensor_copy(woven, apart)
             h_w = ring.tile([P, BLOCK], U32, name="h_w", align_bytes=64)
             h_sc = ring.tile([P, BLOCK], U8, name="h_sc", align_bytes=64)
             nc.vector.quantize_mx(out=h_w[:].bitcast(FP8X4), scales=h_sc[:], in_=h[:])
             result = ring.tile([P, N // P, BLOCK], F32, name="result")
+            acc = psum.tile([P, N // P, BLOCK], F32, name="acc2")
             for n in range(N // P):
-                acc = psum.tile([P, BLOCK], F32, name="acc2")
                 nc.tensor.matmul_mx(
-                    out=acc[:],
+                    out=acc[:, n, :],
                     lhsT=w2_w[:, n * 2 * P : (n + 1) * 2 * P].bitcast(FP4X4),
                     lhsT_scale=w2_sc[:, n * P : (n + 1) * P],
                     rhs=h_w[:].bitcast(FP8X4),
@@ -208,8 +204,8 @@ def tile_moe_pool_silu_kernel(
                     start=True,
                     stop=True,
                 )
-                if j == BLOCKS - 1 and n == 1:
-                    nc.vector.tensor_copy(result[:, n, :], acc[:])
-                else:
-                    nc.scalar.copy(result[:, n, :], acc[:])
+            if j % 2 == 0:
+                nc.scalar.copy(result[:], acc[:])
+            else:
+                nc.vector.tensor_copy(result[:], acc[:])
             nc.sync.dma_start(out=out_v[:, :, j * BLOCK : (j + 1) * BLOCK], in_=result[:])

@@ -150,7 +150,8 @@ def tile_moe_pool_silu_kernel(
         load_scales(w2_sc, w2_scales, 1)
         nc.sync.dma_start(out=w2_w.bitcast(I32), in_=w2_words[0].bitcast(I32))
 
-        win_a = [keep.tile([P, T], F32, name="win_a%d" % d) for d in range(PACK)]
+        last = 2
+        win_a = [keep.tile([P, 2 * T if d == last else T], F32, name="win_a%d" % d) for d in range(PACK)]
         for b in range(BLOCKS):
             staged_a = ring.tile([P, PACK, BLOCK], F32, name="staged_a")
             e = b * BLOCK // C1
@@ -161,51 +162,81 @@ def tile_moe_pool_silu_kernel(
                 )
 
         staged_c = keep.tile([P, PACK, T], F32, name="staged_c")
-        last = PACK - 1
-        win_c = [keep.tile([P, WIDE if d == last else T], F32, name="win_c%d" % d) for d in range(PACK)]
+        win_c = [keep.tile([P, width], F32, name="win_c%d" % d) for d, width in enumerate((T, T, 2 * T, WIDE))]
+        nc.gpsimd.memset(win_c[last][:, T:], 1.0)
         for b in range(BLOCKS):
             e = b * BLOCK // C2
             slots = slice(b * BLOCK, (b + 1) * BLOCK)
             first_layer(1, b, wb_w[e], wb_sc, e, staged_c[:, :, slots])
-            for d in range(last):
+        for first in range(0, T, T // 2):
+            for d in range(2):
                 nc.vector.tensor_copy(
-                    win_c[d][:].indirect(list_b[:, b * BLOCK // 16 : (b + 1) * BLOCK // 16]), staged_c[:, d, slots]
+                    win_c[d][:].indirect(list_b[:, first // 16 : (first + T // 2) // 16]),
+                    staged_c[:, d, first : first + T // 2],
                 )
-        nc.vector.tensor_copy(win_c[last][:].indirect(list_b[:]), staged_c[:, last, :])
+        for d in (3, last):
+            nc.vector.tensor_copy(win_c[d][:].indirect(list_b[:]), staged_c[:, d, :])
 
-        planes_h = keep.tile([P, PACK, T], BF16, name="planes_h")
-        for d in range(last):
+        planes_h = keep.tile([P, 2, T], BF16, name="planes_h")
+        for d in range(2):
             nc.gpsimd.tensor_tensor(planes_h[:, d, :], win_a[d][:], win_c[d][:], MULT)
-        out_v = out.rearrange("(b p) t -> p b t", p=P)
+        nc.gpsimd.tensor_tensor(win_a[last][:, T:], win_a[3][:], win_c[3][:, :T], MULT)
+        h = [keep.tile([P, BLOCK, PACK], BF16, name="h%d" % j, align_bytes=64) for j in range(BLOCKS)]
+        pairs = {j: keep.tile([P, 2, BLOCK, 2], BF16, name="pairs%d" % j) for j in range(BLOCKS) if j != BLOCKS - 2}
+        direct = BLOCKS - 2
         for j in range(BLOCKS):
+            low = h[j][:, :, 0:2] if j == direct else pairs[j][:, 0, :, :]
+            nc.scalar.copy(low, planes_h[:, :, j * BLOCK : (j + 1) * BLOCK].rearrange("p d t -> p t d"))
+        left = win_a[last][:].rearrange("p (d t) -> p t d", d=2)
+        right = win_c[last][:].rearrange("p (d t) -> p t d", d=2)
+
+        def product(j):
             tokens = slice(j * BLOCK, (j + 1) * BLOCK)
-            nc.vector.tensor_tensor(planes_h[:, last, tokens], win_a[last][:, tokens], win_c[last][:, tokens], MULT)
-        for j in range(BLOCKS):
-            tokens = slice(j * BLOCK, (j + 1) * BLOCK)
-            h = ring.tile([P, BLOCK * PACK], BF16, name="h", align_bytes=64)
-            woven = h[:].rearrange("p (c i d) -> p c d i", d=PACK, i=RUN)
-            apart = planes_h[:, :, tokens].rearrange("p d (c i) -> p c d i", i=RUN)
-            if j in (0, BLOCKS - 1):
-                nc.scalar.copy(woven, apart)
-            else:
-                nc.vector.tensor_copy(woven, apart)
+            if j == direct:
+                nc.vector.tensor_tensor(h[j][:, :, 2:4], left[:, tokens, :], right[:, tokens, :], MULT)
+                return
+            nc.vector.tensor_tensor(pairs[j][:, 1, :, :], left[:, tokens, :], right[:, tokens, :], MULT)
+            words = pairs[j][:].rearrange("p u t d -> p (u t d)").bitcast(F32).rearrange("p (u t) -> p t u", u=2)
+            nc.scalar.copy(h[j][:].rearrange("p t d -> p (t d)").bitcast(F32).rearrange("p (t u) -> p t u", u=2), words)
+
+        def second_layer(j):
             h_w = ring.tile([P, BLOCK], U32, name="h_w", align_bytes=64)
             h_sc = ring.tile([P, BLOCK], U8, name="h_sc", align_bytes=64)
-            nc.vector.quantize_mx(out=h_w[:].bitcast(FP8X4), scales=h_sc[:], in_=h[:])
-            result = ring.tile([P, N // P, BLOCK], F32, name="result")
-            acc = psum.tile([P, N // P, BLOCK], F32, name="acc2")
-            for n in range(N // P):
-                nc.tensor.matmul_mx(
-                    out=acc[:, n, :],
-                    lhsT=w2_w[:, n * 2 * P : (n + 1) * 2 * P].bitcast(FP4X4),
-                    lhsT_scale=w2_sc[:, n * P : (n + 1) * P],
-                    rhs=h_w[:].bitcast(FP8X4),
-                    rhs_scale=h_sc[:],
-                    start=True,
-                    stop=True,
-                )
-            if j % 2 == 0:
-                nc.scalar.copy(result[:], acc[:])
-            else:
-                nc.vector.tensor_copy(result[:], acc[:])
-            nc.sync.dma_start(out=out_v[:, :, j * BLOCK : (j + 1) * BLOCK], in_=result[:])
+            nc.vector.quantize_mx(out=h_w[:].bitcast(FP8X4), scales=h_sc[:], in_=h[j][:].rearrange("p t d -> p (t d)"))
+            parts_n = 2 if j == BLOCKS - 1 else 1
+            count = N // P // parts_n
+            banks = []
+            for part in range(parts_n):
+                acc = psum.tile([P, count, BLOCK], F32, name="acc2", tag="even" if part else "acc2", bufs=1 if part else 4)
+                banks.append(acc)
+                for m in range(count):
+                    n = part * count + m
+                    nc.tensor.matmul_mx(
+                        out=acc[:, m, :],
+                        lhsT=w2_w[:, n * 2 * P : (n + 1) * 2 * P].bitcast(FP4X4),
+                        lhsT_scale=w2_sc[:, n * P : (n + 1) * P],
+                        rhs=h_w[:].bitcast(FP8X4),
+                        rhs_scale=h_sc[:],
+                        start=True,
+                        stop=True,
+                    )
+            return banks
+
+        def leave(j, banks):
+            tokens = slice(j * BLOCK, (j + 1) * BLOCK)
+            count = N // P // len(banks)
+            for part, acc in enumerate(banks):
+                result = ring.tile([P, count, BLOCK], F32, name="result", bufs=5)
+                if (j + part) % 2 == 0:
+                    nc.scalar.copy(result[:], acc[:])
+                else:
+                    nc.vector.tensor_copy(result[:], acc[:])
+                queue = nc.scalar if part == 1 else nc.sync
+                queue.dma_start(out=out_v[:, part * count : (part + 1) * count, tokens], in_=result[:])
+
+        out_v = out.rearrange("(b p) t -> p b t", p=P)
+        for j in sorted(range(BLOCKS), key=lambda j: j == direct):
+            product(j)
+        sums = [second_layer(j) for j in range(BLOCKS)]
+        for j in range(BLOCKS):
+            leave(j, sums[j])

@@ -43,7 +43,7 @@ def tile_moe_pool_silu_kernel(
         list_b = lists.tile([P, T // 16], U16, name="list_b")
 
         x_sc = keep.tile([P, WIDE], U8, name="x_sc", tag="after_scales", align_bytes=64)
-        x_w = keep.tile([P, T + WIDE], I32, name="x_w", tag="after_words", align_bytes=64)
+        x_w = keep.tile([P, PASSES, WIDE], I32, name="x_w", tag="after_words", align_bytes=64)
         first_w = keep.tile([P, EXPERT], U8, name="first_w", align_bytes=64)
         wa_sc = keep.tile([P, E1 * PASSES * H], U8, name="wa_sc", align_bytes=64)
         got_sc = [keep.tile([P, T], U8, name="got_sc%d" % g, align_bytes=64) for g in range(2)]
@@ -51,8 +51,7 @@ def tile_moe_pool_silu_kernel(
         ident = keep.tile([P, P], F32, name="ident")
 
         nc.gpsimd.memset(x_sc[:].bitcast(I32), 0)
-        nc.gpsimd.memset(x_w[:, PASSES * T - 8 :], 0)
-        nc.gpsimd.memset(wa_sc[:].bitcast(I32), 0)
+        nc.gpsimd.memset(x_w[:, :, T:], 0)
         make_identity(nc, ident[:])
 
         def load_words(queue, tile, words):
@@ -70,17 +69,15 @@ def tile_moe_pool_silu_kernel(
                 )
 
         nc.sync.dma_start(list_a[:], offs)
-        nc.sync.dma_start(list_b[:], offs2)
         for q in range(4):
-            nc.sync.dma_start(
+            (nc.sync, nc.scalar)[q % 2].dma_start(
                 out=x_sc[32 * q : 32 * q + 8, 0:T].bitcast(I32),
                 in_=x_scales.bitcast(I32)[:, 4 * q : 4 * q + 4, :],
             )
-        nc.sync.dma_start(
-            out=x_w[:, : PASSES * T].rearrange("p (s t) -> p s t", s=PASSES),
-            in_=x_words.rearrange("s p t d -> p s (t d)").bitcast(I32),
-        )
-        load_words(nc.scalar, first_w[:], wa_words[0])
+        for s in range(PASSES):
+            nc.sync.dma_start(out=x_w[:, s, :T], in_=x_words[s].rearrange("p t d -> p (t d)").bitcast(I32))
+        nc.sync.dma_start(list_b[:], offs2)
+        load_words(nc.sync, first_w[:], wa_words[0])
         load_scales(wa_sc[:], wa_scales.rearrange("e s b c -> (e s) b c"), E1 * PASSES)
 
         def gather_scales(g, offsets):
@@ -93,7 +90,7 @@ def tile_moe_pool_silu_kernel(
 
         def gather_words(got, offsets, first, count):
             for s in range(PASSES):
-                window = x_w[:, s * T : s * T + WIDE].bitcast(U32)
+                window = x_w[:, s, :].bitcast(U32)
                 nc.vector.tensor_copy(
                     got[:, s, first : first + count], window.indirect(offsets[:, first // 16 : (first + count) // 16])
                 )
@@ -130,11 +127,11 @@ def tile_moe_pool_silu_kernel(
                     nc.tensor.transpose(turned[:, d, :], parted[:, d, :], ident[:])
                 nc.scalar.copy(staged[:, d0 : d0 + count, :], turned[:])
 
-        gather_scales(0, list_a)
-        gather_scales(1, list_b)
         got_w = [keep.tile([P, PASSES, T], U32, name="got_w%d" % g, tag=tag, align_bytes=64) for g, tag in enumerate(("words_a", "words_b"))]
-        for e in range(E1):
-            gather_words(got_w[0], list_a, e * C1, C1)
+        gather_scales(0, list_a)
+        gather_words(got_w[0], list_a, 0, C1)
+        gather_scales(1, list_b)
+        gather_words(got_w[0], list_a, C1, C1)
         gather_words(got_w[1], list_b, 0, T)
         second_w = keep.tile([P, EXPERT], U8, name="second_w", tag="after_scales", align_bytes=64)
         sizes = [EXPERT] * E2 + [2 * N, E2 * PASSES * H, N]
@@ -163,7 +160,7 @@ def tile_moe_pool_silu_kernel(
 
         staged_c = keep.tile([P, PACK, T], F32, name="staged_c")
         win_c = [keep.tile([P, width], F32, name="win_c%d" % d) for d, width in enumerate((T, T, 2 * T, WIDE))]
-        nc.gpsimd.memset(win_c[last][:, T:], 1.0)
+        nc.vector.memset(win_c[last][:, T:], 1.0)
         for b in range(BLOCKS):
             e = b * BLOCK // C2
             slots = slice(b * BLOCK, (b + 1) * BLOCK)

@@ -48,6 +48,7 @@ def tile_moe_pool_silu_kernel(
         wa_sc = keep.tile([P, E1 * PASSES * H], U8, name="wa_sc", align_bytes=64)
         got_sc = [keep.tile([P, T], U8, name="got_sc%d" % g, align_bytes=64) for g in range(2)]
         moved_sc = [keep.tile([P, T], U8, name="moved_sc%d" % g, tag="moved%d" % g, align_bytes=64) for g in range(2)]
+        w2_w = keep.tile([P, 2 * N], U8, name="w2_w", align_bytes=64)
         ident = keep.tile([P, P], F32, name="ident")
 
         nc.gpsimd.memset(x_sc[:].bitcast(I32), 0)
@@ -74,9 +75,9 @@ def tile_moe_pool_silu_kernel(
                 out=x_sc[32 * q : 32 * q + 8, 0:T].bitcast(I32),
                 in_=x_scales.bitcast(I32)[:, 4 * q : 4 * q + 4, :],
             )
-        for s in range(PASSES):
-            nc.sync.dma_start(out=x_w[:, s, :T], in_=x_words[s].rearrange("p t d -> p (t d)").bitcast(I32))
         nc.sync.dma_start(list_b[:], offs2)
+        nc.sync.dma_start(out=w2_w[:].bitcast(I32), in_=w2_words[0].bitcast(I32))
+        nc.sync.dma_start(out=x_w[:, :, :T], in_=x_words.rearrange("s p t d -> p s (t d)").bitcast(I32))
         load_words(nc.sync, first_w[:], wa_words[0])
         load_scales(wa_sc[:], wa_scales.rearrange("e s b c -> (e s) b c"), E1 * PASSES)
 
@@ -129,23 +130,22 @@ def tile_moe_pool_silu_kernel(
 
         got_w = [keep.tile([P, PASSES, T], U32, name="got_w%d" % g, tag=tag, align_bytes=64) for g, tag in enumerate(("words_a", "words_b"))]
         gather_scales(0, list_a)
-        gather_words(got_w[0], list_a, 0, C1)
         gather_scales(1, list_b)
+        gather_words(got_w[0], list_a, 0, C1)
         gather_words(got_w[0], list_a, C1, C1)
         gather_words(got_w[1], list_b, 0, T)
         second_w = keep.tile([P, EXPERT], U8, name="second_w", tag="after_scales", align_bytes=64)
-        sizes = [EXPERT] * E2 + [2 * N, E2 * PASSES * H, N]
+        sizes = [EXPERT] * E2 + [E2 * PASSES * H, N]
         late = keep.tile([P, sum(sizes)], U8, name="late", tag="after_words", align_bytes=64)
         parts = [late[:, sum(sizes[:i]) : sum(sizes[: i + 1])] for i in range(len(sizes))]
         wa_w = [first_w[:], second_w[:]]
         wb_w = parts[:E2]
-        w2_w, wb_sc, w2_sc = parts[E2:]
+        wb_sc, w2_sc = parts[E2:]
         load_words(nc.sync, wa_w[1], wa_words[1])
         load_scales(wb_sc, wb_scales.rearrange("e s b c -> (e s) b c"), E2 * PASSES)
         for e in range(E2):
             load_words(nc.sync, wb_w[e], wb_words[e])
         load_scales(w2_sc, w2_scales, 1)
-        nc.sync.dma_start(out=w2_w.bitcast(I32), in_=w2_words[0].bitcast(I32))
 
         last = 2
         win_a = [keep.tile([P, 2 * T if d == last else T], F32, name="win_a%d" % d) for d in range(PACK)]
@@ -160,7 +160,7 @@ def tile_moe_pool_silu_kernel(
 
         staged_c = keep.tile([P, PACK, T], F32, name="staged_c")
         win_c = [keep.tile([P, width], F32, name="win_c%d" % d) for d, width in enumerate((T, T, 2 * T, WIDE))]
-        nc.vector.memset(win_c[last][:, T:], 1.0)
+        nc.gpsimd.memset(win_c[last][:, T:], 1.0)
         for b in range(BLOCKS):
             e = b * BLOCK // C2
             slots = slice(b * BLOCK, (b + 1) * BLOCK)

@@ -48,10 +48,10 @@ def tile_moe_pool_silu_kernel(
         wa_sc = keep.tile([P, E1 * PASSES * H], U8, name="wa_sc", align_bytes=64)
         got_sc = [keep.tile([P, T], U8, name="got_sc%d" % g, align_bytes=64) for g in range(2)]
         moved_sc = [keep.tile([P, T], U8, name="moved_sc%d" % g, tag="moved%d" % g, align_bytes=64) for g in range(2)]
-        w2_w = keep.tile([P, 2 * N], U8, name="w2_w", align_bytes=64)
         ident = keep.tile([P, P], F32, name="ident")
 
-        nc.gpsimd.memset(x_sc[:].bitcast(I32), 0)
+        nc.gpsimd.memset(x_sc[:, :T].bitcast(I32), 0)
+        nc.gpsimd.memset(x_sc[:, T:].bitcast(I32), 0)
         nc.gpsimd.memset(x_w[:, :, T:], 0)
         make_identity(nc, ident[:])
 
@@ -71,14 +71,13 @@ def tile_moe_pool_silu_kernel(
 
         nc.sync.dma_start(list_a[:], offs)
         for q in range(4):
-            (nc.sync, nc.scalar)[q % 2].dma_start(
+            nc.sync.dma_start(
                 out=x_sc[32 * q : 32 * q + 8, 0:T].bitcast(I32),
                 in_=x_scales.bitcast(I32)[:, 4 * q : 4 * q + 4, :],
             )
         nc.sync.dma_start(list_b[:], offs2)
-        nc.sync.dma_start(out=w2_w[:].bitcast(I32), in_=w2_words[0].bitcast(I32))
         nc.sync.dma_start(out=x_w[:, :, :T], in_=x_words.rearrange("s p t d -> p s (t d)").bitcast(I32))
-        load_words(nc.sync, first_w[:], wa_words[0])
+        load_words(nc.scalar, first_w[:], wa_words[0])
         load_scales(wa_sc[:], wa_scales.rearrange("e s b c -> (e s) b c"), E1 * PASSES)
 
         def gather_scales(g, offsets):
@@ -135,17 +134,18 @@ def tile_moe_pool_silu_kernel(
         gather_words(got_w[0], list_a, C1, C1)
         gather_words(got_w[1], list_b, 0, T)
         second_w = keep.tile([P, EXPERT], U8, name="second_w", tag="after_scales", align_bytes=64)
-        sizes = [EXPERT] * E2 + [E2 * PASSES * H, N]
+        sizes = [EXPERT] * E2 + [2 * N, E2 * PASSES * H, N]
         late = keep.tile([P, sum(sizes)], U8, name="late", tag="after_words", align_bytes=64)
         parts = [late[:, sum(sizes[:i]) : sum(sizes[: i + 1])] for i in range(len(sizes))]
         wa_w = [first_w[:], second_w[:]]
         wb_w = parts[:E2]
-        wb_sc, w2_sc = parts[E2:]
+        w2_w, wb_sc, w2_sc = parts[E2:]
         load_words(nc.sync, wa_w[1], wa_words[1])
         load_scales(wb_sc, wb_scales.rearrange("e s b c -> (e s) b c"), E2 * PASSES)
         for e in range(E2):
             load_words(nc.sync, wb_w[e], wb_words[e])
         load_scales(w2_sc, w2_scales, 1)
+        nc.sync.dma_start(out=w2_w.bitcast(I32), in_=w2_words[0].bitcast(I32))
 
         last = 2
         win_a = [keep.tile([P, 2 * T if d == last else T], F32, name="win_a%d" % d) for d in range(PACK)]
@@ -179,61 +179,56 @@ def tile_moe_pool_silu_kernel(
             nc.gpsimd.tensor_tensor(planes_h[:, d, :], win_a[d][:], win_c[d][:], MULT)
         nc.gpsimd.tensor_tensor(win_a[last][:, T:], win_a[3][:], win_c[3][:, :T], MULT)
         h = [keep.tile([P, BLOCK, PACK], BF16, name="h%d" % j, align_bytes=64) for j in range(BLOCKS)]
-        pairs = {j: keep.tile([P, 2, BLOCK, 2], BF16, name="pairs%d" % j) for j in range(BLOCKS) if j != BLOCKS - 2}
-        direct = BLOCKS - 2
+        pairs = {j: keep.tile([P, 2, BLOCK, 2], BF16, name="pairs%d" % j) for j in range(0, BLOCKS, 2)}
         for j in range(BLOCKS):
-            low = h[j][:, :, 0:2] if j == direct else pairs[j][:, 0, :, :]
+            low = pairs[j][:, 0, :, :] if j in pairs else h[j][:, :, 0:2]
             nc.scalar.copy(low, planes_h[:, :, j * BLOCK : (j + 1) * BLOCK].rearrange("p d t -> p t d"))
         left = win_a[last][:].rearrange("p (d t) -> p t d", d=2)
         right = win_c[last][:].rearrange("p (d t) -> p t d", d=2)
 
         def product(j):
             tokens = slice(j * BLOCK, (j + 1) * BLOCK)
-            if j == direct:
+            if j not in pairs:
                 nc.vector.tensor_tensor(h[j][:, :, 2:4], left[:, tokens, :], right[:, tokens, :], MULT)
                 return
             nc.vector.tensor_tensor(pairs[j][:, 1, :, :], left[:, tokens, :], right[:, tokens, :], MULT)
             words = pairs[j][:].rearrange("p u t d -> p (u t d)").bitcast(F32).rearrange("p (u t) -> p t u", u=2)
             nc.scalar.copy(h[j][:].rearrange("p t d -> p (t d)").bitcast(F32).rearrange("p (t u) -> p t u", u=2), words)
 
+        banks = [("acc2", 4)] * 4 + [("turned", 2)] * 2 + [("even", 1), ("odd", 1)]
+
         def second_layer(j):
             h_w = ring.tile([P, BLOCK], U32, name="h_w", align_bytes=64)
             h_sc = ring.tile([P, BLOCK], U8, name="h_sc", align_bytes=64)
             nc.vector.quantize_mx(out=h_w[:].bitcast(FP8X4), scales=h_sc[:], in_=h[j][:].rearrange("p t d -> p (t d)"))
-            parts_n = 2 if j == BLOCKS - 1 else 1
-            count = N // P // parts_n
-            banks = []
-            for part in range(parts_n):
-                acc = psum.tile([P, count, BLOCK], F32, name="acc2", tag="even" if part else "acc2", bufs=1 if part else 4)
-                banks.append(acc)
-                for m in range(count):
-                    n = part * count + m
-                    nc.tensor.matmul_mx(
-                        out=acc[:, m, :],
-                        lhsT=w2_w[:, n * 2 * P : (n + 1) * 2 * P].bitcast(FP4X4),
-                        lhsT_scale=w2_sc[:, n * P : (n + 1) * P],
-                        rhs=h_w[:].bitcast(FP8X4),
-                        rhs_scale=h_sc[:],
-                        start=True,
-                        stop=True,
-                    )
-            return banks
+            for n in range(N // P):
+                tag, bufs = banks.pop(0)
+                acc = psum.tile([P, BLOCK], F32, name="acc2", tag=tag, bufs=bufs)
+                nc.tensor.matmul_mx(
+                    out=acc[:],
+                    lhsT=w2_w[:, n * 2 * P : (n + 1) * 2 * P].bitcast(FP4X4),
+                    lhsT_scale=w2_sc[:, n * P : (n + 1) * P],
+                    rhs=h_w[:].bitcast(FP8X4),
+                    rhs_scale=h_sc[:],
+                    start=True,
+                    stop=True,
+                )
+                sums.append((j, n, acc))
 
-        def leave(j, banks):
-            tokens = slice(j * BLOCK, (j + 1) * BLOCK)
-            count = N // P // len(banks)
-            for part, acc in enumerate(banks):
-                result = ring.tile([P, count, BLOCK], F32, name="result", bufs=5)
-                if (j + part) % 2 == 0:
-                    nc.scalar.copy(result[:], acc[:])
-                else:
-                    nc.vector.tensor_copy(result[:], acc[:])
-                queue = nc.scalar if part == 1 else nc.sync
-                queue.dma_start(out=out_v[:, part * count : (part + 1) * count, tokens], in_=result[:])
-
-        out_v = out.rearrange("(b p) t -> p b t", p=P)
-        for j in sorted(range(BLOCKS), key=lambda j: j == direct):
-            product(j)
-        sums = [second_layer(j) for j in range(BLOCKS)]
-        for j in range(BLOCKS):
-            leave(j, sums[j])
+        sums = []
+        product(0)
+        product(1)
+        product(2)
+        second_layer(1)
+        second_layer(0)
+        product(3)
+        second_layer(2)
+        second_layer(3)
+        for j, n, acc in sums:
+            result = ring.tile([P, BLOCK], F32, name="result", bufs=8)
+            if j >= BLOCKS // 2 and n == 1:
+                nc.vector.tensor_copy(result[:], acc[:])
+            else:
+                nc.scalar.copy(result[:], acc[:])
+            queue = nc.scalar if (j, n) == (BLOCKS - 1, 0) else nc.sync
+            queue.dma_start(out=out[n * P : (n + 1) * P, j * BLOCK : (j + 1) * BLOCK], in_=result[:])

@@ -112,8 +112,7 @@ def tile_moe_pool_silu_kernel(
                     stop=(s == PASSES - 1),
                 )
             stepped = acc[:].rearrange("u (m d) -> u d m", d=PACK)
-            count = HALF if step == 0 else PACK
-            for d0 in range(0, PACK, count):
+            for d0, count in ((0, 1), (1, 1), (2, 2)) if step == 0 else ((0, PACK),):
                 parted = ring.tile([P, count, P], F32, name="parted")
                 if g == 0:
                     nc.scalar.activation(parted[:], stepped[:, d0 : d0 + count, :], SILU)
@@ -130,8 +129,8 @@ def tile_moe_pool_silu_kernel(
         got_w = [keep.tile([P, PASSES, T], U32, name="got_w%d" % g, tag=tag, align_bytes=64) for g, tag in enumerate(("words_a", "words_b"))]
         gather_scales(0, list_a)
         gather_scales(1, list_b)
-        gather_words(got_w[0], list_a, 0, C1)
-        gather_words(got_w[0], list_a, C1, C1)
+        gather_words(got_w[0], list_a, 0, BLOCK)
+        gather_words(got_w[0], list_a, BLOCK, T - BLOCK)
         gather_words(got_w[1], list_b, 0, T)
         second_w = keep.tile([P, EXPERT], U8, name="second_w", tag="after_scales", align_bytes=64)
         sizes = [EXPERT] * E2 + [2 * N, E2 * PASSES * H, N]
@@ -149,13 +148,14 @@ def tile_moe_pool_silu_kernel(
 
         last = 2
         win_a = [keep.tile([P, 2 * T if d == last else T], F32, name="win_a%d" % d) for d in range(PACK)]
-        for b in range(BLOCKS):
-            staged_a = ring.tile([P, PACK, BLOCK], F32, name="staged_a")
-            e = b * BLOCK // C1
-            first_layer(0, b, wa_w[e], wa_sc, e, staged_a[:])
+        for first, count in ((0, BLOCK), (BLOCK, BLOCK), (C1, C1)):
+            staged_a = ring.tile([P, PACK, count], F32, name="staged_a", bufs=3)
+            for at in range(0, count, BLOCK):
+                e = first // C1
+                first_layer(0, (first + at) // BLOCK, wa_w[e], wa_sc, e, staged_a[:, :, at : at + BLOCK])
             for d in range(PACK):
                 nc.vector.tensor_copy(
-                    win_a[d][:].indirect(list_a[:, b * BLOCK // 16 : (b + 1) * BLOCK // 16]), staged_a[:, d, :]
+                    win_a[d][:].indirect(list_a[:, first // 16 : (first + count) // 16]), staged_a[:, d, :]
                 )
 
         staged_c = keep.tile([P, PACK, T], F32, name="staged_c")

@@ -98,7 +98,10 @@ def tile_moe_pool_silu_kernel(
         def first_layer(g, b, words, scales, e, staged):
             slots = slice(b * BLOCK, (b + 1) * BLOCK)
             step = g * BLOCKS + b
-            acc = psum.tile([P, H], F32, name="acc", tag="odd" if step > 2 and step % 2 else "even", bufs=1)
+            if g == 0:
+                acc = psum.tile([P, H], F32, name="acc", tag="sums%d" % max(b, 1), bufs=1)
+            else:
+                acc = psum.tile([P, H], F32, name="acc", tag="odd" if b % 2 else "sums3", bufs=1)
             planes = (got_sc[g], moved_sc[g])
             for s in range(PASSES):
                 a = e * PASSES + s
@@ -118,7 +121,9 @@ def tile_moe_pool_silu_kernel(
                     nc.scalar.activation(parted[:], stepped[:, d0 : d0 + count, :], SILU)
                 else:
                     nc.scalar.copy(parted[:], stepped[:, d0 : d0 + count, :])
-                if step == 1:
+                if step == 0 and d0 > 0:
+                    turned = psum.tile([P, count, BLOCK], F32, name="turned", tag="sums%d" % (d0 + 1), bufs=1)
+                elif step in (1, 3):
                     turned = psum.tile([P, count, BLOCK], F32, name="turned", tag="odd", bufs=1)
                 else:
                     turned = psum.tile([P, count, BLOCK], F32, name="turned", tag="turned", bufs=2)
@@ -151,7 +156,7 @@ def tile_moe_pool_silu_kernel(
         for first, count in ((0, BLOCK), (BLOCK, BLOCK), (C1, C1)):
             staged_a = ring.tile([P, PACK, count], F32, name="staged_a", bufs=3)
             for at in range(0, count, BLOCK):
-                e = first // C1
+                e = (first + at) // C1
                 first_layer(0, (first + at) // BLOCK, wa_w[e], wa_sc, e, staged_a[:, :, at : at + BLOCK])
             for d in range(PACK):
                 nc.vector.tensor_copy(
@@ -159,43 +164,37 @@ def tile_moe_pool_silu_kernel(
                 )
 
         staged_c = keep.tile([P, PACK, T], F32, name="staged_c")
-        win_c = [keep.tile([P, width], F32, name="win_c%d" % d) for d, width in enumerate((T, T, 2 * T, WIDE))]
-        nc.gpsimd.memset(win_c[last][:, T:], 1.0)
+        win_c = [keep.tile([P, width], F32, name="win_c%d" % d) for d, width in enumerate((WIDE, WIDE, 2 * T, WIDE))]
+        nc.gpsimd.memset(win_c[last][:, T : T + T // 2], 1.0)
         for b in range(BLOCKS):
             e = b * BLOCK // C2
             slots = slice(b * BLOCK, (b + 1) * BLOCK)
             first_layer(1, b, wb_w[e], wb_sc, e, staged_c[:, :, slots])
-        for first in range(0, T, T // 2):
-            for d in range(2):
-                nc.vector.tensor_copy(
-                    win_c[d][:].indirect(list_b[:, first // 16 : (first + T // 2) // 16]),
-                    staged_c[:, d, first : first + T // 2],
-                )
-        for d in (3, last):
+        for d in (0, 1, 3, last):
             nc.vector.tensor_copy(win_c[d][:].indirect(list_b[:]), staged_c[:, d, :])
 
         planes_h = keep.tile([P, 2, T], BF16, name="planes_h")
         for d in range(2):
-            nc.gpsimd.tensor_tensor(planes_h[:, d, :], win_a[d][:], win_c[d][:], MULT)
-        nc.gpsimd.tensor_tensor(win_a[last][:, T:], win_a[3][:], win_c[3][:, :T], MULT)
+            nc.gpsimd.tensor_tensor(planes_h[:, d, :], win_a[d][:], win_c[d][:, :T], MULT)
+        high = keep.tile([P, 2, T // 2], BF16, name="high")
+        nc.gpsimd.tensor_tensor(win_a[last][:, T : T + T // 2], win_a[3][:, : T // 2], win_c[3][:, : T // 2], MULT)
+        nc.gpsimd.tensor_tensor(high[:, 1, :], win_a[3][:, T // 2 :], win_c[3][:, T // 2 : T], MULT)
         h = [keep.tile([P, BLOCK, PACK], BF16, name="h%d" % j, align_bytes=64) for j in range(BLOCKS)]
-        pairs = {j: keep.tile([P, 2, BLOCK, 2], BF16, name="pairs%d" % j) for j in range(0, BLOCKS, 2)}
         for j in range(BLOCKS):
-            low = pairs[j][:, 0, :, :] if j in pairs else h[j][:, :, 0:2]
-            nc.scalar.copy(low, planes_h[:, :, j * BLOCK : (j + 1) * BLOCK].rearrange("p d t -> p t d"))
+            nc.scalar.copy(h[j][:, :, 0:2], planes_h[:, :, j * BLOCK : (j + 1) * BLOCK].rearrange("p d t -> p t d"))
         left = win_a[last][:].rearrange("p (d t) -> p t d", d=2)
         right = win_c[last][:].rearrange("p (d t) -> p t d", d=2)
 
         def product(j):
             tokens = slice(j * BLOCK, (j + 1) * BLOCK)
-            if j not in pairs:
+            if j < BLOCKS // 2:
                 nc.vector.tensor_tensor(h[j][:, :, 2:4], left[:, tokens, :], right[:, tokens, :], MULT)
                 return
-            nc.vector.tensor_tensor(pairs[j][:, 1, :, :], left[:, tokens, :], right[:, tokens, :], MULT)
-            words = pairs[j][:].rearrange("p u t d -> p (u t d)").bitcast(F32).rearrange("p (u t) -> p t u", u=2)
-            nc.scalar.copy(h[j][:].rearrange("p t d -> p (t d)").bitcast(F32).rearrange("p (t u) -> p t u", u=2), words)
+            part = slice(j * BLOCK - T // 2, (j + 1) * BLOCK - T // 2)
+            nc.vector.tensor_tensor(high[:, 0, part], win_a[last][:, tokens], win_c[last][:, tokens], MULT)
+            nc.scalar.copy(h[j][:, :, 2:4], high[:, :, part].rearrange("p d t -> p t d"))
 
-        banks = [("acc2", 4)] * 4 + [("turned", 2)] * 2 + [("even", 1), ("odd", 1)]
+        banks = [("sums%d" % b, 1) for b in range(BLOCKS)] + [("turned", 2)] * 2 + [("spare", 1), ("odd", 1)]
 
         def second_layer(j):
             h_w = ring.tile([P, BLOCK], U32, name="h_w", align_bytes=64)
@@ -216,19 +215,19 @@ def tile_moe_pool_silu_kernel(
                 sums.append((j, n, acc))
 
         sums = []
-        product(0)
-        product(1)
         product(2)
-        second_layer(1)
-        second_layer(0)
         product(3)
+        product(0)
         second_layer(2)
+        second_layer(0)
+        product(1)
         second_layer(3)
+        second_layer(1)
         for j, n, acc in sums:
             result = ring.tile([P, BLOCK], F32, name="result", bufs=8)
-            if j >= BLOCKS // 2 and n == 1:
+            if j % 2 and n == 1:
                 nc.vector.tensor_copy(result[:], acc[:])
             else:
                 nc.scalar.copy(result[:], acc[:])
-            queue = nc.scalar if (j, n) == (BLOCKS - 1, 0) else nc.sync
+            queue = nc.scalar if (j, n) == (1, 0) else nc.sync
             queue.dma_start(out=out[n * P : (n + 1) * P, j * BLOCK : (j + 1) * BLOCK], in_=result[:])

@@ -77,7 +77,7 @@ def tile_moe_pool_silu_kernel(
             )
         nc.sync.dma_start(list_b[:], offs2)
         nc.sync.dma_start(out=x_w[:, :, :T], in_=x_words.rearrange("s p t d -> p s (t d)").bitcast(I32))
-        load_words(nc.scalar, first_w[:], wa_words[0])
+        load_words(nc.sync, first_w[:], wa_words[0])
         load_scales(wa_sc[:], wa_scales.rearrange("e s b c -> (e s) b c"), E1 * PASSES)
 
         def gather_scales(g, offsets):

@@ -47,10 +47,11 @@ def tile_moe_pool_silu_kernel(
         first_w = keep.tile([P, EXPERT], U8, name="first_w", align_bytes=64)
         wa_sc = keep.tile([P, E1 * PASSES * H], U8, name="wa_sc", align_bytes=64)
         got_sc = [keep.tile([P, T], U8, name="got_sc%d" % g, align_bytes=64) for g in range(2)]
-        moved_sc = [keep.tile([P, T], U8, name="moved_sc%d" % g, tag="moved%d" % g, align_bytes=64) for g in range(2)]
+        moved_sc = [[keep.tile([P, T], U8, name="moved_sc%d%d" % (g, s), align_bytes=64) for s in range(PASSES)] for g in range(2)]
         ident = keep.tile([P, P], F32, name="ident")
 
-        nc.gpsimd.memset(x_sc[:, :T].bitcast(I32), 0)
+        nc.gpsimd.memset(x_sc[32:64, :T].bitcast(I32), 0)
+        nc.gpsimd.memset(x_sc[64:, :T].bitcast(I32), 0)
         nc.gpsimd.memset(x_sc[:, T:].bitcast(I32), 0)
         nc.gpsimd.memset(x_w[:, :, T:], 0)
         make_identity(nc, ident[:])
@@ -70,11 +71,7 @@ def tile_moe_pool_silu_kernel(
                 )
 
         nc.sync.dma_start(list_a[:], offs)
-        for q in range(4):
-            nc.sync.dma_start(
-                out=x_sc[32 * q : 32 * q + 8, 0:T].bitcast(I32),
-                in_=x_scales.bitcast(I32)[:, 4 * q : 4 * q + 4, :],
-            )
+        nc.sync.dma_start(out=x_sc[:32, :T].bitcast(I32), in_=x_scales.bitcast(I32).rearrange("s b c -> (s b) c"))
         nc.sync.dma_start(list_b[:], offs2)
         nc.sync.dma_start(out=x_w[:, :, :T], in_=x_words.rearrange("s p t d -> p s (t d)").bitcast(I32))
         load_words(nc.sync, first_w[:], wa_words[0])
@@ -82,11 +79,13 @@ def tile_moe_pool_silu_kernel(
 
         def gather_scales(g, offsets):
             nc.vector.tensor_copy(got_sc[g][:], x_sc[:].indirect(offsets[:]))
-            for first, count in ((0, 64), (64, 32), (96, 4)):
-                nc.sync.dma_start(
-                    out=moved_sc[g][first : first + count, :].bitcast(I32),
-                    in_=got_sc[g][first + 4 : first + 4 + count, :].bitcast(I32),
-                )
+            for s in range(PASSES):
+                for q in range(4):
+                    at = 16 * s + 4 * q
+                    nc.sync.dma_start(
+                        out=moved_sc[g][s][32 * q : 32 * q + 4, :].bitcast(I32),
+                        in_=got_sc[g][at : at + 4, :].bitcast(I32),
+                    )
 
         def gather_words(got, offsets, first, count):
             for s in range(PASSES):
@@ -102,7 +101,7 @@ def tile_moe_pool_silu_kernel(
                 acc = psum.tile([P, H], F32, name="acc", tag="sums%d" % max(b, 1), bufs=1)
             else:
                 acc = psum.tile([P, H], F32, name="acc", tag="odd" if b % 2 else "sums3", bufs=1)
-            planes = (got_sc[g], moved_sc[g])
+            planes = moved_sc[g]
             for s in range(PASSES):
                 a = e * PASSES + s
                 nc.tensor.matmul_mx(

@@ -169,14 +169,15 @@ def tile_moe_pool_silu_kernel(
             e = b * BLOCK // C2
             slots = slice(b * BLOCK, (b + 1) * BLOCK)
             first_layer(1, b, wb_w[e], wb_sc, e, staged_c[:, :, slots])
-        for d in (0, 1, 3, last):
+        for d in (3, 0, 1, last):
             nc.vector.tensor_copy(win_c[d][:].indirect(list_b[:]), staged_c[:, d, :])
 
         planes_h = keep.tile([P, 2, T], BF16, name="planes_h")
-        for d in range(2):
-            nc.gpsimd.tensor_tensor(planes_h[:, d, :], win_a[d][:], win_c[d][:, :T], MULT)
-        high = keep.tile([P, 2, T // 2], BF16, name="high")
+        high = keep.tile([P, 2, T // 2], BF16, name="high", tag="high")
         nc.gpsimd.tensor_tensor(win_a[last][:, T : T + T // 2], win_a[3][:, : T // 2], win_c[3][:, : T // 2], MULT)
+        nc.gpsimd.tensor_tensor(planes_h[:, 0, :], win_a[0][:], win_c[0][:, :T], MULT)
+        for half in (slice(0, T // 2), slice(T // 2, T)):
+            nc.gpsimd.tensor_tensor(planes_h[:, 1, half], win_a[1][:, half], win_c[1][:, half], MULT)
         nc.gpsimd.tensor_tensor(high[:, 1, :], win_a[3][:, T // 2 :], win_c[3][:, T // 2 : T], MULT)
         h = [keep.tile([P, BLOCK, PACK], BF16, name="h%d" % j, align_bytes=64) for j in range(BLOCKS)]
         for j in range(BLOCKS):
@@ -184,13 +185,29 @@ def tile_moe_pool_silu_kernel(
         left = win_a[last][:].rearrange("p (d t) -> p t d", d=2)
         right = win_c[last][:].rearrange("p (d t) -> p t d", d=2)
 
+        factors = psum.tile([P, PACK, BLOCK], F32, name="factors", tag="spare", bufs=1)
+        columns = (0, T, 2 * BLOCK, 3 * BLOCK)
+        for group in ((0, 1, 2, 3),):
+            there = psum.tile([P, PACK, BLOCK], F32, name="there", tag="odd", bufs=1)
+            between = keep.tile([P, PACK, BLOCK], F32, name="between%d" % group[0])
+            for k, f in enumerate(group):
+                nc.tensor.transpose(there[:, k, :], win_a[last][:, columns[f] : columns[f] + BLOCK], ident[:])
+            nc.scalar.copy(between[:, : len(group), :], there[:, : len(group), :])
+            for k, f in enumerate(group):
+                nc.tensor.transpose(factors[:, f, :], between[:, k, :], ident[:])
+
         def product(j):
             tokens = slice(j * BLOCK, (j + 1) * BLOCK)
-            if j < BLOCKS // 2:
-                nc.vector.tensor_tensor(h[j][:, :, 2:4], left[:, tokens, :], right[:, tokens, :], MULT)
+            if j == 0:
+                nc.vector.tensor_tensor(
+                    h[j][:, :, 2:4], factors[:, 0:2, :].rearrange("p d t -> p t d"), right[:, tokens, :], MULT
+                )
+                return
+            if j == 1:
+                nc.gpsimd.tensor_tensor(h[j][:, :, 2:4], left[:, tokens, :], right[:, tokens, :], MULT)
                 return
             part = slice(j * BLOCK - T // 2, (j + 1) * BLOCK - T // 2)
-            nc.vector.tensor_tensor(high[:, 0, part], win_a[last][:, tokens], win_c[last][:, tokens], MULT)
+            nc.vector.tensor_tensor(high[:, 0, part], factors[:, j, :], win_c[last][:, tokens], MULT)
             nc.scalar.copy(h[j][:, :, 2:4], high[:, :, part].rearrange("p d t -> p t d"))
 
         banks = [("sums%d" % b, 1) for b in range(BLOCKS)] + [("turned", 2)] * 2 + [("spare", 1), ("odd", 1)]
@@ -214,19 +231,20 @@ def tile_moe_pool_silu_kernel(
                 sums.append((j, n, acc))
 
         sums = []
+        product(1)
         product(2)
         product(3)
         product(0)
-        second_layer(2)
         second_layer(0)
-        product(1)
-        second_layer(3)
         second_layer(1)
+        second_layer(2)
+        second_layer(3)
+        first = keep.tile([P, N // P, BLOCK], F32, name="first", tag="high")
         for j, n, acc in sums:
-            result = ring.tile([P, BLOCK], F32, name="result", bufs=8)
-            if j % 2 and n == 1:
+            result = first[:, n, :] if j == 0 else ring.tile([P, BLOCK], F32, name="result", bufs=8)
+            if j >= 2 and n == 1:
                 nc.vector.tensor_copy(result[:], acc[:])
             else:
                 nc.scalar.copy(result[:], acc[:])
-            queue = nc.scalar if (j, n) == (1, 0) else nc.sync
+            queue = nc.scalar if (j, n) == (3, 0) else nc.sync
             queue.dma_start(out=out[n * P : (n + 1) * P, j * BLOCK : (j + 1) * BLOCK], in_=result[:])

@@ -25,7 +25,7 @@ BLOCK = 128
 BLOCKS = T // BLOCK
 WIDE = 704
 RUN = 4
-HALF = 2
+ORDER = (0, 1, 3, 2)
 EXPERT = PASSES * 2 * H
 
 
@@ -37,6 +37,7 @@ def tile_moe_pool_silu_kernel(
         lists = ctx.enter_context(tc.tile_pool(name="lists", bufs=1))
         keep = ctx.enter_context(tc.tile_pool(name="keep", bufs=1))
         ring = ctx.enter_context(tc.tile_pool(name="ring", bufs=4))
+        shared = ctx.enter_context(tc.tile_pool(name="shared", bufs=1))
         psum = ctx.enter_context(tc.psum_pool(name="psum", bufs=4))
 
         list_a = lists.tile([P, T // 16], U16, name="list_a")
@@ -127,8 +128,12 @@ def tile_moe_pool_silu_kernel(
                 else:
                     turned = psum.tile([P, count, BLOCK], F32, name="turned", tag="turned", bufs=2)
                 for d in range(count):
-                    nc.tensor.transpose(turned[:, d, :], parted[:, d, :], ident[:])
-                nc.scalar.copy(staged[:, d0 : d0 + count, :], turned[:])
+                    nc.tensor.transpose(turned[:, d, :], parted[:, ORDER[d] if g else d, :], ident[:])
+                if g == 0:
+                    nc.scalar.copy(staged[:, d0 : d0 + count, :], turned[:])
+                else:
+                    nc.scalar.copy(staged[0], turned[:, : PACK - 1, :])
+                    nc.scalar.copy(staged[1], turned[:, PACK - 1 :, :])
 
         got_w = [keep.tile([P, PASSES, T], U32, name="got_w%d" % g, tag=tag, align_bytes=64) for g, tag in enumerate(("words_a", "words_b"))]
         gather_scales(0, list_a)
@@ -137,18 +142,17 @@ def tile_moe_pool_silu_kernel(
         gather_words(got_w[0], list_a, BLOCK, T - BLOCK)
         gather_words(got_w[1], list_b, 0, T)
         second_w = keep.tile([P, EXPERT], U8, name="second_w", tag="after_scales", align_bytes=64)
-        sizes = [EXPERT] * E2 + [2 * N, E2 * PASSES * H, N]
+        sizes = [EXPERT] * E2 + [E2 * PASSES * H, N]
         late = keep.tile([P, sum(sizes)], U8, name="late", tag="after_words", align_bytes=64)
         parts = [late[:, sum(sizes[:i]) : sum(sizes[: i + 1])] for i in range(len(sizes))]
         wa_w = [first_w[:], second_w[:]]
         wb_w = parts[:E2]
-        w2_w, wb_sc, w2_sc = parts[E2:]
+        wb_sc, w2_sc = parts[E2:]
         load_words(nc.sync, wa_w[1], wa_words[1])
         load_scales(wb_sc, wb_scales.rearrange("e s b c -> (e s) b c"), E2 * PASSES)
         for e in range(E2):
             load_words(nc.sync, wb_w[e], wb_words[e])
         load_scales(w2_sc, w2_scales, 1)
-        nc.sync.dma_start(out=w2_w.bitcast(I32), in_=w2_words[0].bitcast(I32))
 
         last = 2
         win_a = [keep.tile([P, 2 * T if d == last else T], F32, name="win_a%d" % d) for d in range(PACK)]
@@ -162,52 +166,41 @@ def tile_moe_pool_silu_kernel(
                     win_a[d][:].indirect(list_a[:, first // 16 : (first + count) // 16]), staged_a[:, d, :]
                 )
 
-        staged_c = keep.tile([P, PACK, T], F32, name="staged_c")
+        staged_c = [
+            shared.tile([P, PACK - 1, T], F32, name="staged_early", offset=4 * T, align_bytes=64),
+            shared.tile([P, 1, T], F32, name="staged_last", offset=0, align_bytes=64),
+        ]
         win_c = [keep.tile([P, width], F32, name="win_c%d" % d) for d, width in enumerate((WIDE, WIDE, 2 * T, WIDE))]
         nc.gpsimd.memset(win_c[last][:, T : T + T // 2], 1.0)
         for b in range(BLOCKS):
             e = b * BLOCK // C2
             slots = slice(b * BLOCK, (b + 1) * BLOCK)
-            first_layer(1, b, wb_w[e], wb_sc, e, staged_c[:, :, slots])
-        for d in (3, 0, 1, last):
-            nc.vector.tensor_copy(win_c[d][:].indirect(list_b[:]), staged_c[:, d, :])
+            first_layer(1, b, wb_w[e], wb_sc, e, [pair[:, :, slots] for pair in staged_c])
+        for k, d in enumerate(ORDER):
+            nc.vector.tensor_copy(win_c[d][:].indirect(list_b[:]), staged_c[k // 3][:, k % 3, :])
 
         planes_h = keep.tile([P, 2, T], BF16, name="planes_h")
         high = keep.tile([P, 2, T // 2], BF16, name="high", tag="high")
+        for d in range(2):
+            nc.gpsimd.tensor_tensor(planes_h[:, d, :], win_a[d][:], win_c[d][:, :T], MULT)
         nc.gpsimd.tensor_tensor(win_a[last][:, T : T + T // 2], win_a[3][:, : T // 2], win_c[3][:, : T // 2], MULT)
-        nc.gpsimd.tensor_tensor(planes_h[:, 0, :], win_a[0][:], win_c[0][:, :T], MULT)
-        for half in (slice(0, T // 2), slice(T // 2, T)):
-            nc.gpsimd.tensor_tensor(planes_h[:, 1, half], win_a[1][:, half], win_c[1][:, half], MULT)
         nc.gpsimd.tensor_tensor(high[:, 1, :], win_a[3][:, T // 2 :], win_c[3][:, T // 2 : T], MULT)
-        h = [keep.tile([P, BLOCK, PACK], BF16, name="h%d" % j, align_bytes=64) for j in range(BLOCKS)]
+        h = [keep.tile([P, BLOCK, PACK], BF16, name="h%d" % j, tag="h%d" % j, align_bytes=64) for j in range(BLOCKS)]
         for j in range(BLOCKS):
             nc.scalar.copy(h[j][:, :, 0:2], planes_h[:, :, j * BLOCK : (j + 1) * BLOCK].rearrange("p d t -> p t d"))
         left = win_a[last][:].rearrange("p (d t) -> p t d", d=2)
         right = win_c[last][:].rearrange("p (d t) -> p t d", d=2)
 
-        factors = psum.tile([P, PACK, BLOCK], F32, name="factors", tag="spare", bufs=1)
-        columns = (0, T, 2 * BLOCK, 3 * BLOCK)
-        for group in ((0, 1, 2, 3),):
-            there = psum.tile([P, PACK, BLOCK], F32, name="there", tag="odd", bufs=1)
-            between = keep.tile([P, PACK, BLOCK], F32, name="between%d" % group[0])
-            for k, f in enumerate(group):
-                nc.tensor.transpose(there[:, k, :], win_a[last][:, columns[f] : columns[f] + BLOCK], ident[:])
-            nc.scalar.copy(between[:, : len(group), :], there[:, : len(group), :])
-            for k, f in enumerate(group):
-                nc.tensor.transpose(factors[:, f, :], between[:, k, :], ident[:])
+        w2_w = shared.tile([P, 2 * N], U8, name="w2_w", offset=4 * T, align_bytes=64)
+        nc.sync.dma_start(out=w2_w[:].bitcast(I32), in_=w2_words[0].bitcast(I32))
 
         def product(j):
             tokens = slice(j * BLOCK, (j + 1) * BLOCK)
-            if j == 0:
-                nc.vector.tensor_tensor(
-                    h[j][:, :, 2:4], factors[:, 0:2, :].rearrange("p d t -> p t d"), right[:, tokens, :], MULT
-                )
-                return
-            if j == 1:
-                nc.gpsimd.tensor_tensor(h[j][:, :, 2:4], left[:, tokens, :], right[:, tokens, :], MULT)
+            if j < BLOCKS // 2:
+                nc.vector.tensor_tensor(h[j][:, :, 2:4], left[:, tokens, :], right[:, tokens, :], MULT)
                 return
             part = slice(j * BLOCK - T // 2, (j + 1) * BLOCK - T // 2)
-            nc.vector.tensor_tensor(high[:, 0, part], factors[:, j, :], win_c[last][:, tokens], MULT)
+            nc.vector.tensor_tensor(high[:, 0, part], win_a[last][:, tokens], win_c[last][:, tokens], MULT)
             nc.scalar.copy(h[j][:, :, 2:4], high[:, :, part].rearrange("p d t -> p t d"))
 
         banks = [("sums%d" % b, 1) for b in range(BLOCKS)] + [("turned", 2)] * 2 + [("spare", 1), ("odd", 1)]
@@ -230,21 +223,38 @@ def tile_moe_pool_silu_kernel(
                 )
                 sums.append((j, n, acc))
 
+        unread = psum.tile([P, T], F32, name="unread", tag="odd", bufs=1)
+        for k in range(4):
+            nc.tensor.matmul_mx(
+                out=unread[:],
+                lhsT=w2_w[:, : 2 * P].bitcast(FP4X4),
+                lhsT_scale=w2_sc[:, :P],
+                rhs=got_w[1][:, 0, :].bitcast(FP8X4),
+                rhs_scale=moved_sc[1][0][:],
+                start=True,
+                stop=True,
+            )
         sums = []
-        product(1)
         product(2)
         product(3)
         product(0)
+        product(1)
         second_layer(0)
-        second_layer(1)
         second_layer(2)
         second_layer(3)
-        first = keep.tile([P, N // P, BLOCK], F32, name="first", tag="high")
+        second_layer(1)
+        after_pairs = keep.tile([P, 2, BLOCK], F32, name="after_pairs", tag="high")
+        after_codes = keep.tile([P, 2, BLOCK], F32, name="after_codes", tag="h1", align_bytes=64)
         for j, n, acc in sums:
-            result = first[:, n, :] if j == 0 else ring.tile([P, BLOCK], F32, name="result", bufs=8)
-            if j >= 2 and n == 1:
-                nc.vector.tensor_copy(result[:], acc[:])
+            if j == 0:
+                result = after_pairs[:, n, :]
+            elif j >= 2 and n == 1:
+                result = after_codes[:, j - 2, :]
             else:
-                nc.scalar.copy(result[:], acc[:])
-            queue = nc.scalar if (j, n) == (3, 0) else nc.sync
-            queue.dma_start(out=out[n * P : (n + 1) * P, j * BLOCK : (j + 1) * BLOCK], in_=result[:])
+                result = ring.tile([P, BLOCK], F32, name="result", bufs=5)[:]
+            if n == 1 and j:
+                nc.vector.tensor_copy(result, acc[:])
+            else:
+                nc.scalar.copy(result, acc[:])
+            queue = nc.scalar if j % 2 and n == 0 else nc.sync
+            queue.dma_start(out=out[n * P : (n + 1) * P, j * BLOCK : (j + 1) * BLOCK], in_=result)

@@ -16,6 +16,7 @@ U8 = mybir.dt.uint8
 FP8X4 = mybir.dt.float8_e4m3fn_x4
 FP4X4 = mybir.dt.float4_e2m1fn_x4
 SILU = mybir.ActivationFunctionType.Silu
+COPY = mybir.ActivationFunctionType.Copy
 MULT = mybir.AluOpType.mult
 
 P = 128
@@ -23,9 +24,8 @@ PACK = 4
 PASSES = 2
 BLOCK = 128
 BLOCKS = T // BLOCK
+HALF = T // 2
 WIDE = 704
-RUN = 4
-ORDER = (0, 1, 3, 2)
 EXPERT = PASSES * 2 * H
 
 
@@ -37,17 +37,17 @@ def tile_moe_pool_silu_kernel(
         lists = ctx.enter_context(tc.tile_pool(name="lists", bufs=1))
         keep = ctx.enter_context(tc.tile_pool(name="keep", bufs=1))
         ring = ctx.enter_context(tc.tile_pool(name="ring", bufs=4))
-        shared = ctx.enter_context(tc.tile_pool(name="shared", bufs=1))
-        psum = ctx.enter_context(tc.psum_pool(name="psum", bufs=4))
+        psum = ctx.enter_context(tc.psum_pool(name="psum", bufs=2))
 
         list_a = lists.tile([P, T // 16], U16, name="list_a")
         list_b = lists.tile([P, T // 16], U16, name="list_b")
 
         x_sc = keep.tile([P, WIDE], U8, name="x_sc", tag="after_scales", align_bytes=64)
-        x_w = keep.tile([P, PASSES, WIDE], I32, name="x_w", tag="after_words", align_bytes=64)
+        x_w = keep.tile([P, PASSES, WIDE], I32, name="x_w", align_bytes=64)
         first_w = keep.tile([P, EXPERT], U8, name="first_w", align_bytes=64)
         wa_sc = keep.tile([P, E1 * PASSES * H], U8, name="wa_sc", align_bytes=64)
         got_sc = [keep.tile([P, T], U8, name="got_sc%d" % g, align_bytes=64) for g in range(2)]
+        got_w = [keep.tile([P, PASSES, T], U32, name="got_w%d" % g, align_bytes=64) for g in range(2)]
         moved_sc = [[keep.tile([P, T], U8, name="moved_sc%d%d" % (g, s), align_bytes=64) for s in range(PASSES)] for g in range(2)]
         ident = keep.tile([P, P], F32, name="ident")
 
@@ -57,10 +57,10 @@ def tile_moe_pool_silu_kernel(
         nc.gpsimd.memset(x_w[:, :, T:], 0)
         make_identity(nc, ident[:])
 
-        def load_words(queue, tile, words):
-            queue.dma_start(
-                out=tile.bitcast(I32).rearrange("p (s c) -> p s c", s=PASSES),
-                in_=words.bitcast(I32).rearrange("s p c -> p s c"),
+        def load_words(tile, words, planes):
+            nc.sync.dma_start(
+                out=tile.bitcast(I32).rearrange("p (a c) -> p a c", a=planes),
+                in_=words.bitcast(I32).rearrange("a p c -> p a c"),
             )
 
         def load_scales(tile, scales, planes):
@@ -75,11 +75,10 @@ def tile_moe_pool_silu_kernel(
         nc.sync.dma_start(out=x_sc[:32, :T].bitcast(I32), in_=x_scales.bitcast(I32).rearrange("s b c -> (s b) c"))
         nc.sync.dma_start(list_b[:], offs2)
         nc.sync.dma_start(out=x_w[:, :, :T], in_=x_words.rearrange("s p t d -> p s (t d)").bitcast(I32))
-        load_words(nc.sync, first_w[:], wa_words[0])
+        load_words(first_w[:], wa_words[0], PASSES)
         load_scales(wa_sc[:], wa_scales.rearrange("e s b c -> (e s) b c"), E1 * PASSES)
 
-        def gather_scales(g, offsets):
-            nc.vector.tensor_copy(got_sc[g][:], x_sc[:].indirect(offsets[:]))
+        def move_scales(g):
             for s in range(PASSES):
                 for q in range(4):
                     at = 16 * s + 4 * q
@@ -88,122 +87,120 @@ def tile_moe_pool_silu_kernel(
                         in_=got_sc[g][at : at + 4, :].bitcast(I32),
                     )
 
-        def gather_words(got, offsets, first, count):
+        def gather_words(g, offsets, first, count):
             for s in range(PASSES):
                 window = x_w[:, s, :].bitcast(U32)
                 nc.vector.tensor_copy(
-                    got[:, s, first : first + count], window.indirect(offsets[:, first // 16 : (first + count) // 16])
+                    got_w[g][:, s, first : first + count], window.indirect(offsets[:, first // 16 : (first + count) // 16])
                 )
 
-        def first_layer(g, b, words, scales, e, staged):
+        nc.vector.tensor_copy(got_sc[0][:], x_sc[:].indirect(list_a[:]))
+        move_scales(0)
+        nc.vector.tensor_copy(got_sc[1][:], x_sc[:].indirect(list_b[:]))
+        gather_words(0, list_a, 0, BLOCK)
+        gather_words(0, list_a, BLOCK, T - BLOCK)
+        gather_words(1, list_b, 0, T)
+
+        sizes = [EXPERT, E2 * EXPERT, E2 * PASSES * H, N, 2 * N]
+        late = keep.tile([P, sum(sizes)], U8, name="late", tag="after_scales", align_bytes=64)
+        second_w, wb_w, wb_sc, w2_sc, w2_w = [late[:, sum(sizes[:i]) : sum(sizes[: i + 1])] for i in range(len(sizes))]
+        load_words(second_w, wa_words[1], PASSES)
+        load_words(wb_w, wb_words.rearrange("e s p c -> (e s) p c"), E2 * PASSES)
+        load_scales(wb_sc, wb_scales.rearrange("e s b c -> (e s) b c"), E2 * PASSES)
+        move_scales(1)
+        load_scales(w2_sc, w2_scales, 1)
+        nc.sync.dma_start(out=w2_w.bitcast(I32), in_=w2_words[0].bitcast(I32))
+
+        win_a = [keep.tile([P, WIDE], F32, name="win_a%d" % d) for d in range(PACK)]
+        win_c = [keep.tile([P, WIDE if d == 3 else T], F32, name="win_c%d" % d) for d in range(PACK)]
+        staged = [keep.tile([P, PACK, T], F32, name="staged%d" % g) for g in range(2)]
+        weights = [(first_w[:], wa_sc[:, : PASSES * H])] * 2 + [(second_w, wa_sc[:, PASSES * H :])] * 2
+        weights = weights + [(wb_w[:, e * EXPERT :], wb_sc[:, e * PASSES * H :]) for e in range(E2)]
+
+        def multiply(step):
+            g, b = divmod(step, BLOCKS)
             slots = slice(b * BLOCK, (b + 1) * BLOCK)
-            step = g * BLOCKS + b
-            if g == 0:
-                acc = psum.tile([P, H], F32, name="acc", tag="sums%d" % max(b, 1), bufs=1)
-            else:
-                acc = psum.tile([P, H], F32, name="acc", tag="odd" if b % 2 else "sums3", bufs=1)
-            planes = moved_sc[g]
+            words, scales = weights[step]
+            acc = psum.tile([P, H], F32, name="acc")
             for s in range(PASSES):
-                a = e * PASSES + s
                 nc.tensor.matmul_mx(
                     out=acc[:],
                     lhsT=got_w[g][:, s, slots].bitcast(FP8X4),
-                    lhsT_scale=planes[s][:, slots],
+                    lhsT_scale=moved_sc[g][s][:, slots],
                     rhs=words[:, s * 2 * H : (s + 1) * 2 * H].bitcast(FP4X4),
-                    rhs_scale=scales[:, a * H : (a + 1) * H],
+                    rhs_scale=scales[:, s * H : (s + 1) * H],
                     start=(s == 0),
                     stop=(s == PASSES - 1),
                 )
-            stepped = acc[:].rearrange("u (m d) -> u d m", d=PACK)
-            for d0, count in ((0, 1), (1, 1), (2, 2)) if step == 0 else ((0, PACK),):
-                parted = ring.tile([P, count, P], F32, name="parted")
-                if g == 0:
-                    nc.scalar.activation(parted[:], stepped[:, d0 : d0 + count, :], SILU)
-                else:
-                    nc.scalar.copy(parted[:], stepped[:, d0 : d0 + count, :])
-                if step == 0 and d0 > 0:
-                    turned = psum.tile([P, count, BLOCK], F32, name="turned", tag="sums%d" % (d0 + 1), bufs=1)
-                elif step in (1, 3):
-                    turned = psum.tile([P, count, BLOCK], F32, name="turned", tag="odd", bufs=1)
-                else:
-                    turned = psum.tile([P, count, BLOCK], F32, name="turned", tag="turned", bufs=2)
-                for d in range(count):
-                    nc.tensor.transpose(turned[:, d, :], parted[:, ORDER[d] if g else d, :], ident[:])
-                if g == 0:
-                    nc.scalar.copy(staged[:, d0 : d0 + count, :], turned[:])
-                else:
-                    nc.scalar.copy(staged[0], turned[:, : PACK - 1, :])
-                    nc.scalar.copy(staged[1], turned[:, PACK - 1 :, :])
+            return acc[:].rearrange("u (m d) -> u d m", d=PACK)
 
-        got_w = [keep.tile([P, PASSES, T], U32, name="got_w%d" % g, tag=tag, align_bytes=64) for g, tag in enumerate(("words_a", "words_b"))]
-        gather_scales(0, list_a)
-        gather_scales(1, list_b)
-        gather_words(got_w[0], list_a, 0, BLOCK)
-        gather_words(got_w[0], list_a, BLOCK, T - BLOCK)
-        gather_words(got_w[1], list_b, 0, T)
-        second_w = keep.tile([P, EXPERT], U8, name="second_w", tag="after_scales", align_bytes=64)
-        sizes = [EXPERT] * E2 + [E2 * PASSES * H, N]
-        late = keep.tile([P, sum(sizes)], U8, name="late", tag="after_words", align_bytes=64)
-        parts = [late[:, sum(sizes[:i]) : sum(sizes[: i + 1])] for i in range(len(sizes))]
-        wa_w = [first_w[:], second_w[:]]
-        wb_w = parts[:E2]
-        wb_sc, w2_sc = parts[E2:]
-        load_words(nc.sync, wa_w[1], wa_words[1])
-        load_scales(wb_sc, wb_scales.rearrange("e s b c -> (e s) b c"), E2 * PASSES)
-        for e in range(E2):
-            load_words(nc.sync, wb_w[e], wb_words[e])
-        load_scales(w2_sc, w2_scales, 1)
+        def turn(step, sums, planes):
+            parted = ring.tile([P, len(planes), P], F32, name="parted")
+            if step < BLOCKS:
+                nc.scalar.activation(parted[:], sums[:, planes.start : planes.stop, :], SILU)
+            else:
+                nc.scalar.copy(parted[:], sums[:, planes.start : planes.stop, :])
+            turned = psum.tile([P, len(planes), BLOCK], F32, name="turned")
+            for d in range(len(planes)):
+                nc.tensor.transpose(turned[:, d, :], parted[:, d, :], ident[:])
+            return turned
+
+        def stage(step, turned, planes):
+            g, b = divmod(step, BLOCKS)
+            nc.scalar.copy(staged[g][:, planes.start : planes.stop, b * BLOCK : (b + 1) * BLOCK], turned[:])
+
+        def scatter(engine, window, offsets, plane, first, count):
+            target = window[:].indirect(offsets[:, first // 16 : (first + count) // 16])
+            if engine == "vector":
+                nc.vector.tensor_copy(target, plane[:, first : first + count])
+            else:
+                nc.scalar.activation(target, plane[:, first : first + count], COPY)
+
+        first_sums = multiply(0)
+        halves = [turn(0, first_sums, planes) for planes in (range(0, 2), range(2, 4))]
+        sums_next = multiply(1)
+        stage(0, halves[0], range(0, 2))
+        stage(0, halves[1], range(2, 4))
+        waiting = None
+        for step in range(1, 2 * BLOCKS):
+            turned = turn(step, sums_next, range(PACK))
+            if step + 1 < 2 * BLOCKS:
+                sums_next = multiply(step + 1)
+            if waiting is not None:
+                stage(step - 1, waiting, range(PACK))
+            waiting = turned
+        stage(2 * BLOCKS - 1, waiting, range(PACK))
+
+        for first, count in ((0, BLOCK), (BLOCK, T - BLOCK)):
+            for d in range(PACK):
+                scatter("vector", win_a[d], list_a, staged[0][:, d, :], first, count)
+        for d in range(PACK - 1):
+            for first in (HALF, 0):
+                scatter("scalar", win_c[d], list_b, staged[1][:, d, :], first, HALF)
+        scatter("vector", win_c[3], list_b, staged[1][:, 3, :], 0, T)
 
         last = 2
-        win_a = [keep.tile([P, 2 * T if d == last else T], F32, name="win_a%d" % d) for d in range(PACK)]
-        for first, count in ((0, BLOCK), (BLOCK, BLOCK), (C1, C1)):
-            staged_a = ring.tile([P, PACK, count], F32, name="staged_a", bufs=3)
-            for at in range(0, count, BLOCK):
-                e = (first + at) // C1
-                first_layer(0, (first + at) // BLOCK, wa_w[e], wa_sc, e, staged_a[:, :, at : at + BLOCK])
-            for d in range(PACK):
-                nc.vector.tensor_copy(
-                    win_a[d][:].indirect(list_a[:, first // 16 : (first + count) // 16]), staged_a[:, d, :]
-                )
-
-        staged_c = [
-            shared.tile([P, PACK - 1, T], F32, name="staged_early", offset=4 * T, align_bytes=64),
-            shared.tile([P, 1, T], F32, name="staged_last", offset=0, align_bytes=64),
-        ]
-        win_c = [keep.tile([P, width], F32, name="win_c%d" % d) for d, width in enumerate((WIDE, WIDE, 2 * T, WIDE))]
-        nc.gpsimd.memset(win_c[last][:, T : T + T // 2], 1.0)
-        for b in range(BLOCKS):
-            e = b * BLOCK // C2
-            slots = slice(b * BLOCK, (b + 1) * BLOCK)
-            first_layer(1, b, wb_w[e], wb_sc, e, [pair[:, :, slots] for pair in staged_c])
-        for k, d in enumerate(ORDER):
-            nc.vector.tensor_copy(win_c[d][:].indirect(list_b[:]), staged_c[k // 3][:, k % 3, :])
-
-        planes_h = keep.tile([P, 2, T], BF16, name="planes_h")
-        high = keep.tile([P, 2, T // 2], BF16, name="high", tag="high")
-        for d in range(2):
-            nc.gpsimd.tensor_tensor(planes_h[:, d, :], win_a[d][:], win_c[d][:, :T], MULT)
-        nc.gpsimd.tensor_tensor(win_a[last][:, T : T + T // 2], win_a[3][:, : T // 2], win_c[3][:, : T // 2], MULT)
-        nc.gpsimd.tensor_tensor(high[:, 1, :], win_a[3][:, T // 2 :], win_c[3][:, T // 2 : T], MULT)
         h = [keep.tile([P, BLOCK, PACK], BF16, name="h%d" % j, tag="h%d" % j, align_bytes=64) for j in range(BLOCKS)]
-        for j in range(BLOCKS):
-            nc.scalar.copy(h[j][:, :, 0:2], planes_h[:, :, j * BLOCK : (j + 1) * BLOCK].rearrange("p d t -> p t d"))
-        left = win_a[last][:].rearrange("p (d t) -> p t d", d=2)
-        right = win_c[last][:].rearrange("p (d t) -> p t d", d=2)
-
-        w2_w = shared.tile([P, 2 * N], U8, name="w2_w", offset=4 * T, align_bytes=64)
-        nc.sync.dma_start(out=w2_w[:].bitcast(I32), in_=w2_words[0].bitcast(I32))
+        low = keep.tile([P, PACK, HALF], BF16, name="low")
+        high = keep.tile([P, 2, HALF], BF16, name="high", tag="high")
+        for d in range(2):
+            nc.gpsimd.tensor_tensor(low[:, d, :], win_a[d][:, :HALF], win_c[d][:, :HALF], MULT)
+            for j in (2, 3):
+                tokens = slice(j * BLOCK, (j + 1) * BLOCK)
+                nc.gpsimd.tensor_tensor(h[j][:, :, d], win_a[d][:, tokens], win_c[d][:, tokens], MULT)
+        nc.vector.tensor_tensor(high[:, 1, :], win_a[3][:, HALF:T], win_c[3][:, HALF:T], MULT)
+        nc.vector.tensor_tensor(low[:, 3, :], win_a[3][:, :HALF], win_c[3][:, :HALF], MULT)
 
         def product(j):
             tokens = slice(j * BLOCK, (j + 1) * BLOCK)
             if j < BLOCKS // 2:
-                nc.vector.tensor_tensor(h[j][:, :, 2:4], left[:, tokens, :], right[:, tokens, :], MULT)
+                nc.vector.tensor_tensor(low[:, last, tokens], win_a[last][:, tokens], win_c[last][:, tokens], MULT)
                 return
-            part = slice(j * BLOCK - T // 2, (j + 1) * BLOCK - T // 2)
+            part = slice(j * BLOCK - HALF, (j + 1) * BLOCK - HALF)
             nc.vector.tensor_tensor(high[:, 0, part], win_a[last][:, tokens], win_c[last][:, tokens], MULT)
             nc.scalar.copy(h[j][:, :, 2:4], high[:, :, part].rearrange("p d t -> p t d"))
 
-        banks = [("sums%d" % b, 1) for b in range(BLOCKS)] + [("turned", 2)] * 2 + [("spare", 1), ("odd", 1)]
+        banks = [("acc", 2), ("turned", 2)] * 2 + [("spare%d" % b, 1) for b in range(4)]
 
         def second_layer(j):
             h_w = ring.tile([P, BLOCK], U32, name="h_w", align_bytes=64)
@@ -223,26 +220,13 @@ def tile_moe_pool_silu_kernel(
                 )
                 sums.append((j, n, acc))
 
-        unread = psum.tile([P, T], F32, name="unread", tag="odd", bufs=1)
-        for k in range(4):
-            nc.tensor.matmul_mx(
-                out=unread[:],
-                lhsT=w2_w[:, : 2 * P].bitcast(FP4X4),
-                lhsT_scale=w2_sc[:, :P],
-                rhs=got_w[1][:, 0, :].bitcast(FP8X4),
-                rhs_scale=moved_sc[1][0][:],
-                start=True,
-                stop=True,
-            )
         sums = []
-        product(2)
-        product(3)
-        product(0)
-        product(1)
-        second_layer(0)
-        second_layer(2)
-        second_layer(3)
-        second_layer(1)
+        for j in (2, 3, 0, 1):
+            product(j)
+        for j in range(BLOCKS // 2):
+            nc.vector.tensor_copy(h[j][:], low[:, :, j * BLOCK : (j + 1) * BLOCK].rearrange("p d t -> p t d"))
+        for j in (2, 0, 3, 1):
+            second_layer(j)
         after_pairs = keep.tile([P, 2, BLOCK], F32, name="after_pairs", tag="high")
         after_codes = keep.tile([P, 2, BLOCK], F32, name="after_codes", tag="h1", align_bytes=64)
         for j, n, acc in sums:

@@ -111,7 +111,7 @@ def tile_moe_pool_silu_kernel(
         load_scales(w2_sc, w2_scales, 1)
         nc.sync.dma_start(out=w2_w.bitcast(I32), in_=w2_words[0].bitcast(I32))
 
-        win_a = [keep.tile([P, WIDE], F32, name="win_a%d" % d) for d in range(PACK)]
+        win_a = [keep.tile([P, T], F32, name="win_a%d" % d) for d in range(PACK)]
         win_c = [keep.tile([P, WIDE if d == 3 else T], F32, name="win_c%d" % d) for d in range(PACK)]
         staged = [keep.tile([P, PACK, T], F32, name="staged%d" % g) for g in range(2)]
         weights = [(first_w[:], wa_sc[:, : PASSES * H])] * 2 + [(second_w, wa_sc[:, PASSES * H :])] * 2
@@ -121,7 +121,7 @@ def tile_moe_pool_silu_kernel(
             g, b = divmod(step, BLOCKS)
             slots = slice(b * BLOCK, (b + 1) * BLOCK)
             words, scales = weights[step]
-            acc = psum.tile([P, H], F32, name="acc")
+            acc = psum.tile([P, H], F32, name="acc", bufs=3)
             for s in range(PASSES):
                 nc.tensor.matmul_mx(
                     out=acc[:],
@@ -140,7 +140,7 @@ def tile_moe_pool_silu_kernel(
                 nc.scalar.activation(parted[:], sums[:, planes.start : planes.stop, :], SILU)
             else:
                 nc.scalar.copy(parted[:], sums[:, planes.start : planes.stop, :])
-            turned = psum.tile([P, len(planes), BLOCK], F32, name="turned")
+            turned = psum.tile([P, len(planes), BLOCK], F32, name="turned", bufs=3)
             for d in range(len(planes)):
                 nc.tensor.transpose(turned[:, d, :], parted[:, d, :], ident[:])
             return turned
@@ -164,6 +164,11 @@ def tile_moe_pool_silu_kernel(
         waiting = None
         for step in range(1, 2 * BLOCKS):
             turned = turn(step, sums_next, range(PACK))
+            if step in (1, 3):
+                first = step // 2 * BLOCK
+                scatter("scalar", win_a[3], list_a, staged[0][:, 3, :], first, BLOCK)
+            if step == 2 * BLOCKS - 1:
+                scatter("scalar", win_c[1], list_b, staged[1][:, 1, :], 0, BLOCK)
             if step + 1 < 2 * BLOCKS:
                 sums_next = multiply(step + 1)
             if waiting is not None:
@@ -171,13 +176,15 @@ def tile_moe_pool_silu_kernel(
             waiting = turned
         stage(2 * BLOCKS - 1, waiting, range(PACK))
 
-        for first, count in ((0, BLOCK), (BLOCK, T - BLOCK)):
-            for d in range(PACK):
+        for first, count, planes in ((0, BLOCK, 3), (BLOCK, BLOCK, 3), (HALF, HALF, 4)):
+            for d in range(planes):
                 scatter("vector", win_a[d], list_a, staged[0][:, d, :], first, count)
-        for d in range(PACK - 1):
-            for first in (HALF, 0):
-                scatter("scalar", win_c[d], list_b, staged[1][:, d, :], first, HALF)
+        for first in (HALF, 0):
+            scatter("scalar", win_c[0], list_b, staged[1][:, 0, :], first, HALF)
+        scatter("vector", win_c[1], list_b, staged[1][:, 1, :], BLOCK, T - BLOCK)
         scatter("vector", win_c[3], list_b, staged[1][:, 3, :], 0, T)
+        for first in (HALF, 0):
+            scatter("scalar", win_c[2], list_b, staged[1][:, 2, :], first, HALF)
 
         last = 2
         h = [keep.tile([P, BLOCK, PACK], BF16, name="h%d" % j, tag="h%d" % j, align_bytes=64) for j in range(BLOCKS)]
@@ -200,7 +207,7 @@ def tile_moe_pool_silu_kernel(
             nc.vector.tensor_tensor(high[:, 0, part], win_a[last][:, tokens], win_c[last][:, tokens], MULT)
             nc.scalar.copy(h[j][:, :, 2:4], high[:, :, part].rearrange("p d t -> p t d"))
 
-        banks = [("acc", 2), ("turned", 2)] * 2 + [("spare%d" % b, 1) for b in range(4)]
+        banks = [("acc", 3), ("turned", 3)] * 3 + [("spare%d" % b, 1) for b in range(2)]
 
         def second_layer(j):
             h_w = ring.tile([P, BLOCK], U32, name="h_w", align_bytes=64)

@@ -26,6 +26,7 @@ BLOCK = 128
 BLOCKS = T // BLOCK
 HALF = T // 2
 WIDE = 704
+SPARE = 64
 EXPERT = PASSES * 2 * H
 
 
@@ -36,6 +37,7 @@ def tile_moe_pool_silu_kernel(
     with ExitStack() as ctx:
         lists = ctx.enter_context(tc.tile_pool(name="lists", bufs=1))
         keep = ctx.enter_context(tc.tile_pool(name="keep", bufs=1))
+        shared = ctx.enter_context(tc.tile_pool(name="shared", bufs=1))
         ring = ctx.enter_context(tc.tile_pool(name="ring", bufs=4))
         psum = ctx.enter_context(tc.psum_pool(name="psum", bufs=2))
 
@@ -44,7 +46,7 @@ def tile_moe_pool_silu_kernel(
 
         x_sc = keep.tile([P, WIDE], U8, name="x_sc", tag="after_scales", align_bytes=64)
         x_w = keep.tile([P, PASSES, WIDE], I32, name="x_w", align_bytes=64)
-        first_w = keep.tile([P, EXPERT], U8, name="first_w", align_bytes=64)
+        wa_w = [keep.tile([P, EXPERT], U8, name="wa_w%d" % e, align_bytes=64) for e in range(E1)]
         wa_sc = keep.tile([P, E1 * PASSES * H], U8, name="wa_sc", align_bytes=64)
         got_sc = [keep.tile([P, T], U8, name="got_sc%d" % g, align_bytes=64) for g in range(2)]
         got_w = [keep.tile([P, PASSES, T], U32, name="got_w%d" % g, align_bytes=64) for g in range(2)]
@@ -55,7 +57,11 @@ def tile_moe_pool_silu_kernel(
         nc.gpsimd.memset(x_sc[64:, :T].bitcast(I32), 0)
         nc.gpsimd.memset(x_sc[:, T:].bitcast(I32), 0)
         nc.gpsimd.memset(x_w[:, :, T:], 0)
+        nc.vector.memset(wa_sc[:].bitcast(I32), 0)
         make_identity(nc, ident[:])
+        unread = keep.tile([P, 2], F32, name="unread")
+        nc.vector.memset(unread[:, :1], 0.0)
+        nc.scalar.activation(unread[:, 1:], unread[:, :1], SILU)
 
         def load_words(tile, words, planes):
             nc.sync.dma_start(
@@ -73,10 +79,25 @@ def tile_moe_pool_silu_kernel(
 
         nc.sync.dma_start(list_a[:], offs)
         nc.sync.dma_start(out=x_sc[:32, :T].bitcast(I32), in_=x_scales.bitcast(I32).rearrange("s b c -> (s b) c"))
-        nc.sync.dma_start(list_b[:], offs2)
-        nc.sync.dma_start(out=x_w[:, :, :T], in_=x_words.rearrange("s p t d -> p s (t d)").bitcast(I32))
-        load_words(first_w[:], wa_words[0], PASSES)
         load_scales(wa_sc[:], wa_scales.rearrange("e s b c -> (e s) b c"), E1 * PASSES)
+        nc.sync.dma_start(list_b[:], offs2)
+        load_words(wa_w[0][:], wa_words[0], PASSES)
+        nc.sync.dma_start(out=x_w[:, :, :T], in_=x_words.rearrange("s p t d -> p s (t d)").bitcast(I32))
+        load_words(wa_w[1][:], wa_words[1], PASSES)
+        by_plane_w = [keep.tile([P, EXPERT], U8, name="by_plane_w%d" % e, align_bytes=64) for e in range(E1)]
+        by_plane_sc = [keep.tile([P, PASSES * H], U8, name="by_plane_sc%d" % e, align_bytes=64) for e in range(E1)]
+
+        def part_words(copy, e):
+            copy(
+                by_plane_w[e][:].bitcast(U16).rearrange("p (s d m) -> p s d m", s=PASSES, d=PACK),
+                wa_w[e][:].bitcast(U16).rearrange("p (s m d) -> p s d m", s=PASSES, d=PACK),
+            )
+
+        def part_scales(e):
+            nc.vector.tensor_copy(
+                by_plane_sc[e][:].rearrange("p (s d m) -> p s d m", s=PASSES, d=PACK),
+                wa_sc[:, e * PASSES * H : (e + 1) * PASSES * H].rearrange("p (s m d) -> p s d m", s=PASSES, d=PACK),
+            )
 
         def move_scales(g):
             for s in range(PASSES):
@@ -97,57 +118,81 @@ def tile_moe_pool_silu_kernel(
         nc.vector.tensor_copy(got_sc[0][:], x_sc[:].indirect(list_a[:]))
         move_scales(0)
         nc.vector.tensor_copy(got_sc[1][:], x_sc[:].indirect(list_b[:]))
-        gather_words(0, list_a, 0, BLOCK)
-        gather_words(0, list_a, BLOCK, T - BLOCK)
+        for e in range(E1):
+            part_scales(e)
+        part_words(nc.scalar.copy, 0)
+        part_words(nc.scalar.copy, 1)
+        for e in range(E1):
+            gather_words(0, list_a, e * C1, C1)
         gather_words(1, list_b, 0, T)
 
-        sizes = [EXPERT, E2 * EXPERT, E2 * PASSES * H, N, 2 * N]
+        sizes = [E2 * EXPERT, E2 * PASSES * H]
         late = keep.tile([P, sum(sizes)], U8, name="late", tag="after_scales", align_bytes=64)
-        second_w, wb_w, wb_sc, w2_sc, w2_w = [late[:, sum(sizes[:i]) : sum(sizes[: i + 1])] for i in range(len(sizes))]
-        load_words(second_w, wa_words[1], PASSES)
-        load_words(wb_w, wb_words.rearrange("e s p c -> (e s) p c"), E2 * PASSES)
+        wb_w, wb_sc = [late[:, sum(sizes[:i]) : sum(sizes[: i + 1])] for i in range(len(sizes))]
         load_scales(wb_sc, wb_scales.rearrange("e s b c -> (e s) b c"), E2 * PASSES)
+        load_words(wb_w, wb_words.rearrange("e s p c -> (e s) p c"), E2 * PASSES)
         move_scales(1)
-        load_scales(w2_sc, w2_scales, 1)
-        nc.sync.dma_start(out=w2_w.bitcast(I32), in_=w2_words[0].bitcast(I32))
 
         win_a = [keep.tile([P, T], F32, name="win_a%d" % d) for d in range(PACK)]
-        win_c = [keep.tile([P, WIDE if d == 3 else T], F32, name="win_c%d" % d) for d in range(PACK)]
+        win_c = {d: keep.tile([P, T], F32, name="win_c%d" % d) for d in (0, 1, 3)}
         staged = [keep.tile([P, PACK, T], F32, name="staged%d" % g) for g in range(2)]
-        weights = [(first_w[:], wa_sc[:, : PASSES * H])] * 2 + [(second_w, wa_sc[:, PASSES * H :])] * 2
-        weights = weights + [(wb_w[:, e * EXPERT :], wb_sc[:, e * PASSES * H :]) for e in range(E2)]
 
-        def multiply(step):
-            g, b = divmod(step, BLOCKS)
+        def first_pool(e, acc, d, s):
+            slots = slice(e * C1, (e + 1) * C1)
+            column = s * H + d * P
+            nc.tensor.matmul_mx(
+                out=acc,
+                lhsT=by_plane_w[e][:, 2 * column : 2 * (column + P)].bitcast(FP4X4),
+                lhsT_scale=by_plane_sc[e][:, column : column + P],
+                rhs=got_w[0][:, s, slots].bitcast(FP8X4),
+                rhs_scale=moved_sc[0][s][:, slots],
+                start=(s == 0),
+                stop=(s == PASSES - 1),
+            )
+
+        def multiply(b):
             slots = slice(b * BLOCK, (b + 1) * BLOCK)
-            words, scales = weights[step]
-            acc = psum.tile([P, H], F32, name="acc", bufs=3)
+            acc = psum.tile([P, H], F32, name="acc", tag="plane", bufs=4)
             for s in range(PASSES):
+                a = b * PASSES + s
                 nc.tensor.matmul_mx(
                     out=acc[:],
-                    lhsT=got_w[g][:, s, slots].bitcast(FP8X4),
-                    lhsT_scale=moved_sc[g][s][:, slots],
-                    rhs=words[:, s * 2 * H : (s + 1) * 2 * H].bitcast(FP4X4),
-                    rhs_scale=scales[:, s * H : (s + 1) * H],
+                    lhsT=got_w[1][:, s, slots].bitcast(FP8X4),
+                    lhsT_scale=moved_sc[1][s][:, slots],
+                    rhs=wb_w[:, a * 2 * H : (a + 1) * 2 * H].bitcast(FP4X4),
+                    rhs_scale=wb_sc[:, a * H : (a + 1) * H],
                     start=(s == 0),
                     stop=(s == PASSES - 1),
                 )
             return acc[:].rearrange("u (m d) -> u d m", d=PACK)
 
-        def turn(step, sums, planes):
-            parted = ring.tile([P, len(planes), P], F32, name="parted")
-            if step < BLOCKS:
-                nc.scalar.activation(parted[:], sums[:, planes.start : planes.stop, :], SILU)
-            else:
-                nc.scalar.copy(parted[:], sums[:, planes.start : planes.stop, :])
-            turned = psum.tile([P, len(planes), BLOCK], F32, name="turned", bufs=3)
-            for d in range(len(planes)):
+        def turn(sums):
+            parted = ring.tile([P, PACK, P], F32, name="parted")
+            nc.scalar.copy(parted[:], sums)
+            turned = psum.tile([P, PACK, BLOCK], F32, name="turned", bufs=4)
+            for d in range(PACK):
                 nc.tensor.transpose(turned[:, d, :], parted[:, d, :], ident[:])
             return turned
 
-        def stage(step, turned, planes):
-            g, b = divmod(step, BLOCKS)
-            nc.scalar.copy(staged[g][:, planes.start : planes.stop, b * BLOCK : (b + 1) * BLOCK], turned[:])
+        def stage(b, turned):
+            nc.scalar.copy(staged[1][:, :, b * BLOCK : (b + 1) * BLOCK], turned[:])
+
+        def second_pool(e):
+            slots = slice(e * C2, (e + 1) * C2)
+            acc = psum.tile([P, PACK, C2], F32, name="rows", tag="plane", bufs=4)
+            for j in range(PACK):
+                for s in range(PASSES):
+                    column = (e * PASSES + s) * H + j * P
+                    nc.tensor.matmul_mx(
+                        out=acc[:, j, :],
+                        lhsT=wb_w[:, 2 * column : 2 * (column + P)].bitcast(FP4X4),
+                        lhsT_scale=wb_sc[:, column : column + P],
+                        rhs=got_w[1][:, s, slots].bitcast(FP8X4),
+                        rhs_scale=moved_sc[1][s][:, slots],
+                        start=(s == 0),
+                        stop=(s == PASSES - 1),
+                    )
+            nc.scalar.copy(rows_c[:, :, slots], acc[:])
 
         def scatter(engine, window, offsets, plane, first, count):
             target = window[:].indirect(offsets[:, first // 16 : (first + count) // 16])
@@ -156,58 +201,67 @@ def tile_moe_pool_silu_kernel(
             else:
                 nc.scalar.activation(target, plane[:, first : first + count], COPY)
 
-        first_sums = multiply(0)
-        halves = [turn(0, first_sums, planes) for planes in (range(0, 2), range(2, 4))]
-        sums_next = multiply(1)
-        stage(0, halves[0], range(0, 2))
-        stage(0, halves[1], range(2, 4))
-        waiting = None
-        for step in range(1, 2 * BLOCKS):
-            turned = turn(step, sums_next, range(PACK))
-            if step in (1, 3):
-                first = step // 2 * BLOCK
-                scatter("scalar", win_a[3], list_a, staged[0][:, 3, :], first, BLOCK)
-            if step == 2 * BLOCKS - 1:
-                scatter("scalar", win_c[1], list_b, staged[1][:, 1, :], 0, BLOCK)
-            if step + 1 < 2 * BLOCKS:
-                sums_next = multiply(step + 1)
-            if waiting is not None:
-                stage(step - 1, waiting, range(PACK))
-            waiting = turned
-        stage(2 * BLOCKS - 1, waiting, range(PACK))
+        planes = [psum.tile([P, C1], F32, name="plane", bufs=4) for d in range(PACK)]
+        for s in range(PASSES):
+            for d in range(PACK):
+                first_pool(0, planes[d][:], d, s)
+        for d in range(PACK):
+            nc.scalar.activation(staged[0][:, d, :C1], planes[d][:], SILU)
+        scatter("scalar", win_a[3], list_a, staged[0][:, 3, :], 0, C1)
+        for d0 in (0, 2):
+            pair = psum.tile([P, 2, C1], F32, name="pair", tag="plane", bufs=4)
+            for d in range(2):
+                for s in range(PASSES):
+                    first_pool(1, pair[:, d, :], d0 + d, s)
+            nc.scalar.activation(staged[0][:, d0 : d0 + 2, C1:], pair[:], SILU)
+        scatter("scalar", win_a[3], list_a, staged[0][:, 3, :], C1, C1)
+        scatter("scalar", win_a[2], list_a, staged[0][:, 2, :], 0, BLOCK)
+        for d in range(2):
+            scatter("vector", win_a[d], list_a, staged[0][:, d, :], 0, C1)
+        scatter("vector", win_a[2], list_a, staged[0][:, 2, :], BLOCK, BLOCK)
+        for d in range(PACK - 1):
+            scatter("vector", win_a[d], list_a, staged[0][:, d, :], C1, C1)
 
-        for first, count, planes in ((0, BLOCK, 3), (BLOCK, BLOCK, 3), (HALF, HALF, 4)):
-            for d in range(planes):
-                scatter("vector", win_a[d], list_a, staged[0][:, d, :], first, count)
+        rows_c = shared.tile([P, PACK, HALF], F32, name="rows_c", offset=0, align_bytes=64)
+        turned = []
+        for e in range(E2 // 2):
+            second_pool(e)
+            turned.append(turn(multiply(e + 2)))
+        for d in (1, 0, 3, 2):
+            for j in range(PACK):
+                nc.sync.dma_start(out=staged[1][32 * j : 32 * (j + 1), d, :HALF], in_=rows_c[d:P:PACK, j, :])
+        for b in (2, 3):
+            stage(b, turned[b - 2])
+        win_c[2] = shared.tile([P, T], F32, name="win_c2", offset=0, align_bytes=64)
+        w2 = shared.tile([P, 3 * N], U8, name="w2", offset=4 * T, align_bytes=64)
+        w2_w, w2_sc = w2[:, : 2 * N], w2[:, 2 * N :]
+        load_scales(w2_sc, w2_scales, 1)
+        nc.sync.dma_start(out=w2_w.bitcast(I32), in_=w2_words[0].bitcast(I32))
+
         for first in (HALF, 0):
-            scatter("scalar", win_c[0], list_b, staged[1][:, 0, :], first, HALF)
-        scatter("vector", win_c[1], list_b, staged[1][:, 1, :], BLOCK, T - BLOCK)
-        scatter("vector", win_c[3], list_b, staged[1][:, 3, :], 0, T)
+            scatter("scalar", win_c[1], list_b, staged[1][:, 1, :], first, HALF)
+        for first in (HALF, 0):
+            scatter("vector", win_c[0], list_b, staged[1][:, 0, :], first, HALF)
+        scatter("scalar", win_c[3], list_b, staged[1][:, 3, :], T - SPARE, SPARE)
+        scatter("vector", win_c[3], list_b, staged[1][:, 3, :], 0, HALF)
+        scatter("vector", win_c[3], list_b, staged[1][:, 3, :], HALF, HALF - SPARE)
         for first in (HALF, 0):
             scatter("scalar", win_c[2], list_b, staged[1][:, 2, :], first, HALF)
 
         last = 2
         h = [keep.tile([P, BLOCK, PACK], BF16, name="h%d" % j, tag="h%d" % j, align_bytes=64) for j in range(BLOCKS)]
-        low = keep.tile([P, PACK, HALF], BF16, name="low")
-        high = keep.tile([P, 2, HALF], BF16, name="high", tag="high")
+        planes_h = keep.tile([P, PACK, T], BF16, name="planes_h", tag="high")
         for d in range(2):
-            nc.gpsimd.tensor_tensor(low[:, d, :], win_a[d][:, :HALF], win_c[d][:, :HALF], MULT)
-            for j in (2, 3):
-                tokens = slice(j * BLOCK, (j + 1) * BLOCK)
-                nc.gpsimd.tensor_tensor(h[j][:, :, d], win_a[d][:, tokens], win_c[d][:, tokens], MULT)
-        nc.vector.tensor_tensor(high[:, 1, :], win_a[3][:, HALF:T], win_c[3][:, HALF:T], MULT)
-        nc.vector.tensor_tensor(low[:, 3, :], win_a[3][:, :HALF], win_c[3][:, :HALF], MULT)
+            nc.gpsimd.tensor_tensor(planes_h[:, d, :], win_a[d][:, :T], win_c[d][:, :T], MULT)
+        nc.vector.tensor_tensor(planes_h[:, 3, :], win_a[3][:, :T], win_c[3][:, :T], MULT)
 
         def product(j):
             tokens = slice(j * BLOCK, (j + 1) * BLOCK)
-            if j < BLOCKS // 2:
-                nc.vector.tensor_tensor(low[:, last, tokens], win_a[last][:, tokens], win_c[last][:, tokens], MULT)
-                return
-            part = slice(j * BLOCK - HALF, (j + 1) * BLOCK - HALF)
-            nc.vector.tensor_tensor(high[:, 0, part], win_a[last][:, tokens], win_c[last][:, tokens], MULT)
-            nc.scalar.copy(h[j][:, :, 2:4], high[:, :, part].rearrange("p d t -> p t d"))
+            nc.vector.tensor_tensor(planes_h[:, last, tokens], win_a[last][:, tokens], win_c[last][:, tokens], MULT)
+            if j >= BLOCKS // 2:
+                nc.scalar.copy(h[j][:], planes_h[:, :, tokens].rearrange("p d t -> p t d"))
 
-        banks = [("acc", 3), ("turned", 3)] * 3 + [("spare%d" % b, 1) for b in range(2)]
+        banks = [("plane", 4), ("turned", 4)] * 4
 
         def second_layer(j):
             h_w = ring.tile([P, BLOCK], U32, name="h_w", align_bytes=64)
@@ -231,7 +285,7 @@ def tile_moe_pool_silu_kernel(
         for j in (2, 3, 0, 1):
             product(j)
         for j in range(BLOCKS // 2):
-            nc.vector.tensor_copy(h[j][:], low[:, :, j * BLOCK : (j + 1) * BLOCK].rearrange("p d t -> p t d"))
+            nc.vector.tensor_copy(h[j][:], planes_h[:, :, j * BLOCK : (j + 1) * BLOCK].rearrange("p d t -> p t d"))
         for j in (2, 0, 3, 1):
             second_layer(j)
         after_pairs = keep.tile([P, 2, BLOCK], F32, name="after_pairs", tag="high")

@@ -26,7 +26,6 @@ BLOCK = 128
 BLOCKS = T // BLOCK
 HALF = T // 2
 WIDE = 704
-SPARE = 64
 EXPERT = PASSES * 2 * H
 
 
@@ -134,7 +133,7 @@ def tile_moe_pool_silu_kernel(
         move_scales(1)
 
         win_a = [keep.tile([P, T], F32, name="win_a%d" % d) for d in range(PACK)]
-        win_c = {d: keep.tile([P, T], F32, name="win_c%d" % d) for d in (0, 1, 3)}
+        win_c = {d: keep.tile([P, WIDE if d == 3 else T], F32, name="win_c%d" % d) for d in (0, 1, 3)}
         staged = [keep.tile([P, PACK, T], F32, name="staged%d" % g) for g in range(2)]
 
         def first_pool(e, acc, d, s):
@@ -242,9 +241,7 @@ def tile_moe_pool_silu_kernel(
             scatter("scalar", win_c[1], list_b, staged[1][:, 1, :], first, HALF)
         for first in (HALF, 0):
             scatter("vector", win_c[0], list_b, staged[1][:, 0, :], first, HALF)
-        scatter("scalar", win_c[3], list_b, staged[1][:, 3, :], T - SPARE, SPARE)
-        scatter("vector", win_c[3], list_b, staged[1][:, 3, :], 0, HALF)
-        scatter("vector", win_c[3], list_b, staged[1][:, 3, :], HALF, HALF - SPARE)
+        scatter("vector", win_c[3], list_b, staged[1][:, 3, :], 0, T)
         for first in (HALF, 0):
             scatter("scalar", win_c[2], list_b, staged[1][:, 2, :], first, HALF)
 

@@ -1,7 +1,6 @@
 from contextlib import ExitStack
 
 import concourse.mybir as mybir
-from concourse.masks import make_identity
 
 K, T, H, N = 1024, 512, 512, 256
 E1, C1, E2, C2 = 2, 256, 4, 128
@@ -22,11 +21,15 @@ MULT = mybir.AluOpType.mult
 P = 128
 PACK = 4
 PASSES = 2
+ROWS = 16
 BLOCK = 128
 BLOCKS = T // BLOCK
 HALF = T // 2
 WIDE = 704
 EXPERT = PASSES * 2 * H
+PARTED = 4
+FILL = 128
+SECOND = 2 * PASSES * T + 3 * EXPERT
 
 
 def tile_moe_pool_silu_kernel(
@@ -37,27 +40,29 @@ def tile_moe_pool_silu_kernel(
         lists = ctx.enter_context(tc.tile_pool(name="lists", bufs=1))
         keep = ctx.enter_context(tc.tile_pool(name="keep", bufs=1))
         shared = ctx.enter_context(tc.tile_pool(name="shared", bufs=1))
+        head = ctx.enter_context(tc.tile_pool(name="head", bufs=1))
         ring = ctx.enter_context(tc.tile_pool(name="ring", bufs=4))
-        psum = ctx.enter_context(tc.psum_pool(name="psum", bufs=2))
+        psum = ctx.enter_context(tc.psum_pool(name="psum", bufs=1))
+
+        def bank(b, shape):
+            return psum.tile([P] + shape, F32, name="bank%d" % b, tag="bank%d" % b)
 
         list_a = lists.tile([P, T // 16], U16, name="list_a")
         list_b = lists.tile([P, T // 16], U16, name="list_b")
 
-        x_sc = keep.tile([P, WIDE], U8, name="x_sc", tag="after_scales", align_bytes=64)
-        x_w = keep.tile([P, PASSES, WIDE], I32, name="x_w", align_bytes=64)
-        wa_w = [keep.tile([P, EXPERT], U8, name="wa_w%d" % e, align_bytes=64) for e in range(E1)]
-        wa_sc = keep.tile([P, E1 * PASSES * H], U8, name="wa_sc", align_bytes=64)
+        x_sc = keep.tile([P, WIDE], U8, name="x_sc", align_bytes=64)
+        x_w = keep.tile([P, PASSES, T], I32, name="x_w", align_bytes=64)
+        rows = head.tile([P, H], U8, name="rows", offset=PASSES * T - H // 2, align_bytes=64)
+        rows_by_plane = head.tile([P, H], U8, name="rows_by_plane", offset=SECOND - H // 2, align_bytes=64)
+        raw_w = [keep.tile([P, EXPERT], U8, name="raw_w%d" % e, align_bytes=64)[:] for e in range(PARTED - 1)]
+        by_plane_w = [keep.tile([P, EXPERT], U8, name="by_plane_w%d" % e, align_bytes=64) for e in range(PARTED)]
+        by_plane_sc = keep.tile([P, PARTED * PASSES * H], U8, name="by_plane_sc", align_bytes=64)
         got_sc = [keep.tile([P, T], U8, name="got_sc%d" % g, align_bytes=64) for g in range(2)]
         got_w = [keep.tile([P, PASSES, T], U32, name="got_w%d" % g, align_bytes=64) for g in range(2)]
-        moved_sc = [[keep.tile([P, T], U8, name="moved_sc%d%d" % (g, s), align_bytes=64) for s in range(PASSES)] for g in range(2)]
-        ident = keep.tile([P, P], F32, name="ident")
 
         nc.gpsimd.memset(x_sc[32:64, :T].bitcast(I32), 0)
         nc.gpsimd.memset(x_sc[64:, :T].bitcast(I32), 0)
         nc.gpsimd.memset(x_sc[:, T:].bitcast(I32), 0)
-        nc.gpsimd.memset(x_w[:, :, T:], 0)
-        nc.vector.memset(wa_sc[:].bitcast(I32), 0)
-        make_identity(nc, ident[:])
         unread = keep.tile([P, 2], F32, name="unread")
         nc.vector.memset(unread[:, :1], 0.0)
         nc.scalar.activation(unread[:, 1:], unread[:, :1], SILU)
@@ -76,122 +81,80 @@ def tile_moe_pool_silu_kernel(
                     in_=rows[:, 4 * q : 4 * q + 4, :].rearrange("a r c -> r a c"),
                 )
 
+        def move_scales(plane, rows, planes):
+            for q in range(4):
+                nc.sync.dma_start(
+                    out=plane[32 * q : 32 * q + 4, :].bitcast(I32).rearrange("r (a c) -> r a c", a=planes),
+                    in_=rows[4 * planes * q : 4 * planes * (q + 1), :].bitcast(I32),
+                )
+
         nc.sync.dma_start(list_a[:], offs)
-        nc.sync.dma_start(out=x_sc[:32, :T].bitcast(I32), in_=x_scales.bitcast(I32).rearrange("s b c -> (s b) c"))
-        load_scales(wa_sc[:], wa_scales.rearrange("e s b c -> (e s) b c"), E1 * PASSES)
+        nc.sync.dma_start(out=x_sc[: ROWS * PASSES, :T].bitcast(I32), in_=x_scales.bitcast(I32).rearrange("s b c -> b s c"))
+        for pool, scales in enumerate((wa_scales, wb_scales[:2])):
+            nc.sync.dma_start(out=rows[pool:P:2, :].bitcast(I32), in_=scales.bitcast(I32).rearrange("e s b c -> b (e s) c"))
+        load_words(raw_w[0], wa_words[0], PASSES)
+        nc.sync.dma_start(out=x_w[:], in_=x_words.rearrange("s p t d -> p s (t d)").bitcast(I32))
+        load_words(raw_w[1], wa_words[1], PASSES)
+        load_words(raw_w[2], wb_words[0], PASSES)
         nc.sync.dma_start(list_b[:], offs2)
-        load_words(wa_w[0][:], wa_words[0], PASSES)
-        nc.sync.dma_start(out=x_w[:, :, :T], in_=x_words.rearrange("s p t d -> p s (t d)").bitcast(I32))
-        load_words(wa_w[1][:], wa_words[1], PASSES)
-        by_plane_w = [keep.tile([P, EXPERT], U8, name="by_plane_w%d" % e, align_bytes=64) for e in range(E1)]
-        by_plane_sc = [keep.tile([P, PASSES * H], U8, name="by_plane_sc%d" % e, align_bytes=64) for e in range(E1)]
 
-        def part_words(copy, e):
-            copy(
-                by_plane_w[e][:].bitcast(U16).rearrange("p (s d m) -> p s d m", s=PASSES, d=PACK),
-                wa_w[e][:].bitcast(U16).rearrange("p (s m d) -> p s d m", s=PASSES, d=PACK),
-            )
-
-        def part_scales(e):
-            nc.vector.tensor_copy(
-                by_plane_sc[e][:].rearrange("p (s d m) -> p s d m", s=PASSES, d=PACK),
-                wa_sc[:, e * PASSES * H : (e + 1) * PASSES * H].rearrange("p (s m d) -> p s d m", s=PASSES, d=PACK),
-            )
-
-        def move_scales(g):
-            for s in range(PASSES):
-                for q in range(4):
-                    at = 16 * s + 4 * q
-                    nc.sync.dma_start(
-                        out=moved_sc[g][s][32 * q : 32 * q + 4, :].bitcast(I32),
-                        in_=got_sc[g][at : at + 4, :].bitcast(I32),
-                    )
-
-        def gather_words(g, offsets, first, count):
+        def gather_words(g, offsets, first):
             for s in range(PASSES):
                 window = x_w[:, s, :].bitcast(U32)
                 nc.vector.tensor_copy(
-                    got_w[g][:, s, first : first + count], window.indirect(offsets[:, first // 16 : (first + count) // 16])
+                    got_w[g][:, s, first : first + HALF], window.indirect(offsets[:, first // 16 : (first + HALF) // 16])
                 )
 
-        nc.vector.tensor_copy(got_sc[0][:], x_sc[:].indirect(list_a[:]))
-        move_scales(0)
-        nc.vector.tensor_copy(got_sc[1][:], x_sc[:].indirect(list_b[:]))
-        for e in range(E1):
-            part_scales(e)
-        part_words(nc.scalar.copy, 0)
-        part_words(nc.scalar.copy, 1)
-        for e in range(E1):
-            gather_words(0, list_a, e * C1, C1)
-        gather_words(1, list_b, 0, T)
-
-        sizes = [E2 * EXPERT, E2 * PASSES * H]
-        late = keep.tile([P, sum(sizes)], U8, name="late", tag="after_scales", align_bytes=64)
-        wb_w, wb_sc = [late[:, sum(sizes[:i]) : sum(sizes[: i + 1])] for i in range(len(sizes))]
-        load_scales(wb_sc, wb_scales.rearrange("e s b c -> (e s) b c"), E2 * PASSES)
-        load_words(wb_w, wb_words.rearrange("e s p c -> (e s) p c"), E2 * PASSES)
-        move_scales(1)
-
-        win_a = [keep.tile([P, T], F32, name="win_a%d" % d) for d in range(PACK)]
-        win_c = {d: keep.tile([P, WIDE if d == 3 else T], F32, name="win_c%d" % d) for d in (0, 1, 3)}
-        staged = [keep.tile([P, PACK, T], F32, name="staged%d" % g) for g in range(2)]
-
-        def first_pool(e, acc, d, s):
-            slots = slice(e * C1, (e + 1) * C1)
-            column = s * H + d * P
-            nc.tensor.matmul_mx(
-                out=acc,
-                lhsT=by_plane_w[e][:, 2 * column : 2 * (column + P)].bitcast(FP4X4),
-                lhsT_scale=by_plane_sc[e][:, column : column + P],
-                rhs=got_w[0][:, s, slots].bitcast(FP8X4),
-                rhs_scale=moved_sc[0][s][:, slots],
-                start=(s == 0),
-                stop=(s == PASSES - 1),
+        def part_words(e):
+            nc.scalar.copy(
+                by_plane_w[e][:].bitcast(U16).rearrange("p (s d m) -> p s d m", s=PASSES, d=PACK),
+                raw_w[e].bitcast(U16).rearrange("p (s m d) -> p s d m", s=PASSES, d=PACK),
             )
 
-        def multiply(b):
-            slots = slice(b * BLOCK, (b + 1) * BLOCK)
-            acc = psum.tile([P, H], F32, name="acc", tag="plane", bufs=4)
+        nc.gpsimd.tensor_copy(
+            rows_by_plane[:].rearrange("p (d m) -> p d m", d=PACK), rows[:].rearrange("p (m d) -> p d m", d=PACK)
+        )
+        move_scales(by_plane_sc, rows_by_plane, PARTED * PASSES)
+        moved_sc = [head.tile([P, PASSES * T], U8, name="moved_sc0", offset=0, align_bytes=64)]
+        nc.vector.tensor_copy(got_sc[0][:], x_sc[:].indirect(list_a[:]))
+        move_scales(moved_sc[0], got_sc[0], PASSES)
+        wb_rest = head.tile([P, 3 * EXPERT], U8, name="wb_rest", offset=PASSES * T, align_bytes=64)
+        load_words(wb_rest[:], wb_words[1:].rearrange("e s p c -> (e s) p c"), 3 * PASSES)
+        raw_w.append(wb_rest[:, :EXPERT])
+        wb_w = wb_rest[:, EXPERT:]
+        for e in range(PARTED):
+            part_words(e)
+        gather_words(0, list_a, 0)
+        nc.vector.tensor_copy(got_sc[1][:], x_sc[:].indirect(list_b[:]))
+        gather_words(0, list_a, HALF)
+        gather_words(1, list_b, HALF)
+        gather_words(1, list_b, 0)
+
+        moved_sc.append(head.tile([P, PASSES * T], U8, name="moved_sc1", offset=SECOND - PASSES * T, align_bytes=64))
+        wb_sc = head.tile([P, 2 * PASSES * H], U8, name="wb_sc", offset=SECOND, align_bytes=64)
+        load_scales(wb_sc[:], wb_scales[2:].rearrange("e s b c -> (e s) b c"), 2 * PASSES)
+        move_scales(moved_sc[1], got_sc[1], PASSES)
+
+        staged = [keep.tile([P, PACK, T], F32, name="staged%d" % g) for g in range(2)]
+        win_a = [keep.tile([P, T], F32, name="win_a%d" % d) for d in range(PACK - 1)]
+        win_c = [keep.tile([P, WIDE if d == 1 else T], F32, name="win_c%d" % d) for d in range(PACK - 1)]
+
+        def by_plane(pool, e, slots, d, acc):
             for s in range(PASSES):
-                a = b * PASSES + s
+                column = s * H + d * P
+                scales = (2 * (PASSES * e + s) + pool) * H + d * P
                 nc.tensor.matmul_mx(
-                    out=acc[:],
-                    lhsT=got_w[1][:, s, slots].bitcast(FP8X4),
-                    lhsT_scale=moved_sc[1][s][:, slots],
-                    rhs=wb_w[:, a * 2 * H : (a + 1) * 2 * H].bitcast(FP4X4),
-                    rhs_scale=wb_sc[:, a * H : (a + 1) * H],
+                    out=acc,
+                    lhsT=by_plane_w[2 * pool + e][:, 2 * column : 2 * (column + P)].bitcast(FP4X4),
+                    lhsT_scale=by_plane_sc[:, scales : scales + P],
+                    rhs=got_w[pool][:, s, slots].bitcast(FP8X4),
+                    rhs_scale=moved_sc[pool][:, s * T + slots.start : s * T + slots.stop],
                     start=(s == 0),
                     stop=(s == PASSES - 1),
                 )
-            return acc[:].rearrange("u (m d) -> u d m", d=PACK)
 
-        def turn(sums):
-            parted = ring.tile([P, PACK, P], F32, name="parted")
-            nc.scalar.copy(parted[:], sums)
-            turned = psum.tile([P, PACK, BLOCK], F32, name="turned", bufs=4)
-            for d in range(PACK):
-                nc.tensor.transpose(turned[:, d, :], parted[:, d, :], ident[:])
-            return turned
-
-        def stage(b, turned):
-            nc.scalar.copy(staged[1][:, :, b * BLOCK : (b + 1) * BLOCK], turned[:])
-
-        def second_pool(e):
-            slots = slice(e * C2, (e + 1) * C2)
-            acc = psum.tile([P, PACK, C2], F32, name="rows", tag="plane", bufs=4)
-            for j in range(PACK):
-                for s in range(PASSES):
-                    column = (e * PASSES + s) * H + j * P
-                    nc.tensor.matmul_mx(
-                        out=acc[:, j, :],
-                        lhsT=wb_w[:, 2 * column : 2 * (column + P)].bitcast(FP4X4),
-                        lhsT_scale=wb_sc[:, column : column + P],
-                        rhs=got_w[1][:, s, slots].bitcast(FP8X4),
-                        rhs_scale=moved_sc[1][s][:, slots],
-                        start=(s == 0),
-                        stop=(s == PASSES - 1),
-                    )
-            nc.scalar.copy(rows_c[:, :, slots], acc[:])
+        def first_pool(e, d, acc):
+            by_plane(0, e, slice(e * C1, (e + 1) * C1), d, acc)
 
         def scatter(engine, window, offsets, plane, first, count):
             target = window[:].indirect(offsets[:, first // 16 : (first + count) // 16])
@@ -200,73 +163,92 @@ def tile_moe_pool_silu_kernel(
             else:
                 nc.scalar.activation(target, plane[:, first : first + count], COPY)
 
-        planes = [psum.tile([P, C1], F32, name="plane", bufs=4) for d in range(PACK)]
-        for s in range(PASSES):
-            for d in range(PACK):
-                first_pool(0, planes[d][:], d, s)
-        for d in range(PACK):
-            nc.scalar.activation(staged[0][:, d, :C1], planes[d][:], SILU)
-        scatter("scalar", win_a[3], list_a, staged[0][:, 3, :], 0, C1)
-        for d0 in (0, 2):
-            pair = psum.tile([P, 2, C1], F32, name="pair", tag="plane", bufs=4)
+        ends = bank(0, [2, C1])
+        first_pool(0, 0, ends[:, 0, :])
+        nc.scalar.activation(staged[0][:, 0, :C1], ends[:, 0, :], SILU)
+        scatter("vector", win_a[0], list_a, staged[0][:, 0, :], 0, C1)
+        for e, d0 in ((0, 1), (1, 0)):
+            pair = bank(1 + e, [2, C1])
             for d in range(2):
-                for s in range(PASSES):
-                    first_pool(1, pair[:, d, :], d0 + d, s)
-            nc.scalar.activation(staged[0][:, d0 : d0 + 2, C1:], pair[:], SILU)
-        scatter("scalar", win_a[3], list_a, staged[0][:, 3, :], C1, C1)
-        scatter("scalar", win_a[2], list_a, staged[0][:, 2, :], 0, BLOCK)
-        for d in range(2):
-            scatter("vector", win_a[d], list_a, staged[0][:, d, :], 0, C1)
-        scatter("vector", win_a[2], list_a, staged[0][:, 2, :], BLOCK, BLOCK)
+                first_pool(e, d0 + d, pair[:, d, :])
+            nc.scalar.activation(staged[0][:, d0 : d0 + 2, e * C1 : (e + 1) * C1], pair[:], SILU)
+            if e == 0:
+                scatter("scalar", win_a[2], list_a, staged[0][:, 2, :], 0, FILL)
+        first_pool(1, 2, ends[:, 1, :])
+        nc.scalar.activation(staged[0][:, 2, C1:], ends[:, 1, :], SILU)
+        scatter("vector", win_a[1], list_a, staged[0][:, 1, :], 0, C1)
+        scatter("vector", win_a[2], list_a, staged[0][:, 2, :], FILL, C1 - FILL)
         for d in range(PACK - 1):
             scatter("vector", win_a[d], list_a, staged[0][:, d, :], C1, C1)
 
         rows_c = shared.tile([P, PACK, HALF], F32, name="rows_c", offset=0, align_bytes=64)
-        turned = []
-        for e in range(E2 // 2):
-            second_pool(e)
-            turned.append(turn(multiply(e + 2)))
-        for d in (1, 0, 3, 2):
+        for f in range(2):
+            slots = slice(HALF + f * C2, HALF + (f + 1) * C2)
+            acc = bank(4 + f, [PACK, C2])
             for j in range(PACK):
-                nc.sync.dma_start(out=staged[1][32 * j : 32 * (j + 1), d, :HALF], in_=rows_c[d:P:PACK, j, :])
-        for b in (2, 3):
-            stage(b, turned[b - 2])
-        win_c[2] = shared.tile([P, T], F32, name="win_c2", offset=0, align_bytes=64)
-        w2 = shared.tile([P, 3 * N], U8, name="w2", offset=4 * T, align_bytes=64)
+                for s in range(PASSES):
+                    column = (f * PASSES + s) * H + j * P
+                    nc.tensor.matmul_mx(
+                        out=acc[:, j, :],
+                        lhsT=wb_w[:, 2 * column : 2 * (column + P)].bitcast(FP4X4),
+                        lhsT_scale=wb_sc[:, column : column + P],
+                        rhs=got_w[1][:, s, slots].bitcast(FP8X4),
+                        rhs_scale=moved_sc[1][:, s * T + slots.start : s * T + slots.stop],
+                        start=(s == 0),
+                        stop=(s == PASSES - 1),
+                    )
+            nc.scalar.copy(rows_c[:, :, f * C2 : (f + 1) * C2], acc[:])
+        for d in range(PACK):
+            for j in range(PACK):
+                nc.sync.dma_start(out=staged[1][32 * j : 32 * (j + 1), d, HALF:], in_=rows_c[d:P:PACK, j, :])
+
+        for f in range(2):
+            slots = slice(f * C2, (f + 1) * C2)
+            acc = bank(6 + f, [PACK, C2])
+            for d in range(PACK):
+                by_plane(1, f, slots, d, acc[:, d, :])
+            nc.scalar.copy(staged[1][:, :, slots], acc[:])
+        last = bank(3, [E1, C1])
+        for e in range(E1):
+            first_pool(e, 3, last[:, e, :])
+        nc.scalar.activation(staged[0][:, 3, :], last[:].rearrange("p e u -> p (e u)"), SILU)
+
+        w2 = shared.tile([P, 3 * N], U8, name="w2", offset=0, align_bytes=64)
+        win_c.append(shared.tile([P, T], F32, name="win_c3", offset=3 * N, align_bytes=64))
+        win_a.append(shared.tile([P, WIDE], F32, name="win_a3", offset=3 * N + 4 * T, align_bytes=64))
         w2_w, w2_sc = w2[:, : 2 * N], w2[:, 2 * N :]
         load_scales(w2_sc, w2_scales, 1)
         nc.sync.dma_start(out=w2_w.bitcast(I32), in_=w2_words[0].bitcast(I32))
 
-        for first in (HALF, 0):
-            scatter("scalar", win_c[1], list_b, staged[1][:, 1, :], first, HALF)
-        for first in (HALF, 0):
-            scatter("vector", win_c[0], list_b, staged[1][:, 0, :], first, HALF)
-        scatter("vector", win_c[3], list_b, staged[1][:, 3, :], 0, T)
-        for first in (HALF, 0):
-            scatter("scalar", win_c[2], list_b, staged[1][:, 2, :], first, HALF)
+        scatter("vector", win_c[1], list_b, staged[1][:, 1, :], 0, T)
+        scatter("vector", win_a[3], list_a, staged[0][:, 3, :], 0, T)
+        for d in (0, 2, 3):
+            for first in (0, HALF):
+                scatter("scalar", win_c[d], list_b, staged[1][:, d, :], first, HALF)
 
-        last = 2
-        h = [keep.tile([P, BLOCK, PACK], BF16, name="h%d" % j, tag="h%d" % j, align_bytes=64) for j in range(BLOCKS)]
-        planes_h = keep.tile([P, PACK, T], BF16, name="planes_h", tag="high")
+        woven = keep.tile([P, T * PACK], BF16, name="woven", align_bytes=64)
+        h = woven[:].rearrange("p (t d) -> p t d", d=PACK)
+        high = keep.tile([P, 2, T], BF16, name="high")
         for d in range(2):
-            nc.gpsimd.tensor_tensor(planes_h[:, d, :], win_a[d][:, :T], win_c[d][:, :T], MULT)
-        nc.vector.tensor_tensor(planes_h[:, 3, :], win_a[3][:, :T], win_c[3][:, :T], MULT)
+            nc.gpsimd.tensor_tensor(h[:, :, d], win_a[d][:, :T], win_c[d][:, :T], MULT)
+        nc.gpsimd.tensor_tensor(high[:, 0, :], win_a[2][:, :T], win_c[2][:, :T], MULT)
 
-        def product(j):
+        for j in range(BLOCKS):
             tokens = slice(j * BLOCK, (j + 1) * BLOCK)
-            nc.vector.tensor_tensor(planes_h[:, last, tokens], win_a[last][:, tokens], win_c[last][:, tokens], MULT)
-            if j >= BLOCKS // 2:
-                nc.scalar.copy(h[j][:], planes_h[:, :, tokens].rearrange("p d t -> p t d"))
+            nc.vector.tensor_tensor(high[:, 1, tokens], win_a[3][:, tokens], win_c[3][:, tokens], MULT)
+            nc.scalar.copy(h[:, tokens, 2:], high[:, :, tokens].rearrange("p d t -> p t d"))
 
-        banks = [("plane", 4), ("turned", 4)] * 4
-
-        def second_layer(j):
+        sums = []
+        for j in range(BLOCKS):
             h_w = ring.tile([P, BLOCK], U32, name="h_w", align_bytes=64)
             h_sc = ring.tile([P, BLOCK], U8, name="h_sc", align_bytes=64)
-            nc.vector.quantize_mx(out=h_w[:].bitcast(FP8X4), scales=h_sc[:], in_=h[j][:].rearrange("p t d -> p (t d)"))
+            nc.vector.quantize_mx(
+                out=h_w[:].bitcast(FP8X4),
+                scales=h_sc[:],
+                in_=woven[:, j * BLOCK * PACK : (j + 1) * BLOCK * PACK],
+            )
             for n in range(N // P):
-                tag, bufs = banks.pop(0)
-                acc = psum.tile([P, BLOCK], F32, name="acc2", tag=tag, bufs=bufs)
+                acc = bank(2 * j + n, [BLOCK])
                 nc.tensor.matmul_mx(
                     out=acc[:],
                     lhsT=w2_w[:, n * 2 * P : (n + 1) * 2 * P].bitcast(FP4X4),
@@ -278,25 +260,12 @@ def tile_moe_pool_silu_kernel(
                 )
                 sums.append((j, n, acc))
 
-        sums = []
-        for j in (2, 3, 0, 1):
-            product(j)
-        for j in range(BLOCKS // 2):
-            nc.vector.tensor_copy(h[j][:], planes_h[:, :, j * BLOCK : (j + 1) * BLOCK].rearrange("p d t -> p t d"))
-        for j in (2, 0, 3, 1):
-            second_layer(j)
-        after_pairs = keep.tile([P, 2, BLOCK], F32, name="after_pairs", tag="high")
-        after_codes = keep.tile([P, 2, BLOCK], F32, name="after_codes", tag="h1", align_bytes=64)
         for j, n, acc in sums:
-            if j == 0:
-                result = after_pairs[:, n, :]
-            elif j >= 2 and n == 1:
-                result = after_codes[:, j - 2, :]
+            result = ring.tile([P, BLOCK], F32, name="result", bufs=8)
+            on_scalar = j == 1 or (j >= 2 and n == 1)
+            if on_scalar:
+                nc.scalar.copy(result[:], acc[:])
             else:
-                result = ring.tile([P, BLOCK], F32, name="result", bufs=5)[:]
-            if n == 1 and j:
-                nc.vector.tensor_copy(result, acc[:])
-            else:
-                nc.scalar.copy(result, acc[:])
-            queue = nc.scalar if j % 2 and n == 0 else nc.sync
-            queue.dma_start(out=out[n * P : (n + 1) * P, j * BLOCK : (j + 1) * BLOCK], in_=result)
+                nc.vector.tensor_copy(result[:], acc[:])
+            queue = nc.scalar if j >= 2 and n == 1 else nc.sync
+            queue.dma_start(out=out[n * P : (n + 1) * P, j * BLOCK : (j + 1) * BLOCK], in_=result[:])

@@ -27,9 +27,8 @@ BLOCKS = T // BLOCK
 HALF = T // 2
 WIDE = 704
 EXPERT = PASSES * 2 * H
-PARTED = 4
+PARTED = 6
 FILL = 128
-SECOND = 2 * PASSES * T + 3 * EXPERT
 
 
 def tile_moe_pool_silu_kernel(
@@ -50,19 +49,24 @@ def tile_moe_pool_silu_kernel(
         list_a = lists.tile([P, T // 16], U16, name="list_a")
         list_b = lists.tile([P, T // 16], U16, name="list_b")
 
-        x_sc = keep.tile([P, WIDE], U8, name="x_sc", align_bytes=64)
+        x_sc = keep.tile([P, WIDE], U8, name="x_sc", tag="after_scales", align_bytes=64)
         x_w = keep.tile([P, PASSES, T], I32, name="x_w", align_bytes=64)
-        rows = head.tile([P, H], U8, name="rows", offset=PASSES * T - H // 2, align_bytes=64)
-        rows_by_plane = head.tile([P, H], U8, name="rows_by_plane", offset=SECOND - H // 2, align_bytes=64)
-        raw_w = [keep.tile([P, EXPERT], U8, name="raw_w%d" % e, align_bytes=64)[:] for e in range(PARTED - 1)]
-        by_plane_w = [keep.tile([P, EXPERT], U8, name="by_plane_w%d" % e, align_bytes=64) for e in range(PARTED)]
-        by_plane_sc = keep.tile([P, PARTED * PASSES * H], U8, name="by_plane_sc", align_bytes=64)
+        wa_sc = keep.tile([P, E1 * PASSES * H], U8, name="wa_sc", align_bytes=64)
+        raw_w = [keep.tile([P, EXPERT], U8, name="raw_w%d" % e, align_bytes=64)[:] for e in range(E1)]
+        by_plane_w = [keep.tile([P, EXPERT], U8, name="by_plane_w%d" % e, align_bytes=64) for e in range(PARTED - 1)]
+        by_plane_w.append(shared.tile([P, EXPERT], U8, name="by_plane_last", offset=EXPERT, align_bytes=64))
+        by_plane_sc = [keep.tile([P, PASSES * H], U8, name="by_plane_sc%d" % e, align_bytes=64)[:] for e in range(E1)]
+        rows = head.tile([P, H], U8, name="rows", offset=0, align_bytes=64)
+        rows_by_plane = keep.tile([P, H], U8, name="rows_by_plane", align_bytes=64)
+        wb_sc = keep.tile([P, E2 * PASSES * H], U8, name="wb_sc", tag="after_sums", align_bytes=64)
+        by_plane_sc.extend(wb_sc[:, f * PASSES * H : (f + 1) * PASSES * H] for f in range(E2))
         got_sc = [keep.tile([P, T], U8, name="got_sc%d" % g, align_bytes=64) for g in range(2)]
         got_w = [keep.tile([P, PASSES, T], U32, name="got_w%d" % g, align_bytes=64) for g in range(2)]
 
         nc.gpsimd.memset(x_sc[32:64, :T].bitcast(I32), 0)
         nc.gpsimd.memset(x_sc[64:, :T].bitcast(I32), 0)
         nc.gpsimd.memset(x_sc[:, T:].bitcast(I32), 0)
+        nc.vector.memset(wa_sc[:].bitcast(I32), 0)
         unread = keep.tile([P, 2], F32, name="unread")
         nc.vector.memset(unread[:, :1], 0.0)
         nc.scalar.activation(unread[:, 1:], unread[:, :1], SILU)
@@ -90,13 +94,12 @@ def tile_moe_pool_silu_kernel(
 
         nc.sync.dma_start(list_a[:], offs)
         nc.sync.dma_start(out=x_sc[: ROWS * PASSES, :T].bitcast(I32), in_=x_scales.bitcast(I32).rearrange("s b c -> b s c"))
-        for pool, scales in enumerate((wa_scales, wb_scales[:2])):
-            nc.sync.dma_start(out=rows[pool:P:2, :].bitcast(I32), in_=scales.bitcast(I32).rearrange("e s b c -> b (e s) c"))
+        nc.sync.dma_start(list_b[:], offs2)
+        load_scales(wa_sc[:], wa_scales.rearrange("e s b c -> (e s) b c"), E1 * PASSES)
         load_words(raw_w[0], wa_words[0], PASSES)
         nc.sync.dma_start(out=x_w[:], in_=x_words.rearrange("s p t d -> p s (t d)").bitcast(I32))
         load_words(raw_w[1], wa_words[1], PASSES)
-        load_words(raw_w[2], wb_words[0], PASSES)
-        nc.sync.dma_start(list_b[:], offs2)
+        nc.sync.dma_start(out=rows[:].bitcast(I32), in_=wb_scales.bitcast(I32).rearrange("e s b c -> b (e s) c"))
 
         def gather_words(g, offsets, first):
             for s in range(PASSES):
@@ -105,48 +108,56 @@ def tile_moe_pool_silu_kernel(
                     got_w[g][:, s, first : first + HALF], window.indirect(offsets[:, first // 16 : (first + HALF) // 16])
                 )
 
-        def part_words(e):
-            nc.scalar.copy(
+        def part_words(copy, e):
+            copy(
                 by_plane_w[e][:].bitcast(U16).rearrange("p (s d m) -> p s d m", s=PASSES, d=PACK),
                 raw_w[e].bitcast(U16).rearrange("p (s m d) -> p s d m", s=PASSES, d=PACK),
             )
 
+        def part_scales(e, scales):
+            nc.gpsimd.tensor_copy(
+                by_plane_sc[e].rearrange("p (s d m) -> p s d m", s=PASSES, d=PACK),
+                scales.rearrange("p (s m d) -> p s d m", s=PASSES, d=PACK),
+            )
+
+        part_scales(0, wa_sc[:, : PASSES * H])
         nc.gpsimd.tensor_copy(
             rows_by_plane[:].rearrange("p (d m) -> p d m", d=PACK), rows[:].rearrange("p (m d) -> p d m", d=PACK)
         )
-        move_scales(by_plane_sc, rows_by_plane, PARTED * PASSES)
-        moved_sc = [head.tile([P, PASSES * T], U8, name="moved_sc0", offset=0, align_bytes=64)]
+        part_scales(1, wa_sc[:, PASSES * H :])
+        moved_sc = [keep.tile([P, PASSES * T], U8, name="moved_sc%d" % g, align_bytes=64) for g in range(2)]
         nc.vector.tensor_copy(got_sc[0][:], x_sc[:].indirect(list_a[:]))
         move_scales(moved_sc[0], got_sc[0], PASSES)
-        wb_rest = head.tile([P, 3 * EXPERT], U8, name="wb_rest", offset=PASSES * T, align_bytes=64)
-        load_words(wb_rest[:], wb_words[1:].rearrange("e s p c -> (e s) p c"), 3 * PASSES)
-        raw_w.append(wb_rest[:, :EXPERT])
-        wb_w = wb_rest[:, EXPERT:]
-        for e in range(PARTED):
-            part_words(e)
-        gather_words(0, list_a, 0)
         nc.vector.tensor_copy(got_sc[1][:], x_sc[:].indirect(list_b[:]))
-        gather_words(0, list_a, HALF)
-        gather_words(1, list_b, HALF)
-        gather_words(1, list_b, 0)
+        for e in range(E1):
+            part_words(nc.scalar.copy, e)
+        for g, offsets in enumerate((list_a, list_b)):
+            for first in (0, HALF):
+                gather_words(g, offsets, first)
 
-        moved_sc.append(head.tile([P, PASSES * T], U8, name="moved_sc1", offset=SECOND - PASSES * T, align_bytes=64))
-        wb_sc = head.tile([P, 2 * PASSES * H], U8, name="wb_sc", offset=SECOND, align_bytes=64)
-        load_scales(wb_sc[:], wb_scales[2:].rearrange("e s b c -> (e s) b c"), 2 * PASSES)
+        wb_w = [
+            keep.tile([P, 2 * EXPERT], U8, name="wb_w0", tag="after_scales", align_bytes=64),
+            head.tile([P, 2 * EXPERT], U8, name="wb_w1", offset=0, align_bytes=64),
+        ]
+        load_words(wb_w[0][:], wb_words[:2].rearrange("e s p c -> (e s) p c"), 2 * PASSES)
         move_scales(moved_sc[1], got_sc[1], PASSES)
+        move_scales(wb_sc, rows_by_plane, E2 * PASSES)
+        load_words(wb_w[1][:], wb_words[2:].rearrange("e s p c -> (e s) p c"), 2 * PASSES)
+        raw_w.extend(wb_w[f // 2][:, f % 2 * EXPERT : (f % 2 + 1) * EXPERT] for f in range(E2))
+        for f in range(E2):
+            part_words(nc.gpsimd.tensor_copy, E1 + f)
 
-        staged = [keep.tile([P, PACK, T], F32, name="staged%d" % g) for g in range(2)]
+        staged = [keep.tile([P, PACK - 1 + g, T], F32, name="staged%d" % g) for g in range(2)]
         win_a = [keep.tile([P, T], F32, name="win_a%d" % d) for d in range(PACK - 1)]
-        win_c = [keep.tile([P, WIDE if d == 1 else T], F32, name="win_c%d" % d) for d in range(PACK - 1)]
+        win_c = [keep.tile([P, WIDE if d == 1 else T], F32, name="win_c%d" % d) for d in range(2)]
 
         def by_plane(pool, e, slots, d, acc):
             for s in range(PASSES):
                 column = s * H + d * P
-                scales = (2 * (PASSES * e + s) + pool) * H + d * P
                 nc.tensor.matmul_mx(
                     out=acc,
                     lhsT=by_plane_w[2 * pool + e][:, 2 * column : 2 * (column + P)].bitcast(FP4X4),
-                    lhsT_scale=by_plane_sc[:, scales : scales + P],
+                    lhsT_scale=by_plane_sc[2 * pool + e][:, column : column + P],
                     rhs=got_w[pool][:, s, slots].bitcast(FP8X4),
                     rhs_scale=moved_sc[pool][:, s * T + slots.start : s * T + slots.stop],
                     start=(s == 0),
@@ -175,56 +186,37 @@ def tile_moe_pool_silu_kernel(
             if e == 0:
                 scatter("scalar", win_a[2], list_a, staged[0][:, 2, :], 0, FILL)
         first_pool(1, 2, ends[:, 1, :])
-        nc.scalar.activation(staged[0][:, 2, C1:], ends[:, 1, :], SILU)
+        scatter("scalar", win_a[2], list_a, staged[0][:, 2, :], FILL, C1 - FILL)
         scatter("vector", win_a[1], list_a, staged[0][:, 1, :], 0, C1)
-        scatter("vector", win_a[2], list_a, staged[0][:, 2, :], FILL, C1 - FILL)
-        for d in range(PACK - 1):
+        for d in range(2):
             scatter("vector", win_a[d], list_a, staged[0][:, d, :], C1, C1)
 
-        rows_c = shared.tile([P, PACK, HALF], F32, name="rows_c", offset=0, align_bytes=64)
-        for f in range(2):
-            slots = slice(HALF + f * C2, HALF + (f + 1) * C2)
-            acc = bank(4 + f, [PACK, C2])
-            for j in range(PACK):
-                for s in range(PASSES):
-                    column = (f * PASSES + s) * H + j * P
-                    nc.tensor.matmul_mx(
-                        out=acc[:, j, :],
-                        lhsT=wb_w[:, 2 * column : 2 * (column + P)].bitcast(FP4X4),
-                        lhsT_scale=wb_sc[:, column : column + P],
-                        rhs=got_w[1][:, s, slots].bitcast(FP8X4),
-                        rhs_scale=moved_sc[1][:, s * T + slots.start : s * T + slots.stop],
-                        start=(s == 0),
-                        stop=(s == PASSES - 1),
-                    )
-            nc.scalar.copy(rows_c[:, :, f * C2 : (f + 1) * C2], acc[:])
-        for d in range(PACK):
-            for j in range(PACK):
-                nc.sync.dma_start(out=staged[1][32 * j : 32 * (j + 1), d, HALF:], in_=rows_c[d:P:PACK, j, :])
-
-        for f in range(2):
+        for f in range(E2):
             slots = slice(f * C2, (f + 1) * C2)
-            acc = bank(6 + f, [PACK, C2])
+            acc = bank(4 + f, [PACK, C2])
             for d in range(PACK):
                 by_plane(1, f, slots, d, acc[:, d, :])
             nc.scalar.copy(staged[1][:, :, slots], acc[:])
         last = bank(3, [E1, C1])
         for e in range(E1):
             first_pool(e, 3, last[:, e, :])
-        nc.scalar.activation(staged[0][:, 3, :], last[:].rearrange("p e u -> p (e u)"), SILU)
+        staged_last = shared.tile([P, C1 + T], F32, name="staged_last", offset=0, align_bytes=64)
+        nc.scalar.activation(staged_last[:, :C1], ends[:, 1, :], SILU)
+        nc.scalar.activation(staged_last[:, C1:], last[:].rearrange("p e u -> p (e u)"), SILU)
 
-        w2 = shared.tile([P, 3 * N], U8, name="w2", offset=0, align_bytes=64)
-        win_c.append(shared.tile([P, T], F32, name="win_c3", offset=3 * N, align_bytes=64))
-        win_a.append(shared.tile([P, WIDE], F32, name="win_a3", offset=3 * N + 4 * T, align_bytes=64))
+        w2 = head.tile([P, 3 * N], U8, name="w2", offset=0, align_bytes=64)
+        win_c.append(keep.tile([P, T], F32, name="win_c2", tag="after_sums", align_bytes=64))
+        win_c.append(shared.tile([P, T], F32, name="win_c3", offset=4 * (C1 + T), align_bytes=64))
+        win_a.append(keep.tile([P, WIDE], F32, name="win_a3"))
         w2_w, w2_sc = w2[:, : 2 * N], w2[:, 2 * N :]
         load_scales(w2_sc, w2_scales, 1)
         nc.sync.dma_start(out=w2_w.bitcast(I32), in_=w2_words[0].bitcast(I32))
 
         scatter("vector", win_c[1], list_b, staged[1][:, 1, :], 0, T)
-        scatter("vector", win_a[3], list_a, staged[0][:, 3, :], 0, T)
-        for d in (0, 2, 3):
-            for first in (0, HALF):
-                scatter("scalar", win_c[d], list_b, staged[1][:, d, :], first, HALF)
+        nc.vector.tensor_copy(win_a[2][:].indirect(list_a[:, C1 // 16 :]), staged_last[:, :C1])
+        scatter("vector", win_a[3], list_a, staged_last[:, C1:], 0, T)
+        for d, first in ((0, 0), (2, 0), (0, HALF), (2, HALF), (3, 0), (3, HALF)):
+            scatter("scalar", win_c[d], list_b, staged[1][:, d, :], first, HALF)
 
         woven = keep.tile([P, T * PACK], BF16, name="woven", align_bytes=64)
         h = woven[:].rearrange("p (t d) -> p t d", d=PACK)

@@ -53,12 +53,14 @@ def tile_moe_pool_silu_kernel(
         x_w = keep.tile([P, PASSES, T], I32, name="x_w", align_bytes=64)
         wa_sc = keep.tile([P, E1 * PASSES * H], U8, name="wa_sc", align_bytes=64)
         raw_w = [keep.tile([P, EXPERT], U8, name="raw_w%d" % e, align_bytes=64)[:] for e in range(E1)]
-        by_plane_w = [keep.tile([P, EXPERT], U8, name="by_plane_w%d" % e, align_bytes=64) for e in range(PARTED - 1)]
-        by_plane_w.append(shared.tile([P, EXPERT], U8, name="by_plane_last", offset=EXPERT, align_bytes=64))
+        by_plane_w = [
+            keep.tile([P, EXPERT], U8, name="by_plane_w%d" % e, tag="plane_w%d" % e, align_bytes=64) for e in range(PARTED - 1)
+        ]
+        by_plane_w.append(shared.tile([P, EXPERT], U8, name="by_plane_last", offset=3 * EXPERT // 2, align_bytes=64))
         by_plane_sc = [keep.tile([P, PASSES * H], U8, name="by_plane_sc%d" % e, align_bytes=64)[:] for e in range(E1)]
         rows = head.tile([P, H], U8, name="rows", offset=0, align_bytes=64)
         rows_by_plane = keep.tile([P, H], U8, name="rows_by_plane", align_bytes=64)
-        wb_sc = keep.tile([P, E2 * PASSES * H], U8, name="wb_sc", tag="after_sums", align_bytes=64)
+        wb_sc = keep.tile([P, E2 * PASSES * H], U8, name="wb_sc", align_bytes=64)
         by_plane_sc.extend(wb_sc[:, f * PASSES * H : (f + 1) * PASSES * H] for f in range(E2))
         got_sc = [keep.tile([P, T], U8, name="got_sc%d" % g, align_bytes=64) for g in range(2)]
         got_w = [keep.tile([P, PASSES, T], U32, name="got_w%d" % g, align_bytes=64) for g in range(2)]
@@ -149,7 +151,7 @@ def tile_moe_pool_silu_kernel(
 
         staged = [keep.tile([P, PACK - 1 + g, T], F32, name="staged%d" % g) for g in range(2)]
         win_a = [keep.tile([P, T], F32, name="win_a%d" % d) for d in range(PACK - 1)]
-        win_c = [keep.tile([P, WIDE if d == 1 else T], F32, name="win_c%d" % d) for d in range(2)]
+        win_c = [keep.tile([P, T], F32, name="win_c%d" % d) for d in range(2)]
 
         def by_plane(pool, e, slots, d, acc):
             for s in range(PASSES):
@@ -178,18 +180,18 @@ def tile_moe_pool_silu_kernel(
         first_pool(0, 0, ends[:, 0, :])
         nc.scalar.activation(staged[0][:, 0, :C1], ends[:, 0, :], SILU)
         scatter("vector", win_a[0], list_a, staged[0][:, 0, :], 0, C1)
-        for e, d0 in ((0, 1), (1, 0)):
-            pair = bank(1 + e, [2, C1])
-            for d in range(2):
-                first_pool(e, d0 + d, pair[:, d, :])
-            nc.scalar.activation(staged[0][:, d0 : d0 + 2, e * C1 : (e + 1) * C1], pair[:], SILU)
-            if e == 0:
-                scatter("scalar", win_a[2], list_a, staged[0][:, 2, :], 0, FILL)
-        first_pool(1, 2, ends[:, 1, :])
+        pairs = [bank(1 + e, [2, C1]) for e in range(E1)]
+        for d in range(2):
+            first_pool(0, 1 + d, pairs[0][:, d, :])
+        nc.scalar.activation(staged[0][:, 1:3, :C1], pairs[0][:], SILU)
+        scatter("scalar", win_a[2], list_a, staged[0][:, 2, :], 0, FILL)
+        first_pool(1, 0, ends[:, 1, :])
+        nc.scalar.activation(staged[0][:, 0, C1:], ends[:, 1, :], SILU)
         scatter("scalar", win_a[2], list_a, staged[0][:, 2, :], FILL, C1 - FILL)
         scatter("vector", win_a[1], list_a, staged[0][:, 1, :], 0, C1)
+        scatter("vector", win_a[0], list_a, staged[0][:, 0, :], C1, C1)
         for d in range(2):
-            scatter("vector", win_a[d], list_a, staged[0][:, d, :], C1, C1)
+            first_pool(1, 1 + d, pairs[1][:, d, :])
 
         for f in range(E2):
             slots = slice(f * C2, (f + 1) * C2)
@@ -200,23 +202,33 @@ def tile_moe_pool_silu_kernel(
         last = bank(3, [E1, C1])
         for e in range(E1):
             first_pool(e, 3, last[:, e, :])
-        staged_last = shared.tile([P, C1 + T], F32, name="staged_last", offset=0, align_bytes=64)
-        nc.scalar.activation(staged_last[:, :C1], ends[:, 1, :], SILU)
-        nc.scalar.activation(staged_last[:, C1:], last[:].rearrange("p e u -> p (e u)"), SILU)
+        staged_last = shared.tile([P, 2 * T], F32, name="staged_last", offset=0, align_bytes=64)
+        nc.scalar.activation(staged_last[:, :T], pairs[1][:].rearrange("p d u -> p (d u)"), SILU)
 
         w2 = head.tile([P, 3 * N], U8, name="w2", offset=0, align_bytes=64)
-        win_c.append(keep.tile([P, T], F32, name="win_c2", tag="after_sums", align_bytes=64))
-        win_c.append(shared.tile([P, T], F32, name="win_c3", offset=4 * (C1 + T), align_bytes=64))
+        win_c.append(keep.tile([P, T], F32, name="win_c2", tag="plane_w%d" % (PARTED - 2), align_bytes=64))
+        win_c.append(shared.tile([P, T], F32, name="win_c3", offset=8 * T, align_bytes=64))
         win_a.append(keep.tile([P, WIDE], F32, name="win_a3"))
         w2_w, w2_sc = w2[:, : 2 * N], w2[:, 2 * N :]
         load_scales(w2_sc, w2_scales, 1)
         nc.sync.dma_start(out=w2_w.bitcast(I32), in_=w2_words[0].bitcast(I32))
 
-        scatter("vector", win_c[1], list_b, staged[1][:, 1, :], 0, T)
-        nc.vector.tensor_copy(win_a[2][:].indirect(list_a[:, C1 // 16 :]), staged_last[:, :C1])
-        scatter("vector", win_a[3], list_a, staged_last[:, C1:], 0, T)
-        for d, first in ((0, 0), (2, 0), (0, HALF), (2, HALF), (3, 0), (3, HALF)):
-            scatter("scalar", win_c[d], list_b, staged[1][:, d, :], first, HALF)
+        def scatter_late(engine, d, first, count):
+            scatter(engine, win_a[d], list_a[:, C1 // 16 :], staged_last[:, (d - 1) * C1 : d * C1], first, count)
+
+        scatter("vector", win_c[0], list_b, staged[1][:, 0, :], 0, HALF)
+        scatter("vector", win_c[2], list_b, staged[1][:, 2, :], 0, C2)
+        scatter("vector", win_c[0], list_b, staged[1][:, 0, :], HALF, HALF)
+        scatter("scalar", win_c[1], list_b, staged[1][:, 1, :], 0, HALF)
+        scatter_late("scalar", 2, 0, C2)
+        scatter("scalar", win_c[1], list_b, staged[1][:, 1, :], HALF, HALF)
+        nc.scalar.activation(staged_last[:, T:], last[:].rearrange("p e u -> p (e u)"), SILU)
+        scatter("scalar", win_c[2], list_b, staged[1][:, 2, :], C2, T - C2)
+        for first in (0, HALF):
+            scatter("scalar", win_c[3], list_b, staged[1][:, 3, :], first, HALF)
+        scatter_late("vector", 1, 0, C1)
+        scatter_late("vector", 2, C2, C1 - C2)
+        scatter("vector", win_a[3], list_a, staged_last[:, T:], 0, T)
 
         woven = keep.tile([P, T * PACK], BF16, name="woven", align_bytes=64)
         h = woven[:].rearrange("p (t d) -> p t d", d=PACK)
@@ -225,13 +237,16 @@ def tile_moe_pool_silu_kernel(
             nc.gpsimd.tensor_tensor(h[:, :, d], win_a[d][:, :T], win_c[d][:, :T], MULT)
         nc.gpsimd.tensor_tensor(high[:, 0, :], win_a[2][:, :T], win_c[2][:, :T], MULT)
 
-        for j in range(BLOCKS):
-            tokens = slice(j * BLOCK, (j + 1) * BLOCK)
+        for first, count in ((2 * BLOCK, BLOCK), (3 * BLOCK, BLOCK), (0, HALF)):
+            tokens = slice(first, first + count)
             nc.vector.tensor_tensor(high[:, 1, tokens], win_a[3][:, tokens], win_c[3][:, tokens], MULT)
-            nc.scalar.copy(h[:, tokens, 2:], high[:, :, tokens].rearrange("p d t -> p t d"))
+        for j in (2, 3, 0, 1):
+            tokens = slice(j * BLOCK, (j + 1) * BLOCK)
+            weave = nc.scalar.copy if j >= 2 else nc.vector.tensor_copy
+            weave(h[:, tokens, 2:], high[:, :, tokens].rearrange("p d t -> p t d"))
 
         sums = []
-        for j in range(BLOCKS):
+        for step, j in enumerate((2, 0, 3, 1)):
             h_w = ring.tile([P, BLOCK], U32, name="h_w", align_bytes=64)
             h_sc = ring.tile([P, BLOCK], U8, name="h_sc", align_bytes=64)
             nc.vector.quantize_mx(
@@ -240,7 +255,7 @@ def tile_moe_pool_silu_kernel(
                 in_=woven[:, j * BLOCK * PACK : (j + 1) * BLOCK * PACK],
             )
             for n in range(N // P):
-                acc = bank(2 * j + n, [BLOCK])
+                acc = bank(2 * step + n, [BLOCK])
                 nc.tensor.matmul_mx(
                     out=acc[:],
                     lhsT=w2_w[:, n * 2 * P : (n + 1) * 2 * P].bitcast(FP4X4),
@@ -250,14 +265,13 @@ def tile_moe_pool_silu_kernel(
                     start=True,
                     stop=True,
                 )
-                sums.append((j, n, acc))
+                sums.append((step, j, n, acc))
 
-        for j, n, acc in sums:
+        for step, j, n, acc in sums:
             result = ring.tile([P, BLOCK], F32, name="result", bufs=8)
-            on_scalar = j == 1 or (j >= 2 and n == 1)
-            if on_scalar:
-                nc.scalar.copy(result[:], acc[:])
-            else:
+            if step >= 1 and n == 1:
                 nc.vector.tensor_copy(result[:], acc[:])
-            queue = nc.scalar if j >= 2 and n == 1 else nc.sync
+            else:
+                nc.scalar.copy(result[:], acc[:])
+            queue = nc.scalar if step >= 2 and n == 0 else nc.sync
             queue.dma_start(out=out[n * P : (n + 1) * P, j * BLOCK : (j + 1) * BLOCK], in_=result[:])

@@ -29,6 +29,7 @@ WIDE = 704
 EXPERT = PASSES * 2 * H
 PARTED = 6
 FILL = 128
+SHARE = 96
 
 
 def tile_moe_pool_silu_kernel(
@@ -98,8 +99,8 @@ def tile_moe_pool_silu_kernel(
         nc.sync.dma_start(out=x_sc[: ROWS * PASSES, :T].bitcast(I32), in_=x_scales.bitcast(I32).rearrange("s b c -> b s c"))
         nc.sync.dma_start(list_b[:], offs2)
         load_scales(wa_sc[:], wa_scales.rearrange("e s b c -> (e s) b c"), E1 * PASSES)
-        load_words(raw_w[0], wa_words[0], PASSES)
         nc.sync.dma_start(out=x_w[:], in_=x_words.rearrange("s p t d -> p s (t d)").bitcast(I32))
+        load_words(raw_w[0], wa_words[0], PASSES)
         load_words(raw_w[1], wa_words[1], PASSES)
         nc.sync.dma_start(out=rows[:].bitcast(I32), in_=wb_scales.bitcast(I32).rearrange("e s b c -> b (e s) c"))
 
@@ -110,10 +111,10 @@ def tile_moe_pool_silu_kernel(
                     got_w[g][:, s, first : first + HALF], window.indirect(offsets[:, first // 16 : (first + HALF) // 16])
                 )
 
-        def part_words(copy, e):
+        def part_words(copy, e, planes=slice(0, PACK)):
             copy(
-                by_plane_w[e][:].bitcast(U16).rearrange("p (s d m) -> p s d m", s=PASSES, d=PACK),
-                raw_w[e].bitcast(U16).rearrange("p (s m d) -> p s d m", s=PASSES, d=PACK),
+                by_plane_w[e][:].bitcast(U16).rearrange("p (s d m) -> p s d m", s=PASSES, d=PACK)[:, :, planes, :],
+                raw_w[e].bitcast(U16).rearrange("p (s m d) -> p s d m", s=PASSES, d=PACK)[:, :, planes, :],
             )
 
         def part_scales(e, scales):
@@ -131,8 +132,9 @@ def tile_moe_pool_silu_kernel(
         nc.vector.tensor_copy(got_sc[0][:], x_sc[:].indirect(list_a[:]))
         move_scales(moved_sc[0], got_sc[0], PASSES)
         nc.vector.tensor_copy(got_sc[1][:], x_sc[:].indirect(list_b[:]))
-        for e in range(E1):
-            part_words(nc.scalar.copy, e)
+        part_words(nc.scalar.copy, 0, slice(0, 1))
+        part_words(nc.scalar.copy, 0, slice(1, PACK))
+        part_words(nc.scalar.copy, 1)
         for g, offsets in enumerate((list_a, list_b)):
             for first in (0, HALF):
                 gather_words(g, offsets, first)
@@ -220,14 +222,14 @@ def tile_moe_pool_silu_kernel(
         scatter("vector", win_c[2], list_b, staged[1][:, 2, :], 0, C2)
         scatter("vector", win_c[0], list_b, staged[1][:, 0, :], HALF, HALF)
         scatter("scalar", win_c[1], list_b, staged[1][:, 1, :], 0, HALF)
-        scatter_late("scalar", 2, 0, C2)
+        scatter_late("scalar", 2, 0, SHARE)
         scatter("scalar", win_c[1], list_b, staged[1][:, 1, :], HALF, HALF)
         nc.scalar.activation(staged_last[:, T:], last[:].rearrange("p e u -> p (e u)"), SILU)
         scatter("scalar", win_c[2], list_b, staged[1][:, 2, :], C2, T - C2)
         for first in (0, HALF):
             scatter("scalar", win_c[3], list_b, staged[1][:, 3, :], first, HALF)
         scatter_late("vector", 1, 0, C1)
-        scatter_late("vector", 2, C2, C1 - C2)
+        scatter_late("vector", 2, SHARE, C1 - SHARE)
         scatter("vector", win_a[3], list_a, staged_last[:, T:], 0, T)
 
         woven = keep.tile([P, T * PACK], BF16, name="woven", align_bytes=64)

@@ -29,7 +29,6 @@ WIDE = 704
 EXPERT = PASSES * 2 * H
 PARTED = 6
 FILL = 128
-SHARE = 96
 
 
 def tile_moe_pool_silu_kernel(
@@ -51,7 +50,7 @@ def tile_moe_pool_silu_kernel(
         list_b = lists.tile([P, T // 16], U16, name="list_b")
 
         x_sc = keep.tile([P, WIDE], U8, name="x_sc", tag="after_scales", align_bytes=64)
-        x_w = keep.tile([P, PASSES, T], I32, name="x_w", align_bytes=64)
+        x_w = keep.tile([P, PASSES, WIDE], I32, name="x_w", align_bytes=64)
         wa_sc = keep.tile([P, E1 * PASSES * H], U8, name="wa_sc", align_bytes=64)
         raw_w = [keep.tile([P, EXPERT], U8, name="raw_w%d" % e, align_bytes=64)[:] for e in range(E1)]
         by_plane_w = [
@@ -69,6 +68,7 @@ def tile_moe_pool_silu_kernel(
         nc.gpsimd.memset(x_sc[32:64, :T].bitcast(I32), 0)
         nc.gpsimd.memset(x_sc[64:, :T].bitcast(I32), 0)
         nc.gpsimd.memset(x_sc[:, T:].bitcast(I32), 0)
+        nc.gpsimd.memset(x_w[:, :, T:], 0)
         nc.vector.memset(wa_sc[:].bitcast(I32), 0)
         unread = keep.tile([P, 2], F32, name="unread")
         nc.vector.memset(unread[:, :1], 0.0)
@@ -99,16 +99,16 @@ def tile_moe_pool_silu_kernel(
         nc.sync.dma_start(out=x_sc[: ROWS * PASSES, :T].bitcast(I32), in_=x_scales.bitcast(I32).rearrange("s b c -> b s c"))
         nc.sync.dma_start(list_b[:], offs2)
         load_scales(wa_sc[:], wa_scales.rearrange("e s b c -> (e s) b c"), E1 * PASSES)
-        nc.sync.dma_start(out=x_w[:], in_=x_words.rearrange("s p t d -> p s (t d)").bitcast(I32))
+        nc.sync.dma_start(out=x_w[:, :, :T], in_=x_words.rearrange("s p t d -> p s (t d)").bitcast(I32))
         load_words(raw_w[0], wa_words[0], PASSES)
-        load_words(raw_w[1], wa_words[1], PASSES)
         nc.sync.dma_start(out=rows[:].bitcast(I32), in_=wb_scales.bitcast(I32).rearrange("e s b c -> b (e s) c"))
+        load_words(raw_w[1], wa_words[1], PASSES)
 
-        def gather_words(g, offsets, first):
+        def gather_words(g, offsets, first, count):
             for s in range(PASSES):
                 window = x_w[:, s, :].bitcast(U32)
                 nc.vector.tensor_copy(
-                    got_w[g][:, s, first : first + HALF], window.indirect(offsets[:, first // 16 : (first + HALF) // 16])
+                    got_w[g][:, s, first : first + count], window.indirect(offsets[:, first // 16 : (first + count) // 16])
                 )
 
         def part_words(copy, e, planes=slice(0, PACK)):
@@ -134,10 +134,11 @@ def tile_moe_pool_silu_kernel(
         nc.vector.tensor_copy(got_sc[1][:], x_sc[:].indirect(list_b[:]))
         part_words(nc.scalar.copy, 0, slice(0, 1))
         part_words(nc.scalar.copy, 0, slice(1, PACK))
-        part_words(nc.scalar.copy, 1)
-        for g, offsets in enumerate((list_a, list_b)):
-            for first in (0, HALF):
-                gather_words(g, offsets, first)
+        part_words(nc.scalar.copy, 1, slice(0, 1))
+        part_words(nc.gpsimd.tensor_copy, 1, slice(1, PACK))
+        for first in (0, HALF):
+            gather_words(0, list_a, first, HALF)
+        gather_words(1, list_b, 0, T)
 
         wb_w = [
             keep.tile([P, 2 * EXPERT], U8, name="wb_w0", tag="after_scales", align_bytes=64),
@@ -181,15 +182,15 @@ def tile_moe_pool_silu_kernel(
         ends = bank(0, [2, C1])
         first_pool(0, 0, ends[:, 0, :])
         nc.scalar.activation(staged[0][:, 0, :C1], ends[:, 0, :], SILU)
-        scatter("vector", win_a[0], list_a, staged[0][:, 0, :], 0, C1)
+        scatter("scalar", win_a[0], list_a, staged[0][:, 0, :], 0, FILL)
+        scatter("vector", win_a[0], list_a, staged[0][:, 0, :], FILL, C1 - FILL)
         pairs = [bank(1 + e, [2, C1]) for e in range(E1)]
         for d in range(2):
             first_pool(0, 1 + d, pairs[0][:, d, :])
         nc.scalar.activation(staged[0][:, 1:3, :C1], pairs[0][:], SILU)
-        scatter("scalar", win_a[2], list_a, staged[0][:, 2, :], 0, FILL)
         first_pool(1, 0, ends[:, 1, :])
         nc.scalar.activation(staged[0][:, 0, C1:], ends[:, 1, :], SILU)
-        scatter("scalar", win_a[2], list_a, staged[0][:, 2, :], FILL, C1 - FILL)
+        scatter("scalar", win_a[2], list_a, staged[0][:, 2, :], 0, C1)
         scatter("vector", win_a[1], list_a, staged[0][:, 1, :], 0, C1)
         scatter("vector", win_a[0], list_a, staged[0][:, 0, :], C1, C1)
         for d in range(2):
@@ -222,14 +223,13 @@ def tile_moe_pool_silu_kernel(
         scatter("vector", win_c[2], list_b, staged[1][:, 2, :], 0, C2)
         scatter("vector", win_c[0], list_b, staged[1][:, 0, :], HALF, HALF)
         scatter("scalar", win_c[1], list_b, staged[1][:, 1, :], 0, HALF)
-        scatter_late("scalar", 2, 0, SHARE)
         scatter("scalar", win_c[1], list_b, staged[1][:, 1, :], HALF, HALF)
         nc.scalar.activation(staged_last[:, T:], last[:].rearrange("p e u -> p (e u)"), SILU)
+        scatter("scalar", win_c[3], list_b, staged[1][:, 3, :], 0, HALF)
         scatter("scalar", win_c[2], list_b, staged[1][:, 2, :], C2, T - C2)
-        for first in (0, HALF):
-            scatter("scalar", win_c[3], list_b, staged[1][:, 3, :], first, HALF)
+        scatter("scalar", win_c[3], list_b, staged[1][:, 3, :], HALF, HALF)
         scatter_late("vector", 1, 0, C1)
-        scatter_late("vector", 2, SHARE, C1 - SHARE)
+        scatter_late("vector", 2, 0, C1)
         scatter("vector", win_a[3], list_a, staged_last[:, T:], 0, T)
 
         woven = keep.tile([P, T * PACK], BF16, name="woven", align_bytes=64)

@@ -28,7 +28,7 @@ HALF = T // 2
 WIDE = 704
 EXPERT = PASSES * 2 * H
 PARTED = 6
-FILL = 128
+FILL = 160
 
 
 def tile_moe_pool_silu_kernel(
@@ -239,8 +239,8 @@ def tile_moe_pool_silu_kernel(
             nc.gpsimd.tensor_tensor(h[:, :, d], win_a[d][:, :T], win_c[d][:, :T], MULT)
         nc.gpsimd.tensor_tensor(high[:, 0, :], win_a[2][:, :T], win_c[2][:, :T], MULT)
 
-        for first, count in ((2 * BLOCK, BLOCK), (3 * BLOCK, BLOCK), (0, HALF)):
-            tokens = slice(first, first + count)
+        for j in (2, 0, 3, 1):
+            tokens = slice(j * BLOCK, (j + 1) * BLOCK)
             nc.vector.tensor_tensor(high[:, 1, tokens], win_a[3][:, tokens], win_c[3][:, tokens], MULT)
         for j in (2, 3, 0, 1):
             tokens = slice(j * BLOCK, (j + 1) * BLOCK)

@@ -28,7 +28,7 @@ HALF = T // 2
 WIDE = 704
 EXPERT = PASSES * 2 * H
 PARTED = 6
-FILL = 160
+FILL = 192
 
 
 def tile_moe_pool_silu_kernel(
@@ -180,8 +180,9 @@ def tile_moe_pool_silu_kernel(
                 nc.scalar.activation(target, plane[:, first : first + count], COPY)
 
         ends = bank(0, [2, C1])
-        first_pool(0, 0, ends[:, 0, :])
-        nc.scalar.activation(staged[0][:, 0, :C1], ends[:, 0, :], SILU)
+        for acc, first in ((ends[:, 0, :BLOCK], 0), (bank(7, [BLOCK])[:], BLOCK)):
+            by_plane(0, 0, slice(first, first + BLOCK), 0, acc)
+            nc.scalar.activation(staged[0][:, 0, first : first + BLOCK], acc, SILU)
         scatter("scalar", win_a[0], list_a, staged[0][:, 0, :], 0, FILL)
         scatter("vector", win_a[0], list_a, staged[0][:, 0, :], FILL, C1 - FILL)
         pairs = [bank(1 + e, [2, C1]) for e in range(E1)]

@@ -272,9 +272,9 @@ def tile_moe_pool_silu_kernel(
 
         for step, j, n, acc in sums:
             result = ring.tile([P, BLOCK], F32, name="result", bufs=8)
-            if step >= 1 and n == 1:
+            if step == 3 or (step >= 1 and n == 1):
                 nc.vector.tensor_copy(result[:], acc[:])
             else:
                 nc.scalar.copy(result[:], acc[:])
-            queue = nc.scalar if step >= 2 and n == 0 else nc.sync
+            queue = nc.scalar if step in (1, 2) and n == 0 else nc.sync
             queue.dma_start(out=out[n * P : (n + 1) * P, j * BLOCK : (j + 1) * BLOCK], in_=result[:])

from contextlib import ExitStack

import concourse.mybir as mybir

K, T, H, N = 1024, 512, 512, 256
E1, C1, E2, C2 = 2, 256, 4, 128
FLOPS = 2 * K * H * T * 2 + 2 * H * N * T

F32 = mybir.dt.float32
BF16 = mybir.dt.bfloat16
I32 = mybir.dt.int32
U32 = mybir.dt.uint32
U16 = mybir.dt.uint16
U8 = mybir.dt.uint8
FP8X4 = mybir.dt.float8_e4m3fn_x4
FP4X4 = mybir.dt.float4_e2m1fn_x4
SILU = mybir.ActivationFunctionType.Silu
COPY = mybir.ActivationFunctionType.Copy
MULT = mybir.AluOpType.mult

P = 128
PACK = 4
PASSES = 2
ROWS = 16
BLOCK = 128
BLOCKS = T // BLOCK
HALF = T // 2
WIDE = 704
EXPERT = PASSES * 2 * H
PARTED = 6
FILL = 192


def tile_moe_pool_silu_kernel(
    tc, x_words, x_scales, wa_words, wa_scales, wb_words, wb_scales, w2_words, w2_scales, offs, offs2, out
):
    nc = tc.nc
    with ExitStack() as ctx:
        lists = ctx.enter_context(tc.tile_pool(name="lists", bufs=1))
        keep = ctx.enter_context(tc.tile_pool(name="keep", bufs=1))
        shared = ctx.enter_context(tc.tile_pool(name="shared", bufs=1))
        head = ctx.enter_context(tc.tile_pool(name="head", bufs=1))
        ring = ctx.enter_context(tc.tile_pool(name="ring", bufs=4))
        psum = ctx.enter_context(tc.psum_pool(name="psum", bufs=1))

        def bank(b, shape):
            return psum.tile([P] + shape, F32, name="bank%d" % b, tag="bank%d" % b)

        list_a = lists.tile([P, T // 16], U16, name="list_a")
        list_b = lists.tile([P, T // 16], U16, name="list_b")

        x_sc = keep.tile([P, WIDE], U8, name="x_sc", tag="after_scales", align_bytes=64)
        x_w = keep.tile([P, PASSES, WIDE], I32, name="x_w", align_bytes=64)
        wa_sc = keep.tile([P, E1 * PASSES * H], U8, name="wa_sc", align_bytes=64)
        raw_w = [keep.tile([P, EXPERT], U8, name="raw_w%d" % e, align_bytes=64)[:] for e in range(E1)]
        by_plane_w = [
            keep.tile([P, EXPERT], U8, name="by_plane_w%d" % e, tag="plane_w%d" % e, align_bytes=64) for e in range(PARTED - 1)
        ]
        by_plane_w.append(shared.tile([P, EXPERT], U8, name="by_plane_last", offset=3 * EXPERT // 2, align_bytes=64))
        by_plane_sc = [keep.tile([P, PASSES * H], U8, name="by_plane_sc%d" % e, align_bytes=64)[:] for e in range(E1)]
        rows = head.tile([P, H], U8, name="rows", offset=0, align_bytes=64)
        rows_by_plane = keep.tile([P, H], U8, name="rows_by_plane", align_bytes=64)
        wb_sc = keep.tile([P, E2 * PASSES * H], U8, name="wb_sc", align_bytes=64)
        by_plane_sc.extend(wb_sc[:, f * PASSES * H : (f + 1) * PASSES * H] for f in range(E2))
        got_sc = [keep.tile([P, T], U8, name="got_sc%d" % g, align_bytes=64) for g in range(2)]
        got_w = [keep.tile([P, PASSES, T], U32, name="got_w%d" % g, align_bytes=64) for g in range(2)]

        nc.gpsimd.memset(x_sc[32:64, :T].bitcast(I32), 0)
        nc.gpsimd.memset(x_sc[64:, :T].bitcast(I32), 0)
        nc.gpsimd.memset(x_sc[:, T:].bitcast(I32), 0)
        nc.gpsimd.memset(x_w[:, :, T:], 0)
        nc.vector.memset(wa_sc[:].bitcast(I32), 0)
        unread = keep.tile([P, 2], F32, name="unread")
        nc.vector.memset(unread[:, :1], 0.0)
        nc.scalar.activation(unread[:, 1:], unread[:, :1], SILU)

        def load_words(tile, words, planes):
            nc.sync.dma_start(
                out=tile.bitcast(I32).rearrange("p (a c) -> p a c", a=planes),
                in_=words.bitcast(I32).rearrange("a p c -> p a c"),
            )

        def load_scales(tile, scales, planes):
            rows = scales.bitcast(I32)
            for q in range(4):
                nc.sync.dma_start(
                    out=tile[32 * q : 32 * q + 4, :].bitcast(I32).rearrange("r (a c) -> r a c", a=planes),
                    in_=rows[:, 4 * q : 4 * q + 4, :].rearrange("a r c -> r a c"),
                )

        def move_scales(plane, rows, planes):
            for q in range(4):
                nc.sync.dma_start(
                    out=plane[32 * q : 32 * q + 4, :].bitcast(I32).rearrange("r (a c) -> r a c", a=planes),
                    in_=rows[4 * planes * q : 4 * planes * (q + 1), :].bitcast(I32),
                )

        nc.sync.dma_start(list_a[:], offs)
        nc.sync.dma_start(out=x_sc[: ROWS * PASSES, :T].bitcast(I32), in_=x_scales.bitcast(I32).rearrange("s b c -> b s c"))
        nc.sync.dma_start(list_b[:], offs2)
        load_scales(wa_sc[:], wa_scales.rearrange("e s b c -> (e s) b c"), E1 * PASSES)
        nc.sync.dma_start(out=x_w[:, :, :T], in_=x_words.rearrange("s p t d -> p s (t d)").bitcast(I32))
        load_words(raw_w[0], wa_words[0], PASSES)
        nc.sync.dma_start(out=rows[:].bitcast(I32), in_=wb_scales.bitcast(I32).rearrange("e s b c -> b (e s) c"))
        load_words(raw_w[1], wa_words[1], PASSES)

        def gather_words(g, offsets, first, count):
            for s in range(PASSES):
                window = x_w[:, s, :].bitcast(U32)
                nc.vector.tensor_copy(
                    got_w[g][:, s, first : first + count], window.indirect(offsets[:, first // 16 : (first + count) // 16])
                )

        def part_words(copy, e, planes=slice(0, PACK)):
            copy(
                by_plane_w[e][:].bitcast(U16).rearrange("p (s d m) -> p s d m", s=PASSES, d=PACK)[:, :, planes, :],
                raw_w[e].bitcast(U16).rearrange("p (s m d) -> p s d m", s=PASSES, d=PACK)[:, :, planes, :],
            )

        def part_scales(e, scales):
            nc.gpsimd.tensor_copy(
                by_plane_sc[e].rearrange("p (s d m) -> p s d m", s=PASSES, d=PACK),
                scales.rearrange("p (s m d) -> p s d m", s=PASSES, d=PACK),
            )

        part_scales(0, wa_sc[:, : PASSES * H])
        nc.gpsimd.tensor_copy(
            rows_by_plane[:].rearrange("p (d m) -> p d m", d=PACK), rows[:].rearrange("p (m d) -> p d m", d=PACK)
        )
        part_scales(1, wa_sc[:, PASSES * H :])
        moved_sc = [keep.tile([P, PASSES * T], U8, name="moved_sc%d" % g, align_bytes=64) for g in range(2)]
        nc.vector.tensor_copy(got_sc[0][:], x_sc[:].indirect(list_a[:]))
        move_scales(moved_sc[0], got_sc[0], PASSES)
        nc.vector.tensor_copy(got_sc[1][:], x_sc[:].indirect(list_b[:]))
        part_words(nc.scalar.copy, 0, slice(0, 1))
        part_words(nc.scalar.copy, 0, slice(1, PACK))
        part_words(nc.scalar.copy, 1, slice(0, 1))
        part_words(nc.gpsimd.tensor_copy, 1, slice(1, PACK))
        for first in (0, HALF):
            gather_words(0, list_a, first, HALF)
        gather_words(1, list_b, 0, T)

        wb_w = [
            keep.tile([P, 2 * EXPERT], U8, name="wb_w0", tag="after_scales", align_bytes=64),
            head.tile([P, 2 * EXPERT], U8, name="wb_w1", offset=0, align_bytes=64),
        ]
        load_words(wb_w[0][:], wb_words[:2].rearrange("e s p c -> (e s) p c"), 2 * PASSES)
        move_scales(moved_sc[1], got_sc[1], PASSES)
        move_scales(wb_sc, rows_by_plane, E2 * PASSES)
        load_words(wb_w[1][:], wb_words[2:].rearrange("e s p c -> (e s) p c"), 2 * PASSES)
        raw_w.extend(wb_w[f // 2][:, f % 2 * EXPERT : (f % 2 + 1) * EXPERT] for f in range(E2))
        for f in range(E2):
            part_words(nc.gpsimd.tensor_copy, E1 + f)

        staged = [keep.tile([P, PACK - 1 + g, T], F32, name="staged%d" % g) for g in range(2)]
        win_a = [keep.tile([P, T], F32, name="win_a%d" % d) for d in range(PACK - 1)]
        win_c = [keep.tile([P, T], F32, name="win_c%d" % d) for d in range(2)]

        def by_plane(pool, e, slots, d, acc):
            for s in range(PASSES):
                column = s * H + d * P
                nc.tensor.matmul_mx(
                    out=acc,
                    lhsT=by_plane_w[2 * pool + e][:, 2 * column : 2 * (column + P)].bitcast(FP4X4),
                    lhsT_scale=by_plane_sc[2 * pool + e][:, column : column + P],
                    rhs=got_w[pool][:, s, slots].bitcast(FP8X4),
                    rhs_scale=moved_sc[pool][:, s * T + slots.start : s * T + slots.stop],
                    start=(s == 0),
                    stop=(s == PASSES - 1),
                )

        def first_pool(e, d, acc):
            by_plane(0, e, slice(e * C1, (e + 1) * C1), d, acc)

        def scatter(engine, window, offsets, plane, first, count):
            target = window[:].indirect(offsets[:, first // 16 : (first + count) // 16])
            if engine == "vector":
                nc.vector.tensor_copy(target, plane[:, first : first + count])
            else:
                nc.scalar.activation(target, plane[:, first : first + count], COPY)

        ends = bank(0, [2, C1])
        for acc, first in ((ends[:, 0, :BLOCK], 0), (bank(7, [BLOCK])[:], BLOCK)):
            by_plane(0, 0, slice(first, first + BLOCK), 0, acc)
            nc.scalar.activation(staged[0][:, 0, first : first + BLOCK], acc, SILU)
        scatter("scalar", win_a[0], list_a, staged[0][:, 0, :], 0, FILL)
        scatter("vector", win_a[0], list_a, staged[0][:, 0, :], FILL, C1 - FILL)
        pairs = [bank(1 + e, [2, C1]) for e in range(E1)]
        for d in range(2):
            first_pool(0, 1 + d, pairs[0][:, d, :])
        nc.scalar.activation(staged[0][:, 1:3, :C1], pairs[0][:], SILU)
        first_pool(1, 0, ends[:, 1, :])
        nc.scalar.activation(staged[0][:, 0, C1:], ends[:, 1, :], SILU)
        scatter("scalar", win_a[2], list_a, staged[0][:, 2, :], 0, C1)
        scatter("vector", win_a[1], list_a, staged[0][:, 1, :], 0, C1)
        scatter("vector", win_a[0], list_a, staged[0][:, 0, :], C1, C1)
        for d in range(2):
            first_pool(1, 1 + d, pairs[1][:, d, :])

        for f in range(E2):
            slots = slice(f * C2, (f + 1) * C2)
            acc = bank(4 + f, [PACK, C2])
            for d in range(PACK):
                by_plane(1, f, slots, d, acc[:, d, :])
            nc.scalar.copy(staged[1][:, :, slots], acc[:])
        last = bank(3, [E1, C1])
        for e in range(E1):
            first_pool(e, 3, last[:, e, :])
        staged_last = shared.tile([P, 2 * T], F32, name="staged_last", offset=0, align_bytes=64)
        nc.scalar.activation(staged_last[:, :T], pairs[1][:].rearrange("p d u -> p (d u)"), SILU)

        w2 = head.tile([P, 3 * N], U8, name="w2", offset=0, align_bytes=64)
        win_c.append(keep.tile([P, T], F32, name="win_c2", tag="plane_w%d" % (PARTED - 2), align_bytes=64))
        win_c.append(shared.tile([P, T], F32, name="win_c3", offset=8 * T, align_bytes=64))
        win_a.append(keep.tile([P, WIDE], F32, name="win_a3"))
        w2_w, w2_sc = w2[:, : 2 * N], w2[:, 2 * N :]
        load_scales(w2_sc, w2_scales, 1)
        nc.sync.dma_start(out=w2_w.bitcast(I32), in_=w2_words[0].bitcast(I32))

        def scatter_late(engine, d, first, count):
            scatter(engine, win_a[d], list_a[:, C1 // 16 :], staged_last[:, (d - 1) * C1 : d * C1], first, count)

        scatter("vector", win_c[0], list_b, staged[1][:, 0, :], 0, HALF)
        scatter("vector", win_c[2], list_b, staged[1][:, 2, :], 0, C2)
        scatter("vector", win_c[0], list_b, staged[1][:, 0, :], HALF, HALF)
        scatter("scalar", win_c[1], list_b, staged[1][:, 1, :], 0, HALF)
        scatter("scalar", win_c[1], list_b, staged[1][:, 1, :], HALF, HALF)
        nc.scalar.activation(staged_last[:, T:], last[:].rearrange("p e u -> p (e u)"), SILU)
        scatter("scalar", win_c[3], list_b, staged[1][:, 3, :], 0, HALF)
        scatter("scalar", win_c[2], list_b, staged[1][:, 2, :], C2, T - C2)
        scatter("scalar", win_c[3], list_b, staged[1][:, 3, :], HALF, HALF)
        scatter_late("vector", 1, 0, C1)
        scatter_late("vector", 2, 0, C1)
        scatter("vector", win_a[3], list_a, staged_last[:, T:], 0, T)

        woven = keep.tile([P, T * PACK], BF16, name="woven", align_bytes=64)
        h = woven[:].rearrange("p (t d) -> p t d", d=PACK)
        high = keep.tile([P, 2, T], BF16, name="high")
        for d in range(2):
            nc.gpsimd.tensor_tensor(h[:, :, d], win_a[d][:, :T], win_c[d][:, :T], MULT)
        nc.gpsimd.tensor_tensor(high[:, 0, :], win_a[2][:, :T], win_c[2][:, :T], MULT)

        for j in (2, 0, 3, 1):
            tokens = slice(j * BLOCK, (j + 1) * BLOCK)
            nc.vector.tensor_tensor(high[:, 1, tokens], win_a[3][:, tokens], win_c[3][:, tokens], MULT)
        for j in (2, 3, 0, 1):
            tokens = slice(j * BLOCK, (j + 1) * BLOCK)
            weave = nc.scalar.copy if j >= 2 else nc.vector.tensor_copy
            weave(h[:, tokens, 2:], high[:, :, tokens].rearrange("p d t -> p t d"))

        sums = []
        for step, j in enumerate((2, 0, 3, 1)):
            h_w = ring.tile([P, BLOCK], U32, name="h_w", align_bytes=64)
            h_sc = ring.tile([P, BLOCK], U8, name="h_sc", align_bytes=64)
            nc.vector.quantize_mx(
                out=h_w[:].bitcast(FP8X4),
                scales=h_sc[:],
                in_=woven[:, j * BLOCK * PACK : (j + 1) * BLOCK * PACK],
            )
            for n in range(N // P):
                acc = bank(2 * step + n, [BLOCK])
                nc.tensor.matmul_mx(
                    out=acc[:],
                    lhsT=w2_w[:, n * 2 * P : (n + 1) * 2 * P].bitcast(FP4X4),
                    lhsT_scale=w2_sc[:, n * P : (n + 1) * P],
                    rhs=h_w[:].bitcast(FP8X4),
                    rhs_scale=h_sc[:],
                    start=True,
                    stop=True,
                )
                sums.append((step, j, n, acc))

        for step, j, n, acc in sums:
            result = ring.tile([P, BLOCK], F32, name="result", bufs=8)
            if step == 3 or (step >= 1 and n == 1):
                nc.vector.tensor_copy(result[:], acc[:])
            else:
                nc.scalar.copy(result[:], acc[:])
            queue = nc.scalar if step in (1, 2) and n == 0 else nc.sync
            queue.dma_start(out=out[n * P : (n + 1) * P, j * BLOCK : (j + 1) * BLOCK], in_=result[:])
